import numpy as np, ml_dtypes
CORES = [25,29,65,69,153,157,193,197]
N = 8
import mx_ref
BF = ml_dtypes.bfloat16
def gentries(a):
    return np.ascontiguousarray(a.reshape(8, 16, -1).transpose(0, 2, 1)).reshape(8, -1)
def gtable(e):
    e = np.asarray(e); return np.ascontiguousarray(e.reshape(8, -1, 16).transpose(0, 2, 1)).reshape(128, -1).astype(np.int32)
def gcols(t, e):
    v = np.concatenate([t.reshape(8, 16, -1, 4), np.zeros((8, 16, 1, 4), BF)], axis=2)
    return np.ascontiguousarray(np.stack([v[g][:, e[g]] for g in range(8)])).reshape(128, -1)
def tile(rs):
    return np.stack(rs, axis=2).reshape(128, -1).astype(BF)
def pick(q, e):
    c = np.concatenate([q[0].reshape(128, -1, 4), np.zeros((128, 1, 4), np.uint8)], axis=1); s = np.concatenate([q[1], np.ones((16, 1), np.uint8)], axis=1)
    return (np.ascontiguousarray(c[:, e].reshape(128, -1)), np.ascontiguousarray(s[:, e]))
def join(*qs):
    return (np.concatenate([q[0] for q in qs], axis=1), np.concatenate([q[1] for q in qs], axis=1))
def put(q, e, v):
    c, s = q[0].reshape(128, -1, 4).copy(), q[1].copy(); c[:, e] = v[0].reshape(128, -1, 4); s[:, e] = v[1]
    return (c.reshape(128, -1), s)
def pk(c, s):
    return (np.ascontiguousarray(c), mx_ref.live(s))
def emit(q):
    return q[0], q[1]
def packed(v, rng):
    q = [mx_ref.quantize(np.ascontiguousarray(v[r])) for r in range(N)]
    return np.stack([a for a, b in q]), np.stack([mx_ref.plane(b, rng) for a, b in q])
def values_of_codes():
    e, c = np.zeros((128, 128, 4), np.float32), np.zeros((128, 2, 4), np.uint8)
    e[np.arange(128), np.arange(128), 0] = 1
    c[:127, :, 0] = np.arange(256).reshape(2, 128).T[:127]
    return mx_ref.matmul(mx_ref.quantize(e.reshape(128, 512).astype(BF)), (c.reshape(128, 8), np.full((16, 2), 127, np.uint8))).T.reshape(-1).astype(np.float64)
CODE_VALUE, SCALE_VALUE = values_of_codes(), 2.0 ** (np.arange(256) - 127.0)
def decode(q):
    return (CODE_VALUE[q[0]].reshape(16, 8, -1, 4) * SCALE_VALUE[q[1]][:, None, :, None] + 0.0).reshape(128, -1).astype(np.float32)
def f(rng, *shape):
    return mx_ref.flush((rng.standard_normal(shape, dtype=np.float32) * np.exp2(rng.integers(-2, 3, shape[:-1] + (1,)))).astype(BF))
def wide(rng, *shape, cols=0):
    v = rng.standard_normal(shape, dtype=np.float32) * np.exp2(rng.integers(-12, 13, shape)).astype(np.float32)
    if cols: v *= np.repeat(np.exp2(rng.integers(-cols, cols + 1, shape[:-2] + (1, shape[-1] // 4))) * (rng.random(shape[:-2] + (1, shape[-1] // 4)) > 0.0625), 4, axis=-1).astype(np.float32)
    return mx_ref.flush(v.astype(BF))
T, C = 320, 128
def big(v):
    v = v.astype(np.float32)
    v[np.abs(v) < np.float32(2.0 ** -16)] = 0
    return v.astype(BF)
def numbers_of(rng):
    return {"x": np.array(f(rng, N, 128, 4 * T)), "k": np.array(f(rng, N, 128, 4 * C)), "u": np.array(f(rng, N, 128, 512)), "v": np.array(f(rng, N, 128, 512))}
def pointers(rng):
    return {"pt": np.stack([gtable(rng.integers(0, C, (8, T))) for r in range(N)]), "ad": np.stack([gtable(rng.integers(0, C, (8, C))) for r in range(N)])}
def weights(rng, still=[]):
    c = np.arange(512)
    free, hold = c[~np.isin(c // 4 % 16, still)], c[np.isin(c % 16, still)]
    m = np.zeros((N, 512, 512), np.float32)
    if len(free):
        for r in range(N): m[r, free[rng.integers(0, len(free), (12, 512))], c] = (0.5 + 1.5 * rng.random((12, 512))) * rng.choice([-1.0, 1.0], (12, 512))
    m[:, :, hold] = 0
    m[:, 4 * (hold % 128) + hold // 128, hold] = 32
    a, s = packed(m.reshape(N, 128, 4, 512).transpose(0, 1, 3, 2).reshape(N, 128, 2048).astype(BF), rng)
    return {"wc": a, "ws": s}
def setup_inputs(rng):
    return {**numbers_of(rng), **pointers(rng), **weights(rng)}
def setup_inputs_ties(rng):
    d = numbers_of(rng)
    o, e = rng.permutation(N), rng.permutation(8)
    p = rng.integers(0, C, (N, 8, T))
    for i, n in (("x", T), ("k", C)):
        a = d[i].reshape(N, 8, 16, n, 4)
        a[:, :, 0] = 0
        a[:, :, 0, :, 0] = rng.integers(0, 3, (N, 8, n)).astype(np.float32).astype(BF)
        for r in o[2:]:
            a[r, e[0], :8] = 0
            if i == "k": a[r, e[0], 0, :, 0] = 4
            else:
                w = rng.permutation(T)
                go = w // C % 2 == 1
                p[r, e[0]] = w % C
                a[r, e[0], 0, :, 0] = np.where(go, rng.integers(1, 4, T), 0).astype(np.float32).astype(BF)
                a[r, e[0], 1, :, 0] = np.where(go, 0.0, 2.0 ** 24).astype(np.float32).astype(BF)
                p[r, e[1]] = rng.integers(C)
                a[r, e[1], 0, T - 1, 0] = 3
        d[i] = a.reshape(N, 128, 4 * n)
    u = d["u"].reshape(N, 128, 128, 4)
    u[:, :, ::16] = 0
    for r in range(N):
        for h in range(0, 128, 16): u[r, h, h, 0] = 0.0 if r == o[0] else -1.0 if r == o[1] else 1.0
    d["u"] = u.reshape(N, 128, 512)
    return {**d, **pointers(rng), "pt": np.stack([gtable(p[r]) for r in range(N)]), **weights(rng, [0])}
def setup_inputs_near(rng):
    d = numbers_of(rng)
    o = rng.permutation(8)
    sign = np.where(o < 4, 1.0, -1.0)
    for i, n in (("x", T), ("k", C)):
        a = d[i].astype(np.float32).reshape(N, 8, 16, n, 4)
        a[:, :, 0] = 0
        a[:, :, 8:] = 0
        a[:, :, 0, :, 0] = sign[:, None]
        s = rng.integers(0, 16, (N, 8, n))
        a[:, :, 8] = ((s[:, :, :, None] >> np.arange(4)) & 1) * np.exp2(np.arange(4) - 23.0)
        a[:, :, 11, :, 0] = 2.0 ** -10
        for g in range(8):
            if o[g] % 4 == 2:
                a[:, g, 8:] = 0
                a[:, g, 8:10, :, 0] = rng.integers(8, 16, (N, 2, n)) * 2.0 ** -33
            if o[g] == 7:
                a[:, g, 8:] = 0
                a[:, g, 8, :, 0] = 1.96875
                a[:, g, 9, :, 0] = (1.0 + rng.random((N, n))) * np.exp2(-1.0 * rng.integers(13, 17, (N, n)))
            if o[g] % 4 == 1 and i == "x":
                for r in range(N): a[r, g, 0, rng.integers(n), 0] = sign[g] * 2.0 ** 29
        d[i] = a.reshape(N, 128, 4 * n).astype(BF)
    u = d["u"].reshape(N, 128, 128, 4)
    u[:, :, ::16] = 0
    for g in range(8):
        h, c = 16 * g, 1.0 if o[g] % 4 == 0 else 2.0 ** -30
        if o[g] % 4 < 2:
            u[:, h, h, 0] = c
            u[:, h + 11, h, 0] = c
        if o[g] % 4 == 2:
            u[:, h + 8, h, 0] = 1.125 * c
            u[:, h + 9, h, 0] = 1.25 * c if o[g] == 2 else -1.25 * c
        elif o[g] == 7: u[:, h + 9, h, 0] = 1.0
        else: u[:, h + 8, h] = c
    d["u"] = u.reshape(N, 128, 512)
    return {**d, **pointers(rng), **weights(rng, [0, 8, 9, 10, 11, 12, 13, 14, 15])}
def setup_inputs_huge(rng):
    d = numbers_of(rng)
    o = rng.permutation(N)
    for i, n in (("x", T), ("k", C)):
        a = (0.6 + 0.4 * rng.random((N, 128, n, 4))) * 2.0 ** 30
        c = rng.integers(0, 2, (N, 1, n, 1)) * 2.0 - 1.0
        c[o < N // 2] = 1
        d[i] = (a * c).astype(np.float32).reshape(N, 128, 4 * n).astype(BF)
    u = d["u"].reshape(N, 128, 128, 4)
    u[:, :, ::16] = (-2.0 ** 30 * (1 - 0.1 * rng.random((N, 128, 8, 4)))).astype(np.float32).astype(BF)
    d["u"] = u.reshape(N, 128, 512)
    return {**d, **pointers(rng), **weights(rng)}
def setup_inputs_ends(rng):
    d = numbers_of(rng)
    s, h = rng.integers(N), rng.permutation(8)
    o = np.zeros(N, int)
    o[(s - np.arange(N)) % N] = np.concatenate([[0, 2, 1], rng.permutation(np.arange(3, N))])
    e = np.concatenate([rng.permutation((s + np.arange(1, N - 1)) % N)[:2], [s, (s - 1) % N]])
    sign = rng.integers(0, 2, (8, 16, 1, 4)) * 2.0 - 1.0
    sign[h[:2]] = 1
    sign[h[2:4]] = -1
    for r in range(N):
        for i, n in (("x", T), ("k", C)):
            a = np.full((8, 16, n, 4), 2.0 ** -30)
            if o[r] % 2 == 0:
                a = 2.0 ** 30 * (1 - 0.1 * rng.random((8, 16, n, 4)))
                if o[r] == 2:
                    a *= 0.5
                    a[:, :, [0, 1 if i == "x" else C - 1]] = 2.0 ** 30
                a[h[4:6]] = 2.0 ** 30
            if o[r] == 0: a[:] = 2.0 ** 30
            d[i][r] = (a * sign).reshape(128, 4 * n).astype(np.float32).astype(BF)
        c = sign.reshape(128, 4) * (2.0 ** -30 if o[r] % 4 == 1 else 2.0 ** 30) * (-1.0 if o[r] % 4 < 2 else 1.0)
        c = c.astype(np.float32).astype(BF)
        a = d["u"][r].reshape(128, 128, 4).copy()
        a[:, ::16] = c[:, None]
        for g in h[4:6]:
            a[:, 16 * g] = 0
            a[16 * g:16 * g + 16, 16 * g] = c[16 * g:16 * g + 16]
        d["u"][r] = a.reshape(128, 512)
        if o[r] == 0: d["v"][r] = np.tile(c, (1, 128))
    p, a = rng.integers(0, C, (N, 8, T)), rng.integers(0, C, (N, 8, C))
    p[e[0]], a[e[0]] = C - 1, C - 1
    p[e[1]], a[e[1]] = 0, 0
    p[e[2]], a[e[2]] = np.arange(T) % C, np.arange(C)
    p[e[3]], a[e[3]] = (C - 1) * rng.integers(0, 2, (8, T)), C - 1 - np.arange(C)
    p[e[3], :, :4] = [0, C - 1, 0, C - 1]
    d["v"] = (np.where(d["v"] < 0, -1.0, 1.0) * np.where(rng.permutation(N) % 2, 2.0 ** -30, 2.0 ** 30)[:, None, None]).astype(np.float32).astype(BF)
    return {**d, "pt": np.stack([gtable(p[r]) for r in range(N)]), "ad": np.stack([gtable(a[r]) for r in range(N)]), **weights(rng, list(range(16)))}
def setup_inputs_spread(rng):
    d = setup_inputs(rng)
    d["x"] = big(wide(rng, N, 128, 4 * T, cols=6))
    d["k"] = big(wide(rng, N, 128, 4 * C, cols=6))
    return d
def check_inputs(d):
    b = []
    for i in ("x", "k", "u", "v"):
        a = np.abs(d[i].astype(np.float32))
        if not (np.isfinite(a).all() and ((a == 0) | (a >= 2.0 ** -30) & (a <= 2.0 ** 30)).all()): b.append("a value of " + i)
    for i in ("pt", "ad"):
        if not ((d[i] >= 0) & (d[i] < C)).all(): b.append("an entry of " + i)
    none, least, most = [emit(mx_ref.quantize(np.full((128, 16), c, np.float32).astype(BF)))[1][0, 0] for c in (0.0, 2.0 ** -30, 2.0 ** 30)]
    for r in range(N):
        if ((d["wc"][r] & 0x7F) == 0x7F).any(): b.append("wc: a code that is no number")
        s = mx_ref.live(d["ws"][r])
        if ((s != none) & ((s < least) | (s > most))).any(): b.append("ws: a scale out of range")
        a = np.abs(decode(pk(d["wc"][r], d["ws"][r])).astype(np.float64)).reshape(128, 512, 4)
        if not (np.sum(a, axis=(0, 2)) <= 32).all(): b.append("W: the sizes of a column add up to more than 32")
    return b
def half(a, b):
    return ((a.astype(np.float32) + b.astype(np.float32)) * np.float32(0.5)).astype(BF)
def parts(e):
    return np.repeat(np.repeat(e, 16, axis=0), 4, axis=1)
def inserters(s, at, n):
    g = np.arange(8)[:, None]
    o = np.argsort(-s, axis=1, kind="stable")
    place = np.zeros((8, T), np.int64)
    place[g, o] = np.arange(T)
    first = np.full((8, n), T)
    np.minimum.at(first, (np.broadcast_to(g, at.shape), at), place)
    return np.where(first < T, np.take_along_axis(o, np.minimum(first, T - 1), axis=1), -1)
def reference(x, k, u, v, pt, ad, wc, ws):
    qu = [mx_ref.quantize(u[r]) for r in range(N)]
    lay = [pk(wc[r], ws[r]) for r in range(N)]
    now = [x[r] for r in range(N)]
    cell = [decode(mx_ref.quantize(k[r])).astype(BF) for r in range(N)]
    at = [gentries(pt[r]) for r in range(N)]
    near = [gentries(ad[r]) for r in range(N)]
    for n in (C, 2 * C):
        given = []
        slot = []
        for r in range(N):
            q = mx_ref.quantize(now[r])
            own = decode(q).astype(BF)
            win = inserters(mx_ref.matmul(qu[r], q)[::16] + np.float32(0.0), at[r], n)
            a = np.where(parts(win < 0), cell[r], half(cell[r], gcols(own, win)))
            b = np.where(parts(win < 0), cell[r], half(cell[r], gcols(cell[r], near[r])))
            v0, v1 = half(own, gcols(a, at[r])), half(own, gcols(b, at[r]))
            more = mx_ref.matmul(qu[r], mx_ref.quantize(v1))[::16] > mx_ref.matmul(qu[r], mx_ref.quantize(v0))[::16]
            now[r] = np.where(parts(more), v1, v0)
            slot.append(np.where(np.take_along_axis(win, at[r], axis=1) == np.arange(T), at[r], -1))
            given.append(mx_ref.quantize(np.ascontiguousarray(a)))
            at[r] = at[r] + n * more
            near[r] = np.concatenate([np.broadcast_to(np.arange(n) + n, (8, n)), near[r]], axis=1)
            cell[r] = np.concatenate([a, b], axis=1)
        for r in range(N):
            q = given[(r - 1) % N]
            made = tile([mx_ref.matmul(pick(lay[r], np.arange(128 * b, 128 * b + 128)), q) * np.float32(0.03125) for b in range(4)])
            now[r] = np.ascontiguousarray(np.where(parts(slot[r] >= 0), gcols(made, slot[r]), now[r]))
    y, z, op = np.zeros((N, 128, T), np.float32), np.zeros((N, 128, 4 * C), np.float32), np.zeros((N, 8, T), np.float32)
    oc, osc = np.zeros((N, 128, 4 * T), np.uint8), np.zeros((N, 16, T), np.uint8)
    for r in range(N):
        q, qv = mx_ref.quantize(now[r]), mx_ref.quantize(v[r])
        y[r] = mx_ref.matmul(qv, q)
        z[r] = mx_ref.matmul(qv, mx_ref.quantize(np.ascontiguousarray(cell[r])))
        op[r] = at[r]
        oc[r], osc[r] = emit(q)
    return {"y": y, "z": z, "op": op, "oc": oc, "osc": osc}

@@ -1,0 +1,566 @@
+from concourse.bass import DstId, RemoteDMATransfer
+from concourse.mybir import dt, AluOpType as ALU, AxisListType, ActivationFunctionType as AF
+
+F4, BF, I4, U2, C8, S8 = "float32", "bfloat16", "int32", "uint16", "float8_e4m3fn_x4", "uint8"
+PL, L, LS = 576, 336, 328
+NV = 5
+NS = 20 - NV
+BIG = 2.0 ** 86
+
+
+def _sb(n, d):
+    return ("sbuf", [128, n], d)
+
+
+SCRATCH = {
+    "xs": _sb(1280, BF), "ks": _sb(512, BF), "us": _sb(512, BF), "vs": _sb(512, BF),
+    "qxk": _sb(448, C8), "sxk": _sb(448, S8), "qu": _sb(128, C8), "su": _sb(128, S8), "qur": _sb(128, C8), "sur": _sb(128, S8),
+    "qvv": _sb(128, C8), "svv": _sb(128, S8), "qw": _sb(512, C8), "sw": _sb(512, S8),
+    "et": _sb(2048, BF), "ones": _sb(128, BF), "qe": _sb(512, C8), "se": _sb(512, S8),
+    "ptw": _sb(20, I4), "ptr": _sb(320, I4), "adw": _sb(8, I4), "h16": _sb(320, I4), "lo": _sb(320, I4), "hw16": _sb(20, I4),
+    "pidx": _sb(4, I4), "dgi": _sb(16, I4), "iq": _sb(320, F4), "vk": _sb(L, F4), "dg": _sb(L, F4), "tb": _sb(L, F4), "hb": _sb(144, F4), "cid": _sb(256, F4),
+    "keyr": _sb(320, F4), "junk": _sb(1920, BF), "cmpv": _sb(960, BF),
+    "vv": _sb(L, F4), "dgt": _sb(L, F4), "dgs": _sb(L, F4), "inc": _sb(LS, F4), "d0": _sb(LS, F4), "msk": _sb(320, F4), "mks": _sb(2 * L, F4),
+    "sx0": _sb(464, F4), "ss0": _sb(L, F4), "ss1": _sb(L, F4), "st0": _sb(L, F4), "st1": _sb(L, F4),
+    "nr0": _sb(LS, F4), "nr1": _sb(LS, F4), "s2": _sb(2 * LS, F4), "offu": _sb(16, U2),
+    "fg1": _sb(4 * PL, BF), "fg2": _sb(4 * PL, BF), "gh": _sb(1536, BF), "at1": _sb(512, BF), "bt1": _sb(512, BF), "g3": _sb(2048, BF), "ab2": _sb(2048, BF),
+    "vl1": _sb(4 * 768, BF), "vl2": _sb(4 * 896, BF), "xt2": _sb(1280, BF), "xt3": _sb(1280, BF), "fgx": _sb(1792, BF), "ghx": _sb(512, BF), "atx": _sb(512, BF),
+    "tv1": _sb(2560, BF), "tv2": _sb(2560, BF),
+    "qa1": _sb(128, C8), "sa1": _sb(128, S8), "qax": _sb(128, C8), "sax": _sb(128, S8), "qg": _sb(512, C8), "sg3": _sb(512, S8), "qv": _sb(640, C8), "sv3": _sb(640, S8),
+    "qx": _sb(320, C8), "sx": _sb(320, S8), "qx3": _sb(320, C8), "sx3": _sb(320, S8),
+    "t0s": _sb(320, F4), "more": _sb(464, F4), "mor2": _sb(320, F4), "sl": _sb(576, F4), "pti": _sb(320, F4), "opr": _sb(640, F4), "zs": _sb(832, F4),
+    "lcx": _sb(448, C8), "lsx": _sb(448, S8), "llx": _sb(8, U2), "lc1": _sb(128, C8), "ls1": _sb(128, S8), "lc2": _sb(256, C8), "ls2": _sb(256, S8),
+    "rcx": _sb(224, C8), "rsx": _sb(448, S8), "rlx": _sb(8, U2), "rc2": _sb(128, C8), "rs2": _sb(256, S8),
+}
+ALIAS = {}
+
+
+def _pack(base, dtype, parts):
+    at = 0
+    for n, w in parts:
+        ALIAS[n] = (base, at, w)
+        at += -(-w // 16) * 16
+    SCRATCH[base] = _sb(at, dtype)
+
+
+_pack("sm", F4, [("cst", 16), ("iw", 20), ("iw32", 20), ("clf", 22), ("uif", 8), ("vsrc", 16), ("kk", 16), ("cw", 16), ("dg16", 16), ("keyw", 20), ("hwf", 20), ("acc", 16), ("accs", 2),
+                 ("cntv", 8), ("posa", 20), ("offf", 16), ("off2", 16), ("adf", 16), ("cd", 16), ("no", 16), ("pt2f", 20), ("mw", 20), ("slw", 20), ("wf", 20)])
+_pack("ul", U2, [("clu", 20), ("uiu", 8), ("dgl", 22), ("plist", 22), ("el", 4), ("order", 22), ("offv", 16), ("adu", 16), ("ptu", 20), ("wu", 80)])
+for _i in range(8):
+    SCRATCH["p%d" % _i] = ("psum", [128, 512], F4)
+_DS = ["d_ptw", "d_rep", "d_x", "d_k", "d_u", "d_v", "d_w", "d_ws", "d_ad", "d_out1", "d_out2"]
+SEMAPHORES = ["qv_s", "qs_s", "qt_s", "qg_s", "arr1", "arr2", "arrx", "arrl", "rinx", "rinl", "rin2", "loc"] + _DS
+
+
+def _bits(es):
+    return sum(1 << e for e in es)
+
+
+def _relays(src, dst, T, topo):
+    if topo.may_write(src, dst):
+        return []
+    c = [d for d in topo.cores_of(src) if d != src and T.rank_of(d) is None and topo.may_write(d, dst)]
+    a, b = [d for d in c if topo.die(d) == topo.die(src)], [d for d in c if topo.die(d) != topo.die(src)]
+    return [d for p in zip(a, b) for d in p][:3]
+
+
+def _hand_on(g, core, T, topo):
+    sent = 0
+    for r, src in enumerate(T.cores):
+        dst = T.cores[(r + 1) % len(T.cores)]
+        rel = _relays(src, dst, T, topo)
+        if core not in rel:
+            continue
+        j = rel.index(core)
+        rid, pid = topo.addr(dst, core)
+        m = _bits(topo.engines(core, dst)[:8])
+
+        def piece(tag, n):
+            g.wait_ge(T.sem["rin" + tag], 8)
+            if j < 2:
+                h = n // 2
+                o, i = T["lc" + tag][:, h * j:h * j + h].bitcast(dt.uint8), T["rc" + tag][:, 0:h].bitcast(dt.uint8)
+            else:
+                o, i = T["ls" + tag][:, 0:n], T["rs" + tag][:, 0:n]
+            g.remote_dma(o, i, T.sem["arr" + tag], T.sem["loc"], pid, rid, m)
+        piece("x", 448)
+        if j == 2:
+            g.wait_ge(T.sem["rinl"], 8)
+            g.remote_dma(T.llx[:, 0:8], T.rlx[:, 0:8], T.sem["arrl"], T.sem["loc"], pid, rid, m)
+            sent += 8
+        piece("2", 256)
+        sent += 16
+    if sent:
+        g.wait_ge(T.sem["loc"], sent)
+
+
+def rank_program(g, core, T, topo):
+    rank = T.rank_of(core)
+    if rank is None:
+        _hand_on(g, core, T, topo)
+        return
+    nranks = len(T.cores)
+    prev, nxt = T.cores[(rank - 1) % nranks], T.cores[(rank + 1) % nranks]
+    rel, far = _relays(core, nxt, T, topo), bool(_relays(prev, core, T, topo))
+    V, S, E, G, Y = "v", "s", "t", "g", "y"
+    eng = {V: g.vector, S: g.scalar, E: g.tensor, G: g, Y: g.sync}
+    qsem = {V: "qv_s", S: "qs_s", E: "qt_s", G: "qg_s"}
+    cnt = {V: 0, S: 0, E: 0, G: 0}
+    seen = {q: {} for q in eng}
+    hist = {}
+
+    def need(q, sem, n):
+        if seen[q].get(sem, 0) < n:
+            eng[q].wait_ge(T.sem[sem], n)
+            seen[q][sem] = n
+
+    def track(q, outs, ins, token=None):
+        acc = [(r, True) for r in outs] + [(r, False) for r in ins]
+        waits = {}
+        for (name, lo, hi, ph), w in acc:
+            ps = name[0] == "p" and name[1:].isdigit()
+            for (l2, h2, p2, w2, tok, q2) in hist.get(name, []):
+                if l2 < hi and lo < h2 and (ph is None or p2 is None or ph == p2) and (w or w2 or (ps and q2 != q)):
+                    waits[tok[0]] = max(waits.get(tok[0], 0), tok[1])
+        for s, n in waits.items():
+            need(q, s, n)
+        if token is None:
+            cnt[q] += 1
+            token = (qsem[q], cnt[q])
+        for (name, lo, hi, ph), w in acc:
+            h = hist.setdefault(name, [])
+            if w and ph is None:
+                h[:] = [e for e in h if not (lo <= e[0] and e[1] <= hi)]
+            h.append((lo, hi, ph, w, token, q))
+        return token
+
+    def run(q, outs, ins, f):
+        track(q, [o[1] for o in outs], [i[1] for i in ins])
+        f().then_inc(T.sem[qsem[q]], 1)
+
+    def A(name, lo=0, hi=None):
+        if name in ALIAS:
+            name, at, w = ALIAS[name]
+            lo, hi = at + lo, at + (w if hi is None else hi)
+        hi = SCRATCH[name][1][1] if hi is None else hi
+        return (T[name][:, lo:hi], (name, lo, hi, None))
+
+    def B4(name, lo, hi, b):
+        return (T[name][:, lo + b:hi:4], (name, lo, hi, b))
+
+    def St(name, hi, lo=15, step=16):
+        return (T[name][:, lo:hi:step], (name, 0, hi, None))
+
+    def ind(a, li):
+        return a[0] if li is None else a[0].indirect(li[0])
+
+    def opt(*xs):
+        return [x for x in xs if isinstance(x, tuple)]
+
+    def val(x):
+        return x[0] if isinstance(x, tuple) else x
+
+    def tt(o, a, b, op, li=None):
+        run(V, [o], [a, b] + opt(li), lambda: g.vector.tensor_tensor(o[0], ind(a, li), b[0], op))
+
+    def ts(o, a, s1, op0, s2=None, op1=None, li=None):
+        if op1 is None:
+            run(V, [o], [a] + opt(li, s1), lambda: g.vector.tensor_scalar(o[0], ind(a, li), val(s1), None, op0))
+        else:
+            run(V, [o], [a] + opt(li, s1, s2), lambda: g.vector.tensor_scalar(o[0], ind(a, li), val(s1), val(s2), op0, op1))
+
+    def cp(o, a, li=None):
+        run(V, [o], [a] + opt(li), lambda: g.vector.tensor_copy(o[0], ind(a, li)))
+
+    def scatter(o, li, a):
+        run(V, [o], [a, li], lambda: g.vector.tensor_copy(o[0].indirect(li[0]), a[0]))
+
+    def fill(o, c):
+        run(V, [o], [], lambda: g.vector.memset(o[0], c))
+
+    def scan(o, a, b, init, op0, op1):
+        run(V, [o], [a, b], lambda: g.vector.tensor_tensor_scan(o[0], a[0], b[0], init, op0, op1))
+
+    def act(o, a, scale=1.0, bias=0.0, func=None, li=None, accum=None):
+        fn = AF.Copy if func is None else func
+
+        def f():
+            kw = {}
+            if isinstance(bias, tuple) or bias != 0.0:
+                kw["bias"] = val(bias)
+            if scale != 1.0:
+                kw["scale"] = scale
+            if accum is not None:
+                kw["accum_out"] = accum[0]
+            return g.scalar.activation(o[0], ind(a, li), fn, **kw)
+        run(S, [o] + opt(accum), [a] + opt(li, bias), f)
+
+    def iota(o, pattern, base, cm):
+        def f():
+            if SCRATCH[o[1][0]][2] == I4:
+                return g.iota(o[0], pattern, base, cm)
+            return g.iota(o[0], pattern, base, cm, allow_small_or_imprecise_dtypes=True)
+        run(G, [o], [], f)
+
+    def quant(q, s, lo, hi, t, tlo):
+        a, b, c = A(q, lo, hi), A(s, lo, hi), A(t, tlo, tlo + 4 * (hi - lo))
+        run(V, [a, b], [c], lambda: g.vector.quantize_mx(a[0], b[0], c[0]))
+
+    def mm(p, n, wq, ws, wlo, xq, xs, xlo):
+        o = A(p, 0, n)
+        w, w2, x, x2 = A(wq, wlo, wlo + 128), A(ws, wlo, wlo + 128), A(xq, xlo, xlo + n), A(xs, xlo, xlo + n)
+        run(E, [o], [w, w2, x, x2], lambda: g.tensor.matmul_mx(o[0], w[0], w2[0], x[0], x2[0], True, True))
+
+    def dma(q, out, in_, sem, n=16, outs=(), ins=()):
+        track(q, list(outs), list(ins), token=(sem, n))
+        eng[q].dma_start(out, in_).then_inc(T.sem[sem], 16)
+
+    def load(q, name, src, sem):
+        a = A(name)
+        dma(q, a[0], src, sem, outs=[a[1]])
+
+    sent = [0]
+
+    def remote(out, src, reg, sem, dst, es):
+        track(G, [], [reg], token=("loc", 0))
+        rid, pid = topo.addr(dst, core)
+        g.remote_dma(out, src, T.sem[sem], T.sem["loc"], pid, rid, _bits(es))
+        sent[0] += len(es)
+
+    def send(tag, qn, sn, n):
+        c, s = A(qn, 0, n), A(sn, 0, n)
+        if not rel:
+            es = topo.engines(core, nxt)
+            remote(T["lc" + tag][:, 0:n].bitcast(dt.uint8), c[0].bitcast(dt.uint8), c[1], "arr" + tag, nxt, es[0:8])
+            remote(T["ls" + tag][:, 0:n], s[0], s[1], "arr" + tag, nxt, es[8:16])
+            return
+        track(G, [], [c[1]], token=("loc", 0))
+        h, tr = n // 2, []
+        for j in range(2):
+            rid, pid = topo.addr(rel[j], core)
+            es = topo.engines(core, rel[j])[8 * j:8 * j + 8]
+            tr.append(RemoteDMATransfer(dst_ids=[DstId(rid=rid, pnc=pid)], dma_engine_mask=_bits(es), remote_sem=T.sem["rin" + tag],
+                                        src=T[qn][:, h * j:h * j + h].bitcast(dt.uint8), dst=T["rc" + tag][:, 0:h].bitcast(dt.uint8)))
+            sent[0] += len(es)
+        g.remote_dma_fused(tr, local_sem=T.sem["loc"])
+        remote(T["rs" + tag][:, 0:n], s[0], s[1], "rin" + tag, rel[2], topo.engines(core, rel[2])[0:8])
+
+    load(S, "ptw", T.pt[:, :], "d_ptw")
+    for q in range(16):
+        dma(S if q % 2 else Y, T.ptr[q:128:16, :], T.pt[:, :], "d_rep", n=256)
+    hist["ptr"] = [(0, 320, None, True, ("d_rep", 256), "dma")]
+    load(Y, "us", T.u[:, :], "d_u")
+    load(S, "xs", T.x[:, :], "d_x")
+    load(Y, "ks", T.k[:, :], "d_k")
+    dma(Y, T.qw[:, 0:512].bitcast(dt.uint8), T.wc[:, :], "d_w", outs=[("qw", 0, 512, None)])
+    load(Y, "sw", T.ws[:, :], "d_ws")
+    load(Y, "adw", T.ad[:, :], "d_ad")
+    load(Y, "vs", T.v[:, :], "d_v")
+
+    iota(A("pidx", 0, 1), [[1, 1]], 0, 1)
+    iota(A("iq"), [[1, 16], [16, 20]], 0, 0)
+    iota(A("iw"), [[16, 20]], 0, 0)
+    iota(A("clf"), [[1, 22]], 0, 0)
+    iota(A("dgi"), [[1, 16]], 128, -1)
+    iota(A("uif"), [[16, 8]], 0, 0)
+    iota(A("kk"), [[0, 2], [16, 8]], 336, 0)
+    iota(A("hb"), [[1, 9], [0, 16]], 0, 0)
+    fill(A("ones"), 0.5)
+    fill(A("et"), 0.0)
+    for b in range(4):
+        o, i = B4("et", 512 * b, 512 * b + 512, b), A("ones")
+        run(G, [o], [i], lambda: g.affine_select(o[0], i[0], [[-1, 128]], ALU.is_equal, 0.0, 0, 1))
+    iota(A("vk", 0, 320), [[1, 320]], 0, 0)
+    iota(A("vsrc"), [[16, 16]], 336, 0)
+    iota(A("tb"), [[0, L]], 0, 0)
+    iota(St("tb", L, 0), [[0, 21]], 2 ** 22, 0)
+    iota(A("st0", 0, 8), [[0, 8]], 0, 0)
+    iota(A("st1", 0, 8), [[0, 8]], 0, 0)
+    iota(A("cw"), [[16, 16]], 0, 0)
+
+    pf, q_, q8, thA, thB, addA, addB, addB2, tmpc, q20 = [A("cst", j, j + 1) for j in range(10)]
+    qi, q8i = A("pidx", 1, 2), A("pidx", 2, 3)
+    act(A("iq"), A("iq"), scale=0.03125)
+    ts(qi, A("pidx", 0, 1), 15, ALU.bitwise_and)
+    ts(q8i, A("pidx", 0, 1), 7, ALU.bitwise_and)
+    cp(q_, qi)
+    cp(q8, q8i)
+    ts(A("dgl"), A("clf"), 0.0, ALU.mult, q_, ALU.add)
+    ts(A("dgi"), A("dgi"), 15, ALU.bitwise_and)
+    ts(A("dg16"), A("dgi"), 0.0, ALU.not_equal, 2.0 ** 20, ALU.mult)
+    ts(A("iw"), A("iw"), q_, ALU.add)
+    ts(A("iw32"), A("iw"), 0.03125, ALU.mult)
+    ts(thA, q_, 16.0, ALU.mult, 14.0, ALU.add)
+    ts(thB, q8, 16.0, ALU.mult, 14.0, ALU.add)
+    ts(tmpc, q_, 15.0, ALU.is_equal, -336.0, ALU.mult)
+    ts(addA, q_, tmpc, ALU.add, 161.0, ALU.add)
+    ts(addB, q8, 160.0, ALU.add)
+    ts(pf, q_, 8.0, ALU.is_ge, float(LS), ALU.mult)
+    tt(addB2, addB, pf, ALU.add)
+    ts(q20, q_, 20.0, ALU.mult)
+    cp(A("uiu"), A("uif"))
+    ts(A("clu"), A("clf", 0, 20), q20, ALU.add)
+    act(A("dg"), A("dg16"), li=A("dgl", 0, 21))
+    act(A("kk"), A("kk"), bias=q_, func=AF.Identity)
+    act(A("sx0", 320, 464), A("hb"), scale=2.0 ** 80, bias=-32 * 2.0 ** 80, func=AF.Identity)
+    act(A("more", 320, 464), A("hb"), scale=0.0, bias=0.5, func=AF.Identity)
+
+    ts(A("h16"), A("ptr"), 0x70, ALU.bitwise_and)
+    ts(A("hw16"), A("ptw"), 0x70, ALU.bitwise_and)
+    tt(A("keyr"), A("h16"), A("iq"), ALU.add)
+    tt(A("keyw"), A("hw16"), A("iw32"), ALU.add)
+
+    def count(k, bias, out):
+        j = 320 * (k % 6)
+        act(A("junk", j, j + 320), A("keyr"), scale=-1.0, bias=bias, func=AF.Sign, accum=out)
+
+    for k in range(NS):
+        count(k, A("keyw", k, k + 1), A("acc", k, k + 1))
+    count(NS, thA, A("accs", 0, 1))
+
+    def lane(j):
+        o, c = A("cntv", j, j + 1), A("cmpv", 320 * (j % 3), 320 * (j % 3) + 320)
+        ts(c, A("keyr"), A("keyw", NS + j, NS + j + 1), ALU.is_lt)
+        run(V, [o], [c], lambda: g.vector.tensor_reduce(o[0], c[0], AxisListType.X, ALU.add))
+
+    lane(0)
+    lane(1)
+    quant("qxk", "sxk", 0, 320, "xs", 0)
+    quant("qxk", "sxk", 320, 448, "ks", 0)
+    if rel:
+        send("x", "qxk", "sxk", 448)
+    iota(A("cid"), [[1, 256]], 640, 0)
+    iota(A("sl", 0, 448), [[0, 448]], 0, 0)
+    quant("qu", "su", 0, 128, "us", 0)
+    o1, i1, l1 = A("qur"), A("qu"), A("uiu")
+    run(V, [o1], [i1, l1], lambda: g.vector.tensor_copy(T.qur[:, 0:128].bitcast(dt.uint32), T.qu[:, 0:128].bitcast(dt.uint32).indirect(l1[0])))
+    cp(A("sur"), A("su"), li=l1)
+    mm("p4", 320, "qur", "sur", 0, "qxk", "sxk", 0)
+    quant("qe", "se", 0, 512, "et", 0)
+    for b in range(4):
+        mm("p%d" % b, 448, "qe", "se", 128 * b, "qxk", "sxk", 0)
+    for j in range(2, NV):
+        lane(j)
+    ts(A("lo"), A("ptr"), 15, ALU.bitwise_and)
+    ts(A("msk"), A("lo"), q_, ALU.not_equal, BIG, ALU.mult, li=A("clu"))
+    ts(A("vk", 320, 336), A("vsrc"), 448.0, ALU.min, q_, ALU.add)
+    ts(A("vk", 335, 336), q_, 320.0, ALU.add)
+    ts(A("hwf"), A("hw16"), 0.0625, ALU.mult)
+    tt(A("sx0", 0, 320), A("p4", 0, 320), A("msk"), ALU.subtract)
+    ts(A("posa", NS, 20), A("cntv", 0, NV), 1.0, ALU.add)
+    ts(A("posa", 0, NS), A("acc", 0, NS), 0.5, ALU.mult, 160.5, ALU.add)
+    tt(A("posa"), A("posa"), A("hwf"), ALU.add)
+    cp(A("plist", 0, 20), A("posa"))
+    ts(A("plist", 20, 21), A("accs", 0, 1), 0.5, ALU.mult, addA, ALU.add)
+    scatter(A("vv"), A("plist", 0, 21), A("vk"))
+
+    def diag(out, src, n):
+        tt(A("dgt", 0, n), src, A("dg", 0, n), ALU.add)
+        scan(A("dgs", 0, n), A("tb", 0, n), A("dgt", 0, n), 2.0 ** 22, ALU.max, ALU.min)
+        cp(out, St("dgs", n))
+
+    def unpack(b, fg, w, gh):
+        act(A(fg, w * b, w * b + 448), A("p%d" % b, 0, 448))
+        act(A(gh, 128 * b, 128 * b + 128), A("p%d" % b, 320, 448))
+
+    unpack(0, "fg1", PL, "gh")
+    unpack(1, "fg1", PL, "gh")
+    diag(A("order", 0, 21), A("vv"), L)
+    act(A("d0"), A("vv", 0, LS), scale=-2.0 ** 88, bias=319.5 * 2.0 ** 88, func=AF.Identity)
+    act(A("ss0"), A("sx0"), li=A("order", 0, 21))
+    for b in range(2, 4):
+        unpack(b, "fg1", PL, "gh")
+    tt(A("inc"), A("vv", 0, LS), A("vv", 1, LS + 1), ALU.subtract)
+    ts(A("el", 0, 1), A("accs", 0, 1), 0.5, ALU.mult, addB, ALU.add)
+
+    def argmax(c):
+        scan(A("st%d" % c, 8, L), A("d0"), A("ss%d" % c, 0, LS), -BIG, ALU.min, ALU.max)
+        tt(A("nr%d" % c), A("st%d" % c, 8, L), A("st%d" % c, 7, L - 1), ALU.is_equal)
+        scan(A("s2", LS * c, LS * c + LS), A("nr%d" % c), A("inc"), 0.0, ALU.mult, ALU.add)
+
+    argmax(0)
+    tt(A("offf"), A("s2", 0, LS), A("kk"), ALU.add, li=A("el", 0, 1))
+    cp(A("offu", 0, 8), A("offf", 0, 8))
+    if rel:
+        r = A("offu", 0, 8)
+        remote(T.rlx[:, 0:8], r[0], r[1], "rinl", rel[2], topo.engines(core, rel[2])[0:8])
+    for b in range(4):
+        f = PL * b
+        tt(B4("at1", 0, 512, b), A("fg1", f, f + 448), A("gh", 128 * b, 128 * b + 128), ALU.add, li=A("offu", 0, 8))
+    if not rel:
+        quant("qa1", "sa1", 0, 128, "at1", 0)
+        send("1", "qa1", "sa1", 128)
+
+    def parts_of_L(qn, sn, M, vl):
+        for b in range(4):
+            mm("p%d" % b, M, "qw", "sw", 128 * b, qn, sn, 0)
+        for b in range(4):
+            o, i = B4(vl, 2560, 2560 + 4 * M, b), A("p%d" % b, 0, M)
+            if b % 2:
+                ts(o, i, 0.03125, ALU.mult)
+            else:
+                act(o, i, scale=0.03125)
+
+    def new_state(vl, M, xt):
+        for b in (0, 2, 1, 3):
+            o, i, li = B4(xt, 0, 1280, b), A(vl, 0, 2560 + 4 * M), A("wu", 20 * b, 20 * b + 20)
+            if b % 2:
+                act(o, i, li=li)
+            else:
+                cp(o, i, li=li)
+
+    def slots(offu, M):
+        scatter(A("sl", 0, 320 + M), offu, A("cid", 0, M))
+        diag(A("slw"), A("sl", 0, 320), 320)
+
+    own = (1, 2)
+
+    def picks(h, tv, win):
+        for b in range(own[h], 4):
+            act(A(tv, 1280 * h + 320 * b, 1280 * h + 320 * b + 320), win(b), li=A("ptu"))
+
+    def trial(h, vl, fg, tv, win):
+        for b in range(4):
+            o = B4(vl, 1280 * h, 1280 * h + 1280, b)
+            if b < own[h]:
+                tt(o, win(b), A(fg, PL * b, PL * b + 320), ALU.add, li=A("ptu"))
+            else:
+                tt(o, A("p%d" % b, 0, 320), A(tv, 1280 * h + 320 * b, 1280 * h + 320 * b + 320), ALU.add)
+        quant("qv", "sv3", 320 * h, 320 * h + 320, vl, 1280 * h)
+        mm("p%d" % (5 + h), 320, "qur", "sur", 0, "qv", "sv3", 320 * h)
+
+    def choose(more):
+        tt(A(more, 0, 320), A("p6", 0, 320), A("t0s"), ALU.is_gt)
+        diag(A("mw"), A(more, 0, 320), 320)
+        ts(A("wf"), A("mw"), 320.0, ALU.mult)
+        tt(A("wf"), A("wf"), A("iw"), ALU.add)
+        tt(A("wf"), A("wf"), A("slw"), ALU.max)
+        for b in range(4):
+            ts(A("wu", 20 * b, 20 * b + 20), A("wf"), 4.0, ALU.mult, float(b), ALU.add)
+
+    def gh2(b, h):
+        return A("gh", 512 + 256 * b + 128 * h, 640 + 256 * b + 128 * h)
+
+    cp(A("ptu"), A("ptw"))
+    for b in range(4):
+        act(gh2(b, 0), B4("at1", 0, 512, b), scale=0.5)
+    picks(0, "tv1", lambda b: gh2(b, 0))
+    cp(A("adf", 8, 16), A("adw"))
+    ts(A("cw"), A("cw"), q_, ALU.add)
+    tt(A("cd", 0, 8), A("cw", 0, 8), A("adf", 8, 16), ALU.subtract)
+    ts(A("no", 0, 8), A("offf", 0, 8), 319.5, ALU.is_ge)
+    tt(A("no", 0, 8), A("no", 0, 8), A("cd", 0, 8), ALU.mult)
+    tt(A("no", 0, 8), A("no", 0, 8), A("adf", 8, 16), ALU.add)
+    cp(A("adu", 0, 8), A("no", 0, 8))
+    for b in range(4):
+        f = PL * b
+        tt(B4("bt1", 0, 512, b), A("gh", 128 * b, 128 * b + 128), A("fg1", f + 320, f + 448), ALU.add, li=A("adu", 0, 8))
+    for b in range(4):
+        act(gh2(b, 1), B4("bt1", 0, 512, b), scale=0.5)
+    picks(1, "tv1", lambda b: gh2(b, 1))
+    trial(0, "vl1", "fg1", "tv1", lambda b: gh2(b, 0))
+    act(A("t0s"), A("p5", 0, 320))
+    trial(1, "vl1", "fg1", "tv1", lambda b: gh2(b, 1))
+    if far:
+        need(E, "arrx", 24)
+        for b in range(4):
+            mm("p%d" % b, 448, "qe", "se", 128 * b, "lcx", "lsx", 0)
+            unpack(b, "fgx", 448, "ghx")
+    slots(A("offu", 0, 8), 128)
+    choose("more")
+    if far:
+        need(V, "arrl", 8)
+        for b in range(4):
+            tt(B4("atx", 0, 512, b), A("fgx", 448 * b, 448 * b + 448), A("ghx", 128 * b, 128 * b + 128), ALU.add, li=A("llx"))
+        quant("qax", "sax", 0, 128, "atx", 0)
+    for c in range(2):
+        act(A("mks", L * c, L * c + L), A("more"), scale=2 * BIG * (1 - 2 * c), bias=-BIG * (1 - 2 * c), func=AF.Relu, li=A("order", 0, 21))
+    count(0, thB, A("accs", 1, 2))
+    act(A("opr", 320, 640), A("more", 0, 320), scale=128.0)
+    ts(A("el", 2, 3), A("accs", 1, 2), 0.5, ALU.mult, addB2, ALU.add)
+    quant("qvv", "svv", 0, 128, "vs", 0)
+    for b in range(4):
+        act(A("fg2", PL * b + 320, PL * b + 576), A("gh", 512 + 256 * b, 768 + 256 * b))
+    if far:
+        parts_of_L("qax", "sax", 128, "vl1")
+    else:
+        need(E, "arr1", 16)
+        parts_of_L("lc1", "ls1", 128, "vl1")
+    new_state("vl1", 128, "xt2")
+    quant("qx", "sx", 0, 320, "xt2", 0)
+    mm("p4", 320, "qur", "sur", 0, "qx", "sx", 0)
+    for b in range(4):
+        mm("p%d" % b, 320, "qe", "se", 128 * b, "qx", "sx", 0)
+    ts(A("pt2f"), A("mw"), 128.0, ALU.mult)
+    tt(A("pt2f"), A("pt2f"), A("ptw"), ALU.add)
+    cp(A("ptu"), A("pt2f"))
+    ts(A("adf", 0, 8), A("cw", 0, 8), 128.0, ALU.add)
+    tt(A("cd"), A("cw"), A("adf"), ALU.subtract)
+
+    tt(A("sx0", 0, 320), A("p4", 0, 320), A("msk"), ALU.subtract)
+    for c in range(2):
+        tt(A("ss%d" % c), A("sx0"), A("mks", L * c, L * c + L), ALU.subtract, li=A("order", 0, 21))
+    for b in range(4):
+        act(A("fg2", PL * b, PL * b + 320), A("p%d" % b, 0, 320))
+    argmax(0)
+    argmax(1)
+    tt(A("off2"), A("s2"), A("kk"), ALU.add, li=A("el", 2, 3))
+    ts(A("no", 0, 8), A("off2", 8, 16), 319.5, ALU.is_ge, 128.0, ALU.mult)
+    tt(A("off2", 8, 16), A("off2", 8, 16), A("no", 0, 8), ALU.add)
+    cp(A("offv"), A("off2"))
+    for b in range(4):
+        f = PL * b
+        tt(B4("g3", 0, 1024, b), A("fg2", f, f + 576), A("gh", 512 + 256 * b, 768 + 256 * b), ALU.add, li=A("offv"))
+    quant("qg", "sg3", 0, 256, "g3", 0)
+    send("2", "qg", "sg3", 256)
+    iota(A("sl"), [[0, 576]], 0, 0)
+
+    def half2(h):
+        for b in range(4):
+            act(A("ab2", 512 * b + 256 * h, 512 * b + 256 * h + 256), B4("g3", 1024 * h, 1024 * h + 1024, b), scale=0.5)
+
+    def ab2(h):
+        return lambda b: A("ab2", 512 * b + 256 * h, 512 * b + 256 * h + 256)
+
+    half2(0)
+    picks(0, "tv2", ab2(0))
+    ts(A("no"), A("off2"), 319.5, ALU.is_ge)
+    tt(A("no"), A("no"), A("cd"), ALU.mult)
+    tt(A("no"), A("no"), A("adf"), ALU.add)
+    cp(A("adu"), A("no"))
+    for b in range(4):
+        f = PL * b
+        tt(B4("g3", 1024, 2048, b), A("gh", 512 + 256 * b, 768 + 256 * b), A("fg2", f + 320, f + 576), ALU.add, li=A("adu"))
+    half2(1)
+    picks(1, "tv2", ab2(1))
+    trial(0, "vl2", "fg2", "tv2", ab2(0))
+    act(A("t0s"), A("p5", 0, 320))
+    trial(1, "vl2", "fg2", "tv2", ab2(1))
+    slots(A("offv"), 256)
+    choose("mor2")
+    act(A("opr", 0, 320), A("mor2"), scale=256.0)
+    quant("qg", "sg3", 256, 512, "g3", 1024)
+    mm("p7", 512, "qvv", "svv", 0, "qg", "sg3", 0)
+    act(A("zs", 0, 512), A("p7"))
+    dma(Y, T.z[:, :], T.zs[:, 0:512], "d_out1", ins=[A("zs", 0, 512)[1]])
+    cp(A("pti"), A("ptr"), li=A("clu"))
+    tt(A("opr", 320, 640), A("opr", 320, 640), A("pti"), ALU.add)
+
+    need(E, "arr2", 24 if far else 16)
+    parts_of_L("lc2", "ls2", 256, "vl2")
+    new_state("vl2", 256, "xt3")
+    quant("qx3", "sx3", 0, 320, "xt3", 0)
+    mm("p4", 320, "qvv", "svv", 0, "qx3", "sx3", 0)
+    dma(Y, T.oc[:, :], T.qx3[:, 0:320].bitcast(dt.uint8), "d_out1", ins=[A("qx3")[1]])
+    for k in range(4):
+        dma(Y, T.osc[4 * k:4 * k + 4, :], T.sx3[32 * k:32 * k + 4, 0:320], "d_out1", ins=[A("sx3")[1]])
+    act(A("zs", 512, 832), A("p4", 0, 320))
+    dma(S, T.y[:, :], T.zs[:, 512:832], "d_out2", ins=[A("zs", 512, 832)[1]])
+    tt(A("opr", 0, 320), A("opr", 0, 320), A("opr", 320, 640), ALU.add)
+    dma(Y, T.op[:, :], T.opr[0:128:16, 0:320], "d_out1", ins=[A("opr", 0, 320)[1]])
+
+    for q in (V, S, E, G):
+        need(G, qsem[q], cnt[q])
+    for s, n in (("d_ptw", 16), ("d_rep", 256), ("d_x", 16), ("d_k", 16), ("d_u", 16), ("d_v", 16), ("d_w", 16), ("d_ws", 16), ("d_ad", 16), ("d_out1", 112), ("d_out2", 16),
+                 ("loc", sent[0])) + ((("arrx", 24), ("arrl", 8), ("arr2", 24)) if far else (("arr1", 16), ("arr2", 16))):
+        need(G, s, n)

@@ -2,9 +2,10 @@ from concourse.bass import DstId, RemoteDMATransfer
 from concourse.mybir import dt, AluOpType as ALU, AxisListType, ActivationFunctionType as AF
 
 F4, BF, I4, U2, C8, S8 = "float32", "bfloat16", "int32", "uint16", "float8_e4m3fn_x4", "uint8"
-PL, L, LS = 576, 336, 328
-NV = 5
-NS = 20 - NV
+P1, P2 = 448, 576
+L = 336
+TW = 352
+V1, LL = 512, 832
 BIG = 2.0 ** 86
 
 
@@ -16,23 +17,25 @@ SCRATCH = {
     "xs": _sb(1280, BF), "ks": _sb(512, BF), "us": _sb(512, BF), "vs": _sb(512, BF),
     "qxk": _sb(448, C8), "sxk": _sb(448, S8), "qu": _sb(128, C8), "su": _sb(128, S8), "qur": _sb(128, C8), "sur": _sb(128, S8),
     "qvv": _sb(128, C8), "svv": _sb(128, S8), "qw": _sb(512, C8), "sw": _sb(512, S8),
-    "et": _sb(2048, BF), "ones": _sb(128, BF), "qe": _sb(512, C8), "se": _sb(512, S8),
-    "ptw": _sb(20, I4), "ptr": _sb(320, I4), "adw": _sb(8, I4), "h16": _sb(320, I4), "lo": _sb(320, I4), "hw16": _sb(20, I4),
-    "pidx": _sb(4, I4), "dgi": _sb(16, I4), "iq": _sb(320, F4), "vk": _sb(L, F4), "dg": _sb(L, F4), "tb": _sb(L, F4), "hb": _sb(144, F4), "cid": _sb(256, F4),
-    "keyr": _sb(320, F4), "junk": _sb(1920, BF), "cmpv": _sb(960, BF),
-    "vv": _sb(L, F4), "dgt": _sb(L, F4), "dgs": _sb(L, F4), "inc": _sb(LS, F4), "d0": _sb(LS, F4), "msk": _sb(320, F4), "mks": _sb(2 * L, F4),
-    "sx0": _sb(464, F4), "ss0": _sb(L, F4), "ss1": _sb(L, F4), "st0": _sb(L, F4), "st1": _sb(L, F4),
-    "nr0": _sb(LS, F4), "nr1": _sb(LS, F4), "s2": _sb(2 * LS, F4), "offu": _sb(16, U2),
-    "fg1": _sb(4 * PL, BF), "fg2": _sb(4 * PL, BF), "gh": _sb(1536, BF), "at1": _sb(512, BF), "bt1": _sb(512, BF), "g3": _sb(2048, BF), "ab2": _sb(2048, BF),
-    "vl1": _sb(4 * 768, BF), "vl2": _sb(4 * 896, BF), "xt2": _sb(1280, BF), "xt3": _sb(1280, BF), "fgx": _sb(1792, BF), "ghx": _sb(512, BF), "atx": _sb(512, BF),
-    "tv1": _sb(2560, BF), "tv2": _sb(2560, BF),
+    "et": _sb(1056, BF), "ones": _sb(128, BF), "qe": _sb(512, C8), "se": _sb(512, S8),
+    "ptw": _sb(20, I4), "adw": _sb(8, I4), "adx": _sb(16, I4), "pidx": _sb(4, I4),
+    "c8": _sb(128, BF), "j16": _sb(128, BF), "tabi": _sb(128, BF), "tabl": _sb(128, BF), "tabm": _sb(256, BF),
+    "ind": _sb(L, BF), "z0": _sb(L, BF), "junk": _sb(320, BF), "rows": _sb(1424, BF), "vk": _sb(L, BF), "cid": _sb(256, BF),
+    "gt": _sb(2 * TW, BF), "ct": _sb(2 * TW, BF), "sel": _sb(2 * TW, BF), "vt": _sb(2 * TW, BF), "mt": _sb(2 * TW, BF), "lt": _sb(2 * TW, BF),
+    "sl1": _sb(128 + TW, BF), "sl2": _sb(256 + TW, BF),
+    "msk": _sb(320, F4), "sx": _sb(328, F4), "ss": _sb(L, F4), "st": _sb(L + 8, F4), "nr": _sb(L, BF), "s2": _sb(L, F4), "d0": _sb(L, F4), "uu": _sb(L, F4),
+    "offu": _sb(16, U2), "opt": _sb(32, F4),
+    "fg1": _sb(4 * P1, BF), "fg2": _sb(4 * P2, BF), "at1": _sb(512, BF), "g3": _sb(2048, BF),
+    "vl": _sb(4 * (LL + 256), BF), "xt2": _sb(1280, BF), "xt3": _sb(1280, BF), "fgx": _sb(4 * P1, BF), "atx": _sb(512, BF),
+    "tv": _sb(2560, BF), "gh": _sb(512, BF), "gh2": _sb(1024, BF), "ghx": _sb(512, BF),
     "qa1": _sb(128, C8), "sa1": _sb(128, S8), "qax": _sb(128, C8), "sax": _sb(128, S8), "qg": _sb(512, C8), "sg3": _sb(512, S8), "qv": _sb(640, C8), "sv3": _sb(640, S8),
-    "qx": _sb(320, C8), "sx": _sb(320, S8), "qx3": _sb(320, C8), "sx3": _sb(320, S8),
-    "t0s": _sb(320, F4), "more": _sb(464, F4), "mor2": _sb(320, F4), "sl": _sb(576, F4), "pti": _sb(320, F4), "opr": _sb(640, F4), "zs": _sb(832, F4),
+    "qx": _sb(320, C8), "sx2": _sb(320, S8), "qx3": _sb(320, C8), "sx3": _sb(320, S8),
+    "t0s": _sb(320, F4), "zs": _sb(832, F4),
     "lcx": _sb(448, C8), "lsx": _sb(448, S8), "llx": _sb(8, U2), "lc1": _sb(128, C8), "ls1": _sb(128, S8), "lc2": _sb(256, C8), "ls2": _sb(256, S8),
     "rcx": _sb(224, C8), "rsx": _sb(448, S8), "rlx": _sb(8, U2), "rc2": _sb(128, C8), "rs2": _sb(256, S8),
 }
-ALIAS = {}
+ALIAS = {"gate": ("rows", 16, L), "cum": ("rows", 368, L), "vv": ("rows", 720, L), "more": ("rows", 1072, 320)}
+PADS = [(0, 16), (352, 368), (704, 720), (1056, 1072), (1392, 1424)]
 
 
 def _pack(base, dtype, parts):
@@ -43,12 +46,12 @@ def _pack(base, dtype, parts):
     SCRATCH[base] = _sb(at, dtype)
 
 
-_pack("sm", F4, [("cst", 16), ("iw", 20), ("iw32", 20), ("clf", 22), ("uif", 8), ("vsrc", 16), ("kk", 16), ("cw", 16), ("dg16", 16), ("keyw", 20), ("hwf", 20), ("acc", 16), ("accs", 2),
-                 ("cntv", 8), ("posa", 20), ("offf", 16), ("off2", 16), ("adf", 16), ("cd", 16), ("no", 16), ("pt2f", 20), ("mw", 20), ("slw", 20), ("wf", 20)])
-_pack("ul", U2, [("clu", 20), ("uiu", 8), ("dgl", 22), ("plist", 22), ("el", 4), ("order", 22), ("offv", 16), ("adu", 16), ("ptu", 20), ("wu", 80)])
+_pack("sm", F4, [("pt2", 32), ("ptq", 32), ("cst", 16), ("m16", 32), ("c1p", 16), ("colc", 2), ("uif", 8), ("iw", 32), ("cw", 16), ("c1", 16), ("c2", 16), ("acc", 1),
+                 ("o16", 16), ("o8", 8), ("ins", 16), ("adf", 8), ("cd", 8), ("cd2", 16), ("a2", 16), ("slw", 32), ("wf", 32), ("j2", 32), ("t1", 32), ("opv", 32)])
+_pack("ul", U2, [("uiu", 8), ("dl", 2), ("ptu", 20), ("plist", 32), ("el", 2), ("order", 32), ("offv", 16), ("adu", 16), ("l0", 20), ("l1", 20), ("ptv", 20), ("l4", 80), ("wu", 80)])
 for _i in range(8):
     SCRATCH["p%d" % _i] = ("psum", [128, 512], F4)
-_DS = ["d_ptw", "d_rep", "d_x", "d_k", "d_u", "d_v", "d_w", "d_ws", "d_ad", "d_out1", "d_out2"]
+_DS = ["d_ptw", "d_x", "d_k", "d_u", "d_v", "d_w", "d_ws", "d_ad", "d_adx", "d_cp", "d_out1", "d_out2"]
 SEMAPHORES = ["qv_s", "qs_s", "qt_s", "qg_s", "arr1", "arr2", "arrx", "arrl", "rinx", "rinl", "rin2", "loc"] + _DS
 
 
@@ -114,13 +117,16 @@ def rank_program(g, core, T, topo):
             eng[q].wait_ge(T.sem[sem], n)
             seen[q][sem] = n
 
+    def apart(a, b):
+        return a is not None and b is not None and a[0] == b[0] and a[1] != b[1]
+
     def track(q, outs, ins, token=None):
         acc = [(r, True) for r in outs] + [(r, False) for r in ins]
         waits = {}
         for (name, lo, hi, ph), w in acc:
             ps = name[0] == "p" and name[1:].isdigit()
             for (l2, h2, p2, w2, tok, q2) in hist.get(name, []):
-                if l2 < hi and lo < h2 and (ph is None or p2 is None or ph == p2) and (w or w2 or (ps and q2 != q)):
+                if (ps and q2 != q) or (l2 < hi and lo < h2 and not apart(ph, p2) and (w or w2)):
                     waits[tok[0]] = max(waits.get(tok[0], 0), tok[1])
         for s, n in waits.items():
             need(q, s, n)
@@ -138,18 +144,17 @@ def rank_program(g, core, T, topo):
         track(q, [o[1] for o in outs], [i[1] for i in ins])
         f().then_inc(T.sem[qsem[q]], 1)
 
-    def A(name, lo=0, hi=None):
+    def A(name, lo=0, hi=None, step=1, phase=0):
         if name in ALIAS:
             name, at, w = ALIAS[name]
             lo, hi = at + lo, at + (w if hi is None else hi)
         hi = SCRATCH[name][1][1] if hi is None else hi
-        return (T[name][:, lo:hi], (name, lo, hi, None))
+        if step == 1:
+            return (T[name][:, lo:hi], (name, lo, hi, None))
+        return (T[name][:, lo + phase:hi:step], (name, lo, hi, (step, (lo + phase) % step)))
 
     def B4(name, lo, hi, b):
-        return (T[name][:, lo + b:hi:4], (name, lo, hi, b))
-
-    def St(name, hi, lo=15, step=16):
-        return (T[name][:, lo:hi:step], (name, 0, hi, None))
+        return A(name, lo, hi, 4, b)
 
     def ind(a, li):
         return a[0] if li is None else a[0].indirect(li[0])
@@ -179,7 +184,17 @@ def rank_program(g, core, T, topo):
         run(V, [o], [], lambda: g.vector.memset(o[0], c))
 
     def scan(o, a, b, init, op0, op1):
-        run(V, [o], [a, b], lambda: g.vector.tensor_tensor_scan(o[0], a[0], b[0], init, op0, op1))
+        run(V, [o], [a, b] + opt(init), lambda: g.vector.tensor_tensor_scan(o[0], a[0], b[0], val(init), op0, op1))
+
+    def turn1(o, a):
+        run(V, [o], [a], lambda: g.vector.transpose(o[0], a[0]))
+
+    def turn(o, name, lo):
+        if name in ALIAS:
+            name, at, _ = ALIAS[name]
+            lo += at
+        turn1(A(o, 0, TW), A(name, lo, lo + TW))
+        turn1(A(o, TW, 2 * TW), A(name, lo - 16, lo - 16 + TW))
 
     def act(o, a, scale=1.0, bias=0.0, func=None, li=None, accum=None):
         fn = AF.Copy if func is None else func
@@ -188,14 +203,14 @@ def rank_program(g, core, T, topo):
             kw = {}
             if isinstance(bias, tuple) or bias != 0.0:
                 kw["bias"] = val(bias)
-            if scale != 1.0:
-                kw["scale"] = scale
+            if isinstance(scale, tuple) or scale != 1.0:
+                kw["scale"] = val(scale)
             if accum is not None:
                 kw["accum_out"] = accum[0]
             return g.scalar.activation(o[0], ind(a, li), fn, **kw)
-        run(S, [o] + opt(accum), [a] + opt(li, bias), f)
+        run(S, [o] + opt(accum), [a] + opt(li, bias, scale), f)
 
-    def iota(o, pattern, base, cm):
+    def iota(o, pattern, base, cm=0):
         def f():
             if SCRATCH[o[1][0]][2] == I4:
                 return g.iota(o[0], pattern, base, cm)
@@ -246,321 +261,318 @@ def rank_program(g, core, T, topo):
         remote(T["rs" + tag][:, 0:n], s[0], s[1], "rin" + tag, rel[2], topo.engines(core, rel[2])[0:8])
 
     load(S, "ptw", T.pt[:, :], "d_ptw")
-    for q in range(16):
-        dma(S if q % 2 else Y, T.ptr[q:128:16, :], T.pt[:, :], "d_rep", n=256)
-    hist["ptr"] = [(0, 320, None, True, ("d_rep", 256), "dma")]
-    load(Y, "us", T.u[:, :], "d_u")
-    load(S, "xs", T.x[:, :], "d_x")
+    load(Y, "xs", T.x[:, :], "d_x")
+    load(S, "us", T.u[:, :], "d_u")
     load(Y, "ks", T.k[:, :], "d_k")
+    load(S, "adw", T.ad[:, :], "d_ad")
     dma(Y, T.qw[:, 0:512].bitcast(dt.uint8), T.wc[:, :], "d_w", outs=[("qw", 0, 512, None)])
     load(Y, "sw", T.ws[:, :], "d_ws")
-    load(Y, "adw", T.ad[:, :], "d_ad")
     load(Y, "vs", T.v[:, :], "d_v")
 
-    iota(A("pidx", 0, 1), [[1, 1]], 0, 1)
-    iota(A("iq"), [[1, 16], [16, 20]], 0, 0)
-    iota(A("iw"), [[16, 20]], 0, 0)
-    iota(A("clf"), [[1, 22]], 0, 0)
-    iota(A("dgi"), [[1, 16]], 128, -1)
-    iota(A("uif"), [[16, 8]], 0, 0)
-    iota(A("kk"), [[0, 2], [16, 8]], 336, 0)
-    iota(A("hb"), [[1, 9], [0, 16]], 0, 0)
     fill(A("ones"), 0.5)
     fill(A("et"), 0.0)
-    for b in range(4):
-        o, i = B4("et", 512 * b, 512 * b + 512, b), A("ones")
+    iota(A("pidx", 0, 1), [[1, 1]], 0, 17)
+    iota(A("c8"), [[1, 16], [0, 8]], 0)
+    iota(A("j16"), [[0, 8], [1, 16]], 0)
+    for h in range(2):
+        o, i = A("et", 528 * h, 528 * h + 512, 4, 2 + h), A("ones")
         run(G, [o], [i], lambda: g.affine_select(o[0], i[0], [[-1, 128]], ALU.is_equal, 0.0, 0, 1))
-    iota(A("vk", 0, 320), [[1, 320]], 0, 0)
-    iota(A("vsrc"), [[16, 16]], 336, 0)
-    iota(A("tb"), [[0, L]], 0, 0)
-    iota(St("tb", L, 0), [[0, 21]], 2 ** 22, 0)
-    iota(A("st0", 0, 8), [[0, 8]], 0, 0)
-    iota(A("st1", 0, 8), [[0, 8]], 0, 0)
-    iota(A("cw"), [[16, 16]], 0, 0)
+    iota(A("uif"), [[16, 8]], 0)
+    iota(A("colc"), [[256, 2]], 15)
+    iota(A("vk", 16, L), [[1, 320]], -128)
+    iota(A("m16"), [[16, 32]], 0)
+    iota(A("c1p"), [[16, 8], [0, 2]], -528)
+    iota(A("cid"), [[1, 256]], 1)
+    iota(A("sl1"), [[0, 128 + TW]], -1024)
 
-    pf, q_, q8, thA, thB, addA, addB, addB2, tmpc, q20 = [A("cst", j, j + 1) for j in range(10)]
-    qi, q8i = A("pidx", 1, 2), A("pidx", 2, 3)
-    act(A("iq"), A("iq"), scale=0.03125)
-    ts(qi, A("pidx", 0, 1), 15, ALU.bitwise_and)
-    ts(q8i, A("pidx", 0, 1), 7, ALU.bitwise_and)
-    cp(q_, qi)
-    cp(q8, q8i)
-    ts(A("dgl"), A("clf"), 0.0, ALU.mult, q_, ALU.add)
-    ts(A("dgi"), A("dgi"), 15, ALU.bitwise_and)
-    ts(A("dg16"), A("dgi"), 0.0, ALU.not_equal, 2.0 ** 20, ALU.mult)
-    ts(A("iw"), A("iw"), q_, ALU.add)
-    ts(A("iw32"), A("iw"), 0.03125, ALU.mult)
-    ts(thA, q_, 16.0, ALU.mult, 14.0, ALU.add)
-    ts(thB, q8, 16.0, ALU.mult, 14.0, ALU.add)
-    ts(tmpc, q_, 15.0, ALU.is_equal, -336.0, ALU.mult)
-    ts(addA, q_, tmpc, ALU.add, 161.0, ALU.add)
-    ts(addB, q8, 160.0, ALU.add)
-    ts(pf, q_, 8.0, ALU.is_ge, float(LS), ALU.mult)
-    tt(addB2, addB, pf, ALU.add)
-    ts(q20, q_, 20.0, ALU.mult)
+    q_, par, odd, s16 = [A("cst", j, j + 1) for j in range(4)]
+    fill(A("adx"), 0)
+    for l in range(8):
+        dma(Y, T.adx[2 * l + 1:128:16, 0:16], T.ad[l:128:8, :], "d_adx", n=128, outs=[("adx", 0, 16, None)] if l == 0 else ())
+    for j, m in enumerate((15, 16, 1)):
+        ts(A("pidx", 1 + j, 2 + j), A("pidx", 0, 1), m, ALU.bitwise_and)
+    fill(A("sm", 0, 64), 0.0)
+    cp(A("cst", 0, 3), A("pidx", 1, 4))
+    fill(A("z0"), 0.0)
+    ts(A("tabi"), A("c8"), q_, ALU.is_equal)
+    ts(A("tabl"), A("c8"), q_, ALU.is_lt)
+    ts(A("z0", 0, 1), q_, -129.0, ALU.add)
+    ts(s16, q_, 16.0, ALU.mult)
+    ts(A("ind", 0, 16), A("j16", 0, 16), q_, ALU.is_equal)
+    ts(s16, par, 23.0, ALU.mult, s16, ALU.add)
+    for h in range(2):
+        ts(A("tabm", 128 * h, 128 * h + 128), A("j16"), q_, ALU.not_equal, BIG, ALU.mult)
+    for lo, hi in PADS:
+        fill(A("rows", lo, hi), 0.0)
+    fill(A("vk", 0, 16), -768.0)
+    fill(A("sx", 0, 8), -BIG / 2)
+    fill(A("st", 0, 8), 0.0)
+    for b in range(4):
+        quant("qe", "se", 128 * b, 128 * b + 128, "et", 528 * (b % 2) + 2 - 2 * (b // 2))
     cp(A("uiu"), A("uif"))
-    ts(A("clu"), A("clf", 0, 20), q20, ALU.add)
-    act(A("dg"), A("dg16"), li=A("dgl", 0, 21))
-    act(A("kk"), A("kk"), bias=q_, func=AF.Identity)
-    act(A("sx0", 320, 464), A("hb"), scale=2.0 ** 80, bias=-32 * 2.0 ** 80, func=AF.Identity)
-    act(A("more", 320, 464), A("hb"), scale=0.0, bias=0.5, func=AF.Identity)
+    ts(A("dl"), A("colc"), s16, ALU.add, 2.0 * TW - 1, ALU.min)
 
-    ts(A("h16"), A("ptr"), 0x70, ALU.bitwise_and)
-    ts(A("hw16"), A("ptw"), 0x70, ALU.bitwise_and)
-    tt(A("keyr"), A("h16"), A("iq"), ALU.add)
-    tt(A("keyw"), A("hw16"), A("iw32"), ALU.add)
-
-    def count(k, bias, out):
-        j = 320 * (k % 6)
-        act(A("junk", j, j + 320), A("keyr"), scale=-1.0, bias=bias, func=AF.Sign, accum=out)
-
-    for k in range(NS):
-        count(k, A("keyw", k, k + 1), A("acc", k, k + 1))
-    count(NS, thA, A("accs", 0, 1))
-
-    def lane(j):
-        o, c = A("cntv", j, j + 1), A("cmpv", 320 * (j % 3), 320 * (j % 3) + 320)
-        ts(c, A("keyr"), A("keyw", NS + j, NS + j + 1), ALU.is_lt)
-        run(V, [o], [c], lambda: g.vector.tensor_reduce(o[0], c[0], AxisListType.X, ALU.add))
-
-    lane(0)
-    lane(1)
-    quant("qxk", "sxk", 0, 320, "xs", 0)
-    quant("qxk", "sxk", 320, 448, "ks", 0)
+    cp(A("ptu"), A("ptw"))
+    act(A("junk"), A("tabl"), li=A("ptu"), accum=A("acc"))
+    cp(A("ind", 16, L), A("tabi"), li=A("ptu"))
+    quant("qu", "su", 0, 128, "us", 0)
+    ts(A("gate"), A("ind"), 1024.0, ALU.mult, -512.0, ALU.add)
+    o1, i1, l1 = A("qur"), A("qu"), A("uiu")
+    act(A("sur"), A("su"), li=l1)
+    scan(A("cum"), A("ind"), A("z0"), A("acc"), ALU.add, ALU.add)
+    turn("gt", "gate", 0)
+    turn("ct", "cum", 0)
+    run(V, [o1], [i1, l1], lambda: g.vector.tensor_copy(T.qur[:, 0:128].bitcast(dt.uint32), T.qu[:, 0:128].bitcast(dt.uint32).indirect(l1[0])))
+    scan(A("sel"), A("gt"), A("ct"), 0.0, ALU.max, ALU.min)
+    quant("qxk", "sxk", 128, 448, "xs", 0)
+    ts(A("plist"), A("sel"), 128.0, ALU.add, li=A("dl"))
+    quant("qxk", "sxk", 0, 128, "ks", 0)
     if rel:
         send("x", "qxk", "sxk", 448)
-    iota(A("cid"), [[1, 256]], 640, 0)
-    iota(A("sl", 0, 448), [[0, 448]], 0, 0)
-    quant("qu", "su", 0, 128, "us", 0)
-    o1, i1, l1 = A("qur"), A("qu"), A("uiu")
-    run(V, [o1], [i1, l1], lambda: g.vector.tensor_copy(T.qur[:, 0:128].bitcast(dt.uint32), T.qu[:, 0:128].bitcast(dt.uint32).indirect(l1[0])))
-    cp(A("sur"), A("su"), li=l1)
-    mm("p4", 320, "qur", "sur", 0, "qxk", "sxk", 0)
-    quant("qe", "se", 0, 512, "et", 0)
+    mm("p4", 320, "qur", "sur", 0, "qxk", "sxk", 128)
     for b in range(4):
         mm("p%d" % b, 448, "qe", "se", 128 * b, "qxk", "sxk", 0)
-    for j in range(2, NV):
-        lane(j)
-    ts(A("lo"), A("ptr"), 15, ALU.bitwise_and)
-    ts(A("msk"), A("lo"), q_, ALU.not_equal, BIG, ALU.mult, li=A("clu"))
-    ts(A("vk", 320, 336), A("vsrc"), 448.0, ALU.min, q_, ALU.add)
-    ts(A("vk", 335, 336), q_, 320.0, ALU.add)
-    ts(A("hwf"), A("hw16"), 0.0625, ALU.mult)
-    tt(A("sx0", 0, 320), A("p4", 0, 320), A("msk"), ALU.subtract)
-    ts(A("posa", NS, 20), A("cntv", 0, NV), 1.0, ALU.add)
-    ts(A("posa", 0, NS), A("acc", 0, NS), 0.5, ALU.mult, 160.5, ALU.add)
-    tt(A("posa"), A("posa"), A("hwf"), ALU.add)
-    cp(A("plist", 0, 20), A("posa"))
-    ts(A("plist", 20, 21), A("accs", 0, 1), 0.5, ALU.mult, addA, ALU.add)
+    act(A("msk"), A("tabm", 0, 128), li=A("ptu"))
+    act(A("cw"), A("m16", 0, 16), bias=q_, func=AF.Identity)
+    act(A("c1"), A("c1p"), bias=q_, func=AF.Identity)
+    act(A("iw"), A("m16"), bias=q_, func=AF.Identity)
+    act(A("c2"), A("cw"), bias=-656.0, func=AF.Identity)
+    act(A("iw"), A("iw"), scale=1.0 / 512)
     scatter(A("vv"), A("plist", 0, 21), A("vk"))
+    ts(A("el", 0, 1), A("cum", L - 1, L), 128.0, ALU.add)
+    turn("vt", "vv", 0)
+    tt(A("sx", 8, 328), A("p4", 0, 320), A("msk"), ALU.subtract)
+    ts(A("order"), A("vt"), 136.0, ALU.add, 0.0, ALU.max, li=A("dl"))
 
-    def diag(out, src, n):
-        tt(A("dgt", 0, n), src, A("dg", 0, n), ALU.add)
-        scan(A("dgs", 0, n), A("tb", 0, n), A("dgt", 0, n), 2.0 ** 22, ALU.max, ALU.min)
-        cp(out, St("dgs", n))
+    def unpack1(b):
+        act(A("fg1", P1 * b, P1 * b + P1), A("p%d" % b, 0, P1), scale=0.5)
 
-    def unpack(b, fg, w, gh):
-        act(A(fg, w * b, w * b + 448), A("p%d" % b, 0, 448))
-        act(A(gh, 128 * b, 128 * b + 128), A("p%d" % b, 320, 448))
+    unpack1(0)
+    unpack1(1)
+    act(A("d0"), A("vv"), scale=2.0 ** 80, bias=200 * 2.0 ** 80, func=AF.Identity)
+    act(A("uu"), A("vv"), bias=-272.0, func=AF.Identity)
+    unpack1(2)
+    unpack1(3)
+    for b in range(4):
+        act(A("gh", 128 * b, 128 * b + 128), A("p%d" % b, 0, 128), scale=0.5)
 
-    unpack(0, "fg1", PL, "gh")
-    unpack(1, "fg1", PL, "gh")
-    diag(A("order", 0, 21), A("vv"), L)
-    act(A("d0"), A("vv", 0, LS), scale=-2.0 ** 88, bias=319.5 * 2.0 ** 88, func=AF.Identity)
-    act(A("ss0"), A("sx0"), li=A("order", 0, 21))
-    for b in range(2, 4):
-        unpack(b, "fg1", PL, "gh")
-    tt(A("inc"), A("vv", 0, LS), A("vv", 1, LS + 1), ALU.subtract)
-    ts(A("el", 0, 1), A("accs", 0, 1), 0.5, ALU.mult, addB, ALU.add)
+    def argmax(fills):
+        fills = list(fills) + [lambda: None] * 4
+        fills[0]()
+        cp(A("ss"), A("sx"), li=A("order", 0, 21))
+        fills[1]()
+        scan(A("st", 8, L + 8), A("d0"), A("ss"), -BIG, ALU.min, ALU.max)
+        fills[2]()
+        tt(A("nr"), A("st", 8, L + 8), A("st", 7, L + 7), ALU.is_equal)
+        fills[3]()
+        scan(A("s2"), A("nr"), A("uu"), 0.0, ALU.mult, ALU.min)
 
-    def argmax(c):
-        scan(A("st%d" % c, 8, L), A("d0"), A("ss%d" % c, 0, LS), -BIG, ALU.min, ALU.max)
-        tt(A("nr%d" % c), A("st%d" % c, 8, L), A("st%d" % c, 7, L - 1), ALU.is_equal)
-        scan(A("s2", LS * c, LS * c + LS), A("nr%d" % c), A("inc"), 0.0, ALU.mult, ALU.add)
-
-    argmax(0)
-    tt(A("offf"), A("s2", 0, LS), A("kk"), ALU.add, li=A("el", 0, 1))
-    cp(A("offu", 0, 8), A("offf", 0, 8))
+    argmax([lambda: ts(A("pt2", 0, 20), A("ptw"), 2.0, ALU.mult),
+            lambda: cp(A("adf"), A("adw")),
+            lambda: cp(A("l0"), A("pt2", 0, 20)),
+            lambda: ts(A("l1"), A("pt2", 0, 20), 1.0, ALU.add)])
+    tt(A("cd"), A("adf"), A("cw", 0, 8), ALU.subtract)
+    tt(A("o16"), A("s2"), A("c1"), ALU.max, li=A("el", 0, 1))
+    ts(A("ptq", 0, 20), A("ptw"), 1.0 / 128, ALU.mult)
+    tt(A("o8"), A("o16", 0, 16, 2, 0), A("o16", 0, 16, 2, 1), ALU.max)
+    ts(A("offu", 0, 8), A("o8"), 528.0, ALU.add)
     if rel:
         r = A("offu", 0, 8)
         remote(T.rlx[:, 0:8], r[0], r[1], "rinl", rel[2], topo.engines(core, rel[2])[0:8])
-    for b in range(4):
-        f = PL * b
-        tt(B4("at1", 0, 512, b), A("fg1", f, f + 448), A("gh", 128 * b, 128 * b + 128), ALU.add, li=A("offu", 0, 8))
-    if not rel:
-        quant("qa1", "sa1", 0, 128, "at1", 0)
-        send("1", "qa1", "sa1", 128)
 
-    def parts_of_L(qn, sn, M, vl):
-        for b in range(4):
-            mm("p%d" % b, M, "qw", "sw", 128 * b, qn, sn, 0)
-        for b in range(4):
-            o, i = B4(vl, 2560, 2560 + 4 * M, b), A("p%d" % b, 0, M)
-            if b % 2:
-                ts(o, i, 0.03125, ALU.mult)
-            else:
-                act(o, i, scale=0.03125)
+    def a1(b):
+        tt(A("fg2", P2 * b, P2 * b + 256, 2, 0), A("fg1", P1 * b, P1 * b + P1), A("gh", 128 * b, 128 * b + 128), ALU.add, li=A("offu", 0, 8))
+        if not rel:
+            act(B4("at1", 0, 512, b), A("fg2", P2 * b, P2 * b + 256, 2, 0), scale=2.0)
 
-    def new_state(vl, M, xt):
-        for b in (0, 2, 1, 3):
-            o, i, li = B4(xt, 0, 1280, b), A(vl, 0, 2560 + 4 * M), A("wu", 20 * b, 20 * b + 20)
+    def b1(b):
+        tt(A("fg2", P2 * b, P2 * b + 256, 2, 1), A("fg1", P1 * b, P1 * b + 128), A("gh", 128 * b, 128 * b + 128), ALU.add, li=A("adu", 0, 8))
+        o, i = A("gh2", 256 * b, 256 * b + 256), A("fg2", P2 * b, P2 * b + 256)
+        dma(Y, o[0], i[0], "d_cp", n=64, outs=[o[1]], ins=[i[1]])
+
+    def near(n, o, cd):
+        return [lambda: ts(A("ins", 0, n), o, -400.0, ALU.is_ge),
+                lambda: tt(A("ins", 0, n), A("ins", 0, n), cd, ALU.mult),
+                lambda: tt(A("ins", 0, n), A("ins", 0, n), A("cw", 0, n), ALU.add),
+                lambda: cp(A("adu", 0, n), A("ins", 0, n))]
+
+    def pick(h, b, win, li, scale):
+        act(A("tv", 1280 * h + 320 * b, 1280 * h + 320 * b + 320), win, li=li, scale=scale)
+
+    at = [128]
+
+    def add(h, b):
+        tt(B4("vl", 4 * V1 * h, 4 * V1 * h + 1280, b), A("p%d" % b, at[0], at[0] + 320), A("tv", 1280 * h + 320 * b, 1280 * h + 320 * b + 320), ALU.add)
+
+    def score(h):
+        quant("qv", "sv3", 320 * h, 320 * h + 320, "vl", 4 * V1 * h)
+        mm("p%d" % (5 + h), 320, "qur", "sur", 0, "qv", "sv3", 320 * h)
+
+    def slot_scatter(sl, offs, M):
+        scatter(A(sl, 0, M + 320), offs, A("cid", 0, M))
+
+    def slot_list(sl, M):
+        turn("lt", sl, M)
+        ts(A("slw"), A("lt"), LL - 1.0, ALU.add, 1.0 / 512, ALU.mult, li=A("dl"))
+
+    def choose():
+        tt(A("more"), A("p6", 0, 320), A("t0s"), ALU.is_gt)
+        turn("mt", "more", 0)
+        tt(A("wf"), A("mt"), A("iw"), ALU.add, li=A("dl"))
+
+    def choose2():
+        tt(A("wf"), A("wf"), A("slw"), ALU.max)
+
+    def choose3():
+        for b in (1, 0, 3, 2):
+            ts(A("wu", 20 * b, 20 * b + 20), A("wf", 0, 20), 2048.0, ALU.mult, float(b), ALU.add)
+
+    def layer(qn, sn, M, banks):
+        for b in range(4):
+            mm(banks[b], M, "qw", "sw", 128 * b, qn, sn, 0)
+
+    def part_of_L(b, M, banks, q):
+        o, i = B4("vl", 4 * LL, 4 * LL + 4 * M, b), A(banks[b], 0, M)
+        if q == V:
+            ts(o, i, 0.03125, ALU.mult)
+        else:
+            act(o, i, scale=0.03125)
+
+    def new_state(M, xt):
+        for b in (1, 0, 3, 2):
+            o, i, li = B4(xt, 0, 1280, b), A("vl", 0, 4 * LL + 4 * M), A("wu", 20 * b, 20 * b + 20)
             if b % 2:
                 act(o, i, li=li)
             else:
                 cp(o, i, li=li)
 
-    def slots(offu, M):
-        scatter(A("sl", 0, 320 + M), offu, A("cid", 0, M))
-        diag(A("slw"), A("sl", 0, 320), 320)
-
-    own = (1, 2)
-
-    def picks(h, tv, win):
-        for b in range(own[h], 4):
-            act(A(tv, 1280 * h + 320 * b, 1280 * h + 320 * b + 320), win(b), li=A("ptu"))
-
-    def trial(h, vl, fg, tv, win):
-        for b in range(4):
-            o = B4(vl, 1280 * h, 1280 * h + 1280, b)
-            if b < own[h]:
-                tt(o, win(b), A(fg, PL * b, PL * b + 320), ALU.add, li=A("ptu"))
-            else:
-                tt(o, A("p%d" % b, 0, 320), A(tv, 1280 * h + 320 * b, 1280 * h + 320 * b + 320), ALU.add)
-        quant("qv", "sv3", 320 * h, 320 * h + 320, vl, 1280 * h)
-        mm("p%d" % (5 + h), 320, "qur", "sur", 0, "qv", "sv3", 320 * h)
-
-    def choose(more):
-        tt(A(more, 0, 320), A("p6", 0, 320), A("t0s"), ALU.is_gt)
-        diag(A("mw"), A(more, 0, 320), 320)
-        ts(A("wf"), A("mw"), 320.0, ALU.mult)
-        tt(A("wf"), A("wf"), A("iw"), ALU.add)
-        tt(A("wf"), A("wf"), A("slw"), ALU.max)
-        for b in range(4):
-            ts(A("wu", 20 * b, 20 * b + 20), A("wf"), 4.0, ALU.mult, float(b), ALU.add)
-
-    def gh2(b, h):
-        return A("gh", 512 + 256 * b + 128 * h, 640 + 256 * b + 128 * h)
-
-    cp(A("ptu"), A("ptw"))
+    steps = near(8, A("o8"), A("cd"))
     for b in range(4):
-        act(gh2(b, 0), B4("at1", 0, 512, b), scale=0.5)
-    picks(0, "tv1", lambda b: gh2(b, 0))
-    cp(A("adf", 8, 16), A("adw"))
-    ts(A("cw"), A("cw"), q_, ALU.add)
-    tt(A("cd", 0, 8), A("cw", 0, 8), A("adf", 8, 16), ALU.subtract)
-    ts(A("no", 0, 8), A("offf", 0, 8), 319.5, ALU.is_ge)
-    tt(A("no", 0, 8), A("no", 0, 8), A("cd", 0, 8), ALU.mult)
-    tt(A("no", 0, 8), A("no", 0, 8), A("adf", 8, 16), ALU.add)
-    cp(A("adu", 0, 8), A("no", 0, 8))
+        steps[b]()
+        a1(b)
     for b in range(4):
-        f = PL * b
-        tt(B4("bt1", 0, 512, b), A("gh", 128 * b, 128 * b + 128), A("fg1", f + 320, f + 448), ALU.add, li=A("adu", 0, 8))
+        b1(b)
+        pick(0, b, A("fg2", P2 * b, P2 * b + 256), A("l0"), 1.0)
+    if not rel:
+        quant("qa1", "sa1", 0, 128, "at1", 0)
+        send("1", "qa1", "sa1", 128)
+    iota(A("vl", 1280, 4 * V1), [[0, 4 * V1 - 1280]], 0)
+    iota(A("sl2"), [[0, 256 + TW]], -1024)
+    slot_scatter("sl1", A("offu", 0, 8), 128)
     for b in range(4):
-        act(gh2(b, 1), B4("bt1", 0, 512, b), scale=0.5)
-    picks(1, "tv1", lambda b: gh2(b, 1))
-    trial(0, "vl1", "fg1", "tv1", lambda b: gh2(b, 0))
-    act(A("t0s"), A("p5", 0, 320))
-    trial(1, "vl1", "fg1", "tv1", lambda b: gh2(b, 1))
+        pick(1, b, A("fg2", P2 * b, P2 * b + 256), A("l1"), 1.0)
+    add(0, 0)
+    add(0, 1)
+    slot_list("sl1", 128)
+    add(0, 2)
+    add(0, 3)
+    score(0)
+    xb = ["p4", "p7", "p4", "p7"]
     if far:
         need(E, "arrx", 24)
-        for b in range(4):
-            mm("p%d" % b, 448, "qe", "se", 128 * b, "lcx", "lsx", 0)
-            unpack(b, "fgx", 448, "ghx")
-    slots(A("offu", 0, 8), 128)
-    choose("more")
+        for b in range(2):
+            mm(xb[b], P1, "qe", "se", 128 * b, "lcx", "lsx", 0)
+    quant("qvv", "svv", 0, 128, "vs", 0)
+    ts(A("a2", 0, 16, 2, 0), A("adx", 0, 8), 2.0, ALU.mult, 1.0, ALU.add)
+    ts(A("a2", 0, 16, 2, 1), A("adx", 8, 16), 2.0, ALU.mult, 1.0, ALU.add)
+    ts(A("cd2"), A("cw"), 1.0, ALU.add, odd, ALU.mult)
+    for b in range(4):
+        add(1, b)
+    act(A("t0s"), A("p5", 0, 320))
+    score(1)
+    tt(A("cd2"), A("a2"), A("cd2"), ALU.subtract)
+    lb = ["p0", "p1", "p2", "p3"]
     if far:
+        for b in range(4):
+            if b >= 2:
+                mm(xb[b], P1, "qe", "se", 128 * b, "lcx", "lsx", 0)
+            act(A("fgx", P1 * b, P1 * b + P1), A(xb[b], 0, P1))
+            act(A("ghx", 128 * b, 128 * b + 128), A(xb[b], 0, 128))
         need(V, "arrl", 8)
         for b in range(4):
-            tt(B4("atx", 0, 512, b), A("fgx", 448 * b, 448 * b + 448), A("ghx", 128 * b, 128 * b + 128), ALU.add, li=A("llx"))
+            if b == 2:
+                choose()
+            tt(B4("atx", 0, 512, b), A("fgx", P1 * b, P1 * b + P1), A("ghx", 128 * b, 128 * b + 128), ALU.add, li=A("llx"))
         quant("qax", "sax", 0, 128, "atx", 0)
-    for c in range(2):
-        act(A("mks", L * c, L * c + L), A("more"), scale=2 * BIG * (1 - 2 * c), bias=-BIG * (1 - 2 * c), func=AF.Relu, li=A("order", 0, 21))
-    count(0, thB, A("accs", 1, 2))
-    act(A("opr", 320, 640), A("more", 0, 320), scale=128.0)
-    ts(A("el", 2, 3), A("accs", 1, 2), 0.5, ALU.mult, addB2, ALU.add)
-    quant("qvv", "svv", 0, 128, "vs", 0)
-    for b in range(4):
-        act(A("fg2", PL * b + 320, PL * b + 576), A("gh", 512 + 256 * b, 768 + 256 * b))
-    if far:
-        parts_of_L("qax", "sax", 128, "vl1")
+        layer("qax", "sax", 128, lb)
     else:
         need(E, "arr1", 16)
-        parts_of_L("lc1", "ls1", 128, "vl1")
-    new_state("vl1", 128, "xt2")
-    quant("qx", "sx", 0, 320, "xt2", 0)
-    mm("p4", 320, "qur", "sur", 0, "qx", "sx", 0)
+        layer("lc1", "ls1", 128, lb)
+        choose()
     for b in range(4):
-        mm("p%d" % b, 320, "qe", "se", 128 * b, "qx", "sx", 0)
-    ts(A("pt2f"), A("mw"), 128.0, ALU.mult)
-    tt(A("pt2f"), A("pt2f"), A("ptw"), ALU.add)
-    cp(A("ptu"), A("pt2f"))
-    ts(A("adf", 0, 8), A("cw", 0, 8), 128.0, ALU.add)
-    tt(A("cd"), A("cw"), A("adf"), ALU.subtract)
+        part_of_L(b, 128, lb, S)
+    tt(A("j2"), A("mt"), A("pt2"), ALU.add, li=A("dl"))
+    choose2()
+    cp(A("ptv"), A("j2", 0, 20))
+    choose3()
+    new_state(128, "xt2")
+    act(A("msk"), A("tabm"), li=A("ptv"))
+    quant("qx", "sx2", 0, 320, "xt2", 0)
+    mm("p4", 320, "qur", "sur", 0, "qx", "sx2", 0)
+    for b in range(4):
+        mm("p%d" % b, 320, "qe", "se", 128 * b, "qx", "sx2", 0)
+    for b in range(4):
+        ts(A("l4", 20 * b, 20 * b + 20), A("j2", 0, 20), 4.0, ALU.mult, float(b), ALU.add)
+    tt(A("t1"), A("mt"), A("ptq"), ALU.add, li=A("dl"))
 
-    tt(A("sx0", 0, 320), A("p4", 0, 320), A("msk"), ALU.subtract)
-    for c in range(2):
-        tt(A("ss%d" % c), A("sx0"), A("mks", L * c, L * c + L), ALU.subtract, li=A("order", 0, 21))
+    at[0] = 0
+    tt(A("sx", 8, 328), A("p4", 0, 320), A("msk"), ALU.subtract)
     for b in range(4):
-        act(A("fg2", PL * b, PL * b + 320), A("p%d" % b, 0, 320))
-    argmax(0)
-    argmax(1)
-    tt(A("off2"), A("s2"), A("kk"), ALU.add, li=A("el", 2, 3))
-    ts(A("no", 0, 8), A("off2", 8, 16), 319.5, ALU.is_ge, 128.0, ALU.mult)
-    tt(A("off2", 8, 16), A("off2", 8, 16), A("no", 0, 8), ALU.add)
-    cp(A("offv"), A("off2"))
+        act(A("fg2", P2 * b + 256, P2 * b + P2), A("p%d" % b, 0, 320))
+    argmax([lambda: ts(A("t1"), A("t1"), 0.5, ALU.mult)])
+    tt(A("o16"), A("s2"), A("c2"), ALU.max, li=A("el", 0, 1))
+    ts(A("offv"), A("o16"), 656.0, ALU.add)
+    steps = near(16, A("o16"), A("cd2"))
     for b in range(4):
-        f = PL * b
-        tt(B4("g3", 0, 1024, b), A("fg2", f, f + 576), A("gh", 512 + 256 * b, 768 + 256 * b), ALU.add, li=A("offv"))
+        steps[b]()
+        tt(B4("g3", 0, 1024, b), A("fg2", P2 * b, P2 * b + P2), A("gh2", 256 * b, 256 * b + 256), ALU.add, li=A("offv"))
     quant("qg", "sg3", 0, 256, "g3", 0)
     send("2", "qg", "sg3", 256)
-    iota(A("sl"), [[0, 576]], 0, 0)
-
-    def half2(h):
-        for b in range(4):
-            act(A("ab2", 512 * b + 256 * h, 512 * b + 256 * h + 256), B4("g3", 1024 * h, 1024 * h + 1024, b), scale=0.5)
-
-    def ab2(h):
-        return lambda b: A("ab2", 512 * b + 256 * h, 512 * b + 256 * h + 256)
-
-    half2(0)
-    picks(0, "tv2", ab2(0))
-    ts(A("no"), A("off2"), 319.5, ALU.is_ge)
-    tt(A("no"), A("no"), A("cd"), ALU.mult)
-    tt(A("no"), A("no"), A("adf"), ALU.add)
-    cp(A("adu"), A("no"))
     for b in range(4):
-        f = PL * b
-        tt(B4("g3", 1024, 2048, b), A("gh", 512 + 256 * b, 768 + 256 * b), A("fg2", f + 320, f + 576), ALU.add, li=A("adu"))
-    half2(1)
-    picks(1, "tv2", ab2(1))
-    trial(0, "vl2", "fg2", "tv2", ab2(0))
+        pick(0, b, A("g3", 0, 1024), A("l4", 20 * b, 20 * b + 20), 0.5)
+    for b in range(4):
+        tt(B4("g3", 1024, 2048, b), A("fg2", P2 * b, P2 * b + 256), A("gh2", 256 * b, 256 * b + 256), ALU.add, li=A("adu"))
+    for b in range(4):
+        pick(1, b, A("g3", 1024, 2048), A("l4", 20 * b, 20 * b + 20), 0.5)
+    for b in range(4):
+        add(0, b)
+    score(0)
+    slot_scatter("sl2", A("offv"), 256)
+    add(1, 0)
+    add(1, 1)
+    add(1, 2)
+    add(1, 3)
     act(A("t0s"), A("p5", 0, 320))
-    trial(1, "vl2", "fg2", "tv2", ab2(1))
-    slots(A("offv"), 256)
-    choose("mor2")
-    act(A("opr", 0, 320), A("mor2"), scale=256.0)
+    score(1)
+    slot_list("sl2", 256)
+    need(E, "arr2", 24 if far else 16)
+    layer("lc2", "ls2", 256, lb)
+    for b in range(4):
+        part_of_L(b, 256, lb, S)
+    choose()
     quant("qg", "sg3", 256, 512, "g3", 1024)
     mm("p7", 512, "qvv", "svv", 0, "qg", "sg3", 0)
-    act(A("zs", 0, 512), A("p7"))
-    dma(Y, T.z[:, :], T.zs[:, 0:512], "d_out1", ins=[A("zs", 0, 512)[1]])
-    cp(A("pti"), A("ptr"), li=A("clu"))
-    tt(A("opr", 320, 640), A("opr", 320, 640), A("pti"), ALU.add)
-
-    need(E, "arr2", 24 if far else 16)
-    parts_of_L("lc2", "ls2", 256, "vl2")
-    new_state("vl2", 256, "xt3")
+    choose2()
+    tt(A("opv"), A("mt"), A("t1"), ALU.add, li=A("dl"))
+    choose3()
+    new_state(256, "xt3")
     quant("qx3", "sx3", 0, 320, "xt3", 0)
     mm("p4", 320, "qvv", "svv", 0, "qx3", "sx3", 0)
     dma(Y, T.oc[:, :], T.qx3[:, 0:320].bitcast(dt.uint8), "d_out1", ins=[A("qx3")[1]])
     for k in range(4):
         dma(Y, T.osc[4 * k:4 * k + 4, :], T.sx3[32 * k:32 * k + 4, 0:320], "d_out1", ins=[A("sx3")[1]])
-    act(A("zs", 512, 832), A("p4", 0, 320))
+    for h in range(4):
+        act(A("zs", 128 * h, 128 * h + 128), A("p7", 256 * (h // 2), 256 * (h // 2) + 256, 2, h % 2))
+    dma(S, T.z[:, :], T.zs[:, 0:512], "d_out2", ins=[A("zs", 0, 512)[1]])
+    ts(A("opv"), A("opv"), 256.0, ALU.mult)
+    turn1(A("opt"), A("opv"))
+    cp(A("zs", 512, 832), A("p4", 0, 320))
     dma(S, T.y[:, :], T.zs[:, 512:832], "d_out2", ins=[A("zs", 512, 832)[1]])
-    tt(A("opr", 0, 320), A("opr", 0, 320), A("opr", 320, 640), ALU.add)
-    dma(Y, T.op[:, :], T.opr[0:128:16, 0:320], "d_out1", ins=[A("opr", 0, 320)[1]])
+    for k in range(8):
+        dma(Y, T.op[k:k + 1, :], T.opt[32 * (k // 2):32 * (k // 2) + 20, 16 * (k % 2):16 * (k % 2) + 16], "d_out1", ins=[A("opt")[1]])
 
     for q in (V, S, E, G):
         need(G, qsem[q], cnt[q])
-    for s, n in (("d_ptw", 16), ("d_rep", 256), ("d_x", 16), ("d_k", 16), ("d_u", 16), ("d_v", 16), ("d_w", 16), ("d_ws", 16), ("d_ad", 16), ("d_out1", 112), ("d_out2", 16),
+    for s, n in (("d_ptw", 16), ("d_x", 16), ("d_k", 16), ("d_u", 16), ("d_v", 16), ("d_w", 16), ("d_ws", 16), ("d_ad", 16), ("d_adx", 128), ("d_cp", 64), ("d_out1", 208), ("d_out2", 32),
                  ("loc", sent[0])) + ((("arrx", 24), ("arrl", 8), ("arr2", 24)) if far else (("arr1", 16), ("arr2", 16))):
         need(G, s, n)

@@ -6,6 +6,7 @@ P1, P2 = 448, 576
 L = 336
 TW = 352
 V1, LL = 512, 832
+VB = 1024
 BIG = 2.0 ** 86
 
 
@@ -24,17 +25,17 @@ SCRATCH = {
     "gt": _sb(2 * TW, BF), "ct": _sb(2 * TW, BF), "sel": _sb(2 * TW, BF), "vt": _sb(2 * TW, BF), "mt": _sb(2 * TW, BF), "lt": _sb(2 * TW, BF),
     "sl1": _sb(128 + TW, BF), "sl2": _sb(256 + TW, BF),
     "msk": _sb(320, F4), "sx": _sb(328, F4), "ss": _sb(L, F4), "st": _sb(L + 8, F4), "nr": _sb(L, BF), "s2": _sb(L, F4), "d0": _sb(L, F4), "uu": _sb(L, F4),
-    "offu": _sb(16, U2), "opt": _sb(32, F4),
+    "offu": _sb(16, U2), "opr": _sb(320, F4), "tabo": _sb(512, F4),
     "fg1": _sb(4 * P1, BF), "fg2": _sb(4 * P2, BF), "at1": _sb(512, BF), "g3": _sb(2048, BF),
-    "vl": _sb(4 * (LL + 256), BF), "xt2": _sb(1280, BF), "xt3": _sb(1280, BF), "fgx": _sb(4 * P1, BF), "atx": _sb(512, BF),
-    "tv": _sb(2560, BF), "gh": _sb(512, BF), "gh2": _sb(1024, BF), "ghx": _sb(512, BF),
+    "lvl": _sb(VB + 4 * (LL + 128), BF), "xt2": _sb(1280, BF), "xt3": _sb(1280, BF), "fgx": _sb(4 * P1, BF), "atx": _sb(512, BF),
+    "tv": _sb(2560, BF), "gh": _sb(512, BF), "gd": _sb(1024, BF), "x2": _sb(2048, BF), "ah": _sb(512, BF), "tabg": _sb(128, BF), "ghx": _sb(512, BF),
     "qa1": _sb(128, C8), "sa1": _sb(128, S8), "qax": _sb(128, C8), "sax": _sb(128, S8), "qg": _sb(512, C8), "sg3": _sb(512, S8), "qv": _sb(640, C8), "sv3": _sb(640, S8),
     "qx": _sb(320, C8), "sx2": _sb(320, S8), "qx3": _sb(320, C8), "sx3": _sb(320, S8),
     "t0s": _sb(320, F4), "zs": _sb(832, F4),
     "lcx": _sb(448, C8), "lsx": _sb(448, S8), "llx": _sb(8, U2), "lc1": _sb(128, C8), "ls1": _sb(128, S8), "lc2": _sb(256, C8), "ls2": _sb(256, S8),
     "rcx": _sb(224, C8), "rsx": _sb(448, S8), "rlx": _sb(8, U2), "rc2": _sb(128, C8), "rs2": _sb(256, S8),
 }
-ALIAS = {"gate": ("rows", 16, L), "cum": ("rows", 368, L), "vv": ("rows", 720, L), "more": ("rows", 1072, 320)}
+ALIAS = {"vl": ("lvl", VB, 4 * (LL + 128)), "gate": ("rows", 16, L), "cum": ("rows", 368, L), "vv": ("rows", 720, L), "more": ("rows", 1072, 320)}
 PADS = [(0, 16), (352, 368), (704, 720), (1056, 1072), (1392, 1424)]
 
 
@@ -46,13 +47,14 @@ def _pack(base, dtype, parts):
     SCRATCH[base] = _sb(at, dtype)
 
 
-_pack("sm", F4, [("pt2", 32), ("ptq", 32), ("cst", 16), ("m16", 32), ("c1p", 16), ("colc", 2), ("uif", 8), ("iw", 32), ("cw", 16), ("c1", 16), ("c2", 16), ("acc", 1),
+_pack("sm", F4, [("pt2", 32), ("ptq", 32), ("cst", 16), ("m16", 32), ("c1p", 16), ("colc", 8), ("iw8", 128), ("wf8", 128), ("slw8", 128), ("uif", 8), ("iw", 32), ("cw", 16), ("c1", 16), ("c2", 16), ("acc", 1), ("low", 16),
                  ("o16", 16), ("o8", 8), ("ins", 16), ("adf", 8), ("cd", 8), ("cd2", 16), ("a2", 16), ("slw", 32), ("wf", 32), ("j2", 32), ("t1", 32), ("opv", 32)])
-_pack("ul", U2, [("uiu", 8), ("dl", 2), ("ptu", 20), ("plist", 32), ("el", 2), ("order", 32), ("offv", 16), ("adu", 16), ("l0", 20), ("l1", 20), ("ptv", 20), ("l4", 80), ("wu", 80)])
+_pack("ul", U2, [("uiu", 8), ("dl8", 8), ("ptu", 20), ("plist", 32), ("el", 2), ("order", 32), ("offv", 16), ("adu", 16), ("ad2", 16), ("l0", 20), ("l1", 20), ("ptv", 20), ("l4", 80), ("wu", 128)])
+ALIAS["dl"] = ALIAS["dl8"][:2] + (2,)
 for _i in range(8):
     SCRATCH["p%d" % _i] = ("psum", [128, 512], F4)
-_DS = ["d_ptw", "d_x", "d_k", "d_u", "d_v", "d_w", "d_ws", "d_ad", "d_adx", "d_cp", "d_out1", "d_out2"]
-SEMAPHORES = ["qv_s", "qs_s", "qt_s", "qg_s", "arr1", "arr2", "arrx", "arrl", "rinx", "rinl", "rin2", "loc"] + _DS
+_DS = ["d_ptw", "d_x", "d_k", "d_u", "d_v", "d_w", "d_ws", "d_ad", "d_adx", "d_add", "d_out1", "d_out2"]
+SEMAPHORES = ["qv_s", "qs_s", "qt_s", "qg_s", "arr1", "arr2", "arrx", "arrl", "rinx", "rinl", "rin2", "rin3", "loc"] + _DS
 
 
 def _bits(es):
@@ -91,8 +93,15 @@ def _hand_on(g, core, T, topo):
             g.wait_ge(T.sem["rinl"], 8)
             g.remote_dma(T.llx[:, 0:8], T.rlx[:, 0:8], T.sem["arrl"], T.sem["loc"], pid, rid, m)
             sent += 8
-        piece("2", 256)
-        sent += 16
+        if j == 2:
+            piece("2", 256)
+            sent += 16
+            continue
+        for h in range(2):
+            g.wait_ge(T.sem["rin%d" % (2 + h)], 8 - 4 * h)
+            at = 128 * h + 64 * j
+            g.remote_dma(T.lc2[:, at:at + 64].bitcast(dt.uint8), T.rc2[:, 64 * h:64 * h + 64].bitcast(dt.uint8), T.sem["arr2"], T.sem["loc"], pid, rid, m)
+        sent += 24
     if sent:
         g.wait_ge(T.sem["loc"], sent)
 
@@ -246,25 +255,39 @@ def rank_program(g, core, T, topo):
         c, s = A(qn, 0, n), A(sn, 0, n)
         if not rel:
             es = topo.engines(core, nxt)
-            remote(T["lc" + tag][:, 0:n].bitcast(dt.uint8), c[0].bitcast(dt.uint8), c[1], "arr" + tag, nxt, es[0:8])
-            remote(T["ls" + tag][:, 0:n], s[0], s[1], "arr" + tag, nxt, es[8:16])
+            remote(T["lc" + tag][:, 0:n].bitcast(dt.uint8), c[0].bitcast(dt.uint8), c[1], "arr" + tag, nxt, es[0::2])
+            remote(T["ls" + tag][:, 0:n], s[0], s[1], "arr" + tag, nxt, es[0::2])
             return
-        track(G, [], [c[1]], token=("loc", 0))
-        h, tr = n // 2, []
-        for j in range(2):
-            rid, pid = topo.addr(rel[j], core)
-            es = topo.engines(core, rel[j])[8 * j:8 * j + 8]
-            tr.append(RemoteDMATransfer(dst_ids=[DstId(rid=rid, pnc=pid)], dma_engine_mask=_bits(es), remote_sem=T.sem["rin" + tag],
-                                        src=T[qn][:, h * j:h * j + h].bitcast(dt.uint8), dst=T["rc" + tag][:, 0:h].bitcast(dt.uint8)))
+        h = n // 2
+        fused([c[1]], [(rel[j], topo.engines(core, rel[j])[j::2], "rin" + tag, T[qn][:, h * j:h * j + h].bitcast(dt.uint8), T["rc" + tag][:, 0:h].bitcast(dt.uint8))
+                       for j in range(2)])
+        remote(T["rs" + tag][:, 0:n], s[0], s[1], "rin" + tag, rel[2], topo.engines(core, rel[2])[0::2])
+
+    def fused(regs, pieces):
+        track(G, [], regs, token=("loc", 0))
+        tr = []
+        for dst, es, sem, src, out in pieces:
+            rid, pid = topo.addr(dst, core)
+            tr.append(RemoteDMATransfer(dst_ids=[DstId(rid=rid, pnc=pid)], dma_engine_mask=_bits(es), remote_sem=T.sem[sem], src=src, dst=out))
             sent[0] += len(es)
         g.remote_dma_fused(tr, local_sem=T.sem["loc"])
-        remote(T["rs" + tag][:, 0:n], s[0], s[1], "rin" + tag, rel[2], topo.engines(core, rel[2])[0:8])
+
+    def send_half(h):
+        es = topo.engines(core, rel[0])
+        pieces = []
+        for k in range(2):
+            at = 128 * h + 64 * k
+            pieces.append((rel[k], es[1::2][k::2] if h else es[k::2], "rin%d" % (2 + h), T.qg[:, at:at + 64].bitcast(dt.uint8), T.rc2[:, 64 * h:64 * h + 64].bitcast(dt.uint8)))
+        if h:
+            pieces.append((rel[2], es[0::2], "rin2", T.sg3[:, 0:256], T.rs2[:, 0:256]))
+        fused([A("qg", 128 * h, 128 * h + 128)[1], A("sg3", 0, 128 * h + 128)[1]], pieces)
 
     load(S, "ptw", T.pt[:, :], "d_ptw")
     load(Y, "xs", T.x[:, :], "d_x")
-    load(S, "us", T.u[:, :], "d_u")
-    load(Y, "ks", T.k[:, :], "d_k")
+    load(S, "ks", T.k[:, :], "d_k")
+    load(Y, "us", T.u[:, :], "d_u")
     load(S, "adw", T.ad[:, :], "d_ad")
+    need(Y, "d_u", 16)
     dma(Y, T.qw[:, 0:512].bitcast(dt.uint8), T.wc[:, :], "d_w", outs=[("qw", 0, 512, None)])
     load(Y, "sw", T.ws[:, :], "d_ws")
     load(Y, "vs", T.v[:, :], "d_v")
@@ -278,66 +301,84 @@ def rank_program(g, core, T, topo):
         o, i = A("et", 528 * h, 528 * h + 512, 4, 2 + h), A("ones")
         run(G, [o], [i], lambda: g.affine_select(o[0], i[0], [[-1, 128]], ALU.is_equal, 0.0, 0, 1))
     iota(A("uif"), [[16, 8]], 0)
-    iota(A("colc"), [[256, 2]], 15)
+    iota(A("colc"), [[0, 4], [256, 2]], 15)
     iota(A("vk", 16, L), [[1, 320]], -128)
-    iota(A("m16"), [[16, 32]], 0)
-    iota(A("c1p"), [[16, 8], [0, 2]], -528)
-    iota(A("cid"), [[1, 256]], 1)
-    iota(A("sl1"), [[0, 128 + TW]], -1024)
 
-    q_, par, odd, s16 = [A("cst", j, j + 1) for j in range(4)]
-    fill(A("adx"), 0)
-    for l in range(8):
-        dma(Y, T.adx[2 * l + 1:128:16, 0:16], T.ad[l:128:8, :], "d_adx", n=128, outs=[("adx", 0, 16, None)] if l == 0 else ())
+    def const(o, c):
+        n = o[1][2] - o[1][1]
+        act(o, A("ones" if n <= 128 else "et", 0, n), scale=0.0, bias=c, func=AF.Identity)
+
+    q_, par, odd, s16, mq, hq, even = [A("cst", j, j + 1) for j in range(7)]
     for j, m in enumerate((15, 16, 1)):
         ts(A("pidx", 1 + j, 2 + j), A("pidx", 0, 1), m, ALU.bitwise_and)
-    fill(A("sm", 0, 64), 0.0)
-    cp(A("cst", 0, 3), A("pidx", 1, 4))
     fill(A("z0"), 0.0)
-    ts(A("tabi"), A("c8"), q_, ALU.is_equal)
+    cp(A("cst", 0, 3), A("pidx", 1, 4))
+    for lo, hi in PADS[:3]:
+        const(A("rows", lo, hi), 0.0)
+    const(A("vk", 0, 16), -768.0)
     ts(A("tabl"), A("c8"), q_, ALU.is_lt)
+    ts(A("tabi"), A("c8"), q_, ALU.is_equal)
     ts(A("z0", 0, 1), q_, -129.0, ALU.add)
-    ts(s16, q_, 16.0, ALU.mult)
+    act(s16, q_, scale=16.0)
+    act(mq, q_, scale=-BIG)
+    act(s16, par, scale=23.0, bias=s16, func=AF.Identity)
     ts(A("ind", 0, 16), A("j16", 0, 16), q_, ALU.is_equal)
-    ts(s16, par, 23.0, ALU.mult, s16, ALU.add)
+    ts(A("tabg"), A("tabi"), 1024.0, ALU.mult, -512.0, ALU.add)
+    ts(A("gate", 0, 16), A("ind", 0, 16), 1024.0, ALU.mult, -512.0, ALU.add)
     for h in range(2):
-        ts(A("tabm", 128 * h, 128 * h + 128), A("j16"), q_, ALU.not_equal, BIG, ALU.mult)
-    for lo, hi in PADS:
-        fill(A("rows", lo, hi), 0.0)
-    fill(A("vk", 0, 16), -768.0)
-    fill(A("sx", 0, 8), -BIG / 2)
-    fill(A("st", 0, 8), 0.0)
-    for b in range(4):
+        act(A("tabm", 128 * h, 128 * h + 128), A("j16"), scale=BIG, bias=mq, func=AF.Abs)
+    for b in (0, 2, 1, 3):
         quant("qe", "se", 128 * b, 128 * b + 128, "et", 528 * (b % 2) + 2 - 2 * (b // 2))
-    cp(A("uiu"), A("uif"))
-    ts(A("dl"), A("colc"), s16, ALU.add, 2.0 * TW - 1, ALU.min)
 
     cp(A("ptu"), A("ptw"))
+    cp(A("uiu"), A("uif"))
     act(A("junk"), A("tabl"), li=A("ptu"), accum=A("acc"))
     cp(A("ind", 16, L), A("tabi"), li=A("ptu"))
-    quant("qu", "su", 0, 128, "us", 0)
-    ts(A("gate"), A("ind"), 1024.0, ALU.mult, -512.0, ALU.add)
+    ts(A("dl8"), A("colc"), s16, ALU.add, 2.0 * TW - 1, ALU.min)
+    act(A("gate", 16, L), A("tabg"), li=A("ptu"))
     o1, i1, l1 = A("qur"), A("qu"), A("uiu")
-    act(A("sur"), A("su"), li=l1)
     scan(A("cum"), A("ind"), A("z0"), A("acc"), ALU.add, ALU.add)
-    turn("gt", "gate", 0)
-    turn("ct", "cum", 0)
-    run(V, [o1], [i1, l1], lambda: g.vector.tensor_copy(T.qur[:, 0:128].bitcast(dt.uint32), T.qu[:, 0:128].bitcast(dt.uint32).indirect(l1[0])))
-    scan(A("sel"), A("gt"), A("ct"), 0.0, ALU.max, ALU.min)
     quant("qxk", "sxk", 128, 448, "xs", 0)
-    ts(A("plist"), A("sel"), 128.0, ALU.add, li=A("dl"))
+    act(A("msk"), A("tabm", 0, 128), li=A("ptu"))
+    turn("ct", "cum", 0)
+    turn("gt", "gate", 0)
     quant("qxk", "sxk", 0, 128, "ks", 0)
+    iota(A("m16"), [[16, 32]], 0)
+    iota(A("c1p"), [[16, 8], [0, 2]], -528)
+    iota(A("a2"), [[16, 2], [32, 8]], 0)
+    for o in (A("rows", *PADS[3]), A("st", 0, 8), A("rows", *PADS[4]), A("pt2", 20, 32)):
+        if rel:
+            const(o, 0.0)
+        else:
+            iota(o, [[0, o[1][2] - o[1][1]]], 0)
+    const(A("sx", 0, 8), -BIG / 2)
+    act(A("c1"), A("c1p"), bias=q_, func=AF.Identity)
+    act(A("cw"), A("m16", 0, 16), bias=q_, func=AF.Identity)
+
+    def blanks(h):
+        if h == 0:
+            iota(A("vl", 1280, 4 * V1), [[0, 4 * V1 - 1280]], 0)
+            return
+        iota(A("sl2"), [[0, 256 + TW]], 8192)
+        iota(A("iw8"), [[257, 4], [64, 32]], 256)
+        iota(A("tabo"), [[256, 2], [1, 128], [128, 2]], 0)
+
     if rel:
         send("x", "qxk", "sxk", 448)
-    mm("p4", 320, "qur", "sur", 0, "qxk", "sxk", 128)
-    for b in range(4):
+    else:
+        iota(A("cid"), [[1, 256]], 1)
+        iota(A("sl1"), [[0, 128 + TW]], -1024)
+        blanks(0)
+        blanks(1)
+    for b in range(3):
         mm("p%d" % b, 448, "qe", "se", 128 * b, "qxk", "sxk", 0)
-    act(A("msk"), A("tabm", 0, 128), li=A("ptu"))
-    act(A("cw"), A("m16", 0, 16), bias=q_, func=AF.Identity)
-    act(A("c1"), A("c1p"), bias=q_, func=AF.Identity)
-    act(A("iw"), A("m16"), bias=q_, func=AF.Identity)
-    act(A("c2"), A("cw"), bias=-656.0, func=AF.Identity)
-    act(A("iw"), A("iw"), scale=1.0 / 512)
+    scan(A("sel"), A("gt"), A("ct"), 0.0, ALU.max, ALU.min)
+    quant("qu", "su", 0, 128, "us", 0)
+    ts(A("plist"), A("sel"), 128.0, ALU.add, li=A("dl"))
+    act(A("sur"), A("su"), li=l1)
+    run(V, [o1], [i1, l1], lambda: g.vector.tensor_copy(T.qur[:, 0:128].bitcast(dt.uint32), T.qu[:, 0:128].bitcast(dt.uint32).indirect(l1[0])))
+    mm("p4", 320, "qur", "sur", 0, "qxk", "sxk", 128)
+    mm("p3", 448, "qe", "se", 384, "qxk", "sxk", 0)
     scatter(A("vv"), A("plist", 0, 21), A("vk"))
     ts(A("el", 0, 1), A("cum", L - 1, L), 128.0, ALU.add)
     turn("vt", "vv", 0)
@@ -349,17 +390,29 @@ def rank_program(g, core, T, topo):
 
     unpack1(0)
     unpack1(1)
-    act(A("d0"), A("vv"), scale=2.0 ** 80, bias=200 * 2.0 ** 80, func=AF.Identity)
-    act(A("uu"), A("vv"), bias=-272.0, func=AF.Identity)
     unpack1(2)
+
+    def sort_scores():
+        cp(A("ss"), A("sx"), li=A("order", 0, 21))
+
+    act(A("d0"), A("vv"), scale=2.0 ** 80, bias=200 * 2.0 ** 80, func=AF.Identity)
+    sort_scores()
+    act(A("uu"), A("vv"), bias=-272.0, func=AF.Identity)
     unpack1(3)
     for b in range(4):
         act(A("gh", 128 * b, 128 * b + 128), A("p%d" % b, 0, 128), scale=0.5)
+    act(even, odd, scale=-1.0, bias=1.0, func=AF.Identity)
+    act(hq, q_, scale=1.0 / 512)
+    act(A("iw"), A("m16"), bias=q_, func=AF.Identity)
+    act(A("c2"), A("cw"), bias=-656.0, func=AF.Identity)
+    act(A("iw"), A("iw"), scale=1.0 / 512)
+    if rel:
+        act(A("cid"), A("vk", 16, 272), bias=129.0, func=AF.Identity)
+        const(A("sl1"), -1024.0)
 
     def argmax(fills):
         fills = list(fills) + [lambda: None] * 4
         fills[0]()
-        cp(A("ss"), A("sx"), li=A("order", 0, 21))
         fills[1]()
         scan(A("st", 8, L + 8), A("d0"), A("ss"), -BIG, ALU.min, ALU.max)
         fills[2]()
@@ -367,13 +420,14 @@ def rank_program(g, core, T, topo):
         fills[3]()
         scan(A("s2"), A("nr"), A("uu"), 0.0, ALU.mult, ALU.min)
 
-    argmax([lambda: ts(A("pt2", 0, 20), A("ptw"), 2.0, ALU.mult),
-            lambda: cp(A("adf"), A("adw")),
-            lambda: cp(A("l0"), A("pt2", 0, 20)),
-            lambda: ts(A("l1"), A("pt2", 0, 20), 1.0, ALU.add)])
-    tt(A("cd"), A("adf"), A("cw", 0, 8), ALU.subtract)
+    argmax([lambda: None,
+            lambda: ts(A("adx"), A("a2"), q_, ALU.add, 0.5, ALU.mult),
+            lambda: ts(A("pt2", 0, 20), A("ptw"), 2.0, ALU.mult),
+            lambda: ts(A("l1"), A("ptw"), 2.0, ALU.mult, 1.0, ALU.add)])
+    for l in range(8):
+        dma(Y, T.adx[2 * l + 1:128:16, 0:16], T.ad[l:128:8, :], "d_adx", n=128, outs=[("adx", 0, 16, None)] if l == 0 else ())
+    tt(A("cd"), A("adw"), A("cw", 0, 8), ALU.subtract)
     tt(A("o16"), A("s2"), A("c1"), ALU.max, li=A("el", 0, 1))
-    ts(A("ptq", 0, 20), A("ptw"), 1.0 / 128, ALU.mult)
     tt(A("o8"), A("o16", 0, 16, 2, 0), A("o16", 0, 16, 2, 1), ALU.max)
     ts(A("offu", 0, 8), A("o8"), 528.0, ALU.add)
     if rel:
@@ -381,14 +435,16 @@ def rank_program(g, core, T, topo):
         remote(T.rlx[:, 0:8], r[0], r[1], "rinl", rel[2], topo.engines(core, rel[2])[0:8])
 
     def a1(b):
-        tt(A("fg2", P2 * b, P2 * b + 256, 2, 0), A("fg1", P1 * b, P1 * b + P1), A("gh", 128 * b, 128 * b + 128), ALU.add, li=A("offu", 0, 8))
-        if not rel:
-            act(B4("at1", 0, 512, b), A("fg2", P2 * b, P2 * b + 256, 2, 0), scale=2.0)
+        tt(A("ah", 128 * b, 128 * b + 128), A("fg1", P1 * b, P1 * b + P1), A("gh", 128 * b, 128 * b + 128), ALU.add, li=A("offu", 0, 8))
 
     def b1(b):
         tt(A("fg2", P2 * b, P2 * b + 256, 2, 1), A("fg1", P1 * b, P1 * b + 128), A("gh", 128 * b, 128 * b + 128), ALU.add, li=A("adu", 0, 8))
-        o, i = A("gh2", 256 * b, 256 * b + 256), A("fg2", P2 * b, P2 * b + 256)
-        dma(Y, o[0], i[0], "d_cp", n=64, outs=[o[1]], ins=[i[1]])
+
+    def g_copy(o, i):
+        run(G, [o], [i], lambda: g.affine_select(o[0], i[0], [[0, o[1][2] - o[1][1]]], ALU.is_gt, 0.0, 1, 0))
+
+    def second_copy(b):
+        g_copy(A("gd", 256 * b, 256 * b + 256), A("fg2", P2 * b, P2 * b + 256))
 
     def near(n, o, cd):
         return [lambda: ts(A("ins", 0, n), o, -400.0, ALU.is_ge),
@@ -400,13 +456,14 @@ def rank_program(g, core, T, topo):
         act(A("tv", 1280 * h + 320 * b, 1280 * h + 320 * b + 320), win, li=li, scale=scale)
 
     at = [128]
+    sb = ["p5", "p6"]
 
     def add(h, b):
         tt(B4("vl", 4 * V1 * h, 4 * V1 * h + 1280, b), A("p%d" % b, at[0], at[0] + 320), A("tv", 1280 * h + 320 * b, 1280 * h + 320 * b + 320), ALU.add)
 
     def score(h):
         quant("qv", "sv3", 320 * h, 320 * h + 320, "vl", 4 * V1 * h)
-        mm("p%d" % (5 + h), 320, "qur", "sur", 0, "qv", "sv3", 320 * h)
+        mm(sb[h], 320, "qur", "sur", 0, "qv", "sv3", 320 * h)
 
     def slot_scatter(sl, offs, M):
         scatter(A(sl, 0, M + 320), offs, A("cid", 0, M))
@@ -415,8 +472,8 @@ def rank_program(g, core, T, topo):
         turn("lt", sl, M)
         ts(A("slw"), A("lt"), LL - 1.0, ALU.add, 1.0 / 512, ALU.mult, li=A("dl"))
 
-    def choose():
-        tt(A("more"), A("p6", 0, 320), A("t0s"), ALU.is_gt)
+    def choose(h):
+        tt(A("more"), A(sb[h], 0, 320), A("t0s"), ALU.is_gt if h else ALU.is_lt)
         turn("mt", "more", 0)
         tt(A("wf"), A("mt"), A("iw"), ALU.add, li=A("dl"))
 
@@ -438,67 +495,101 @@ def rank_program(g, core, T, topo):
         else:
             act(o, i, scale=0.03125)
 
-    def new_state(M, xt):
+    def new_state(M, xt, own=(0, 2)):
         for b in (1, 0, 3, 2):
             o, i, li = B4(xt, 0, 1280, b), A("vl", 0, 4 * LL + 4 * M), A("wu", 20 * b, 20 * b + 20)
-            if b % 2:
-                act(o, i, li=li)
-            else:
+            if b in own:
                 cp(o, i, li=li)
+            else:
+                act(o, i, li=li)
 
     steps = near(8, A("o8"), A("cd"))
     for b in range(4):
         steps[b]()
         a1(b)
-    for b in range(4):
-        b1(b)
-        pick(0, b, A("fg2", P2 * b, P2 * b + 256), A("l0"), 1.0)
-    if not rel:
+        pick(0, b, A("ah", 128 * b, 128 * b + 128), A("ptu"), 1.0)
+    if rel:
+        blanks(0)
+    else:
+        for b in range(4):
+            ts(B4("at1", 0, 512, b), A("ah", 128 * b, 128 * b + 128), 2.0, ALU.mult)
         quant("qa1", "sa1", 0, 128, "at1", 0)
         send("1", "qa1", "sa1", 128)
-    iota(A("vl", 1280, 4 * V1), [[0, 4 * V1 - 1280]], 0)
-    iota(A("sl2"), [[0, 256 + TW]], -1024)
-    slot_scatter("sl1", A("offu", 0, 8), 128)
     for b in range(4):
+        (act if rel else cp)(A("fg2", P2 * b, P2 * b + 256, 2, 0), A("ah", 128 * b, 128 * b + 128))
+        b1(b)
+        if not far or b < 2:
+            second_copy(b)
+    if rel:
+        blanks(1)
+    slot_scatter("sl1", A("offu", 0, 8), 128)
+
+    def pick_b(b):
         pick(1, b, A("fg2", P2 * b, P2 * b + 256), A("l1"), 1.0)
+
+    def next_means():
+        for b in range(4):
+            act(A("x2", 1024 + 256 * b, 1280 + 256 * b), A("fg2", P2 * b, P2 * b + 256), li=A("ad2"))
+        o = A("x2", 1024, 2048)
+        track(G, [o[1]], [A("gd")[1]], token=("d_add", 16))
+        g.dma_start(o[0], T.gd[:, :], accum_op=ALU.add).then_inc(T.sem["d_add"], 16)
+
+    xb = ["p4", "p7", "p6", "p5"]
+
+    def x_product(b):
+        need(E, "arrx", 24)
+        mm(xb[b], P1, "qe", "se", 128 * b, "lcx", "lsx", 0)
+
+    def x_plane(b):
+        act(A("fgx", P1 * b, P1 * b + P1), A(xb[b], 0, P1))
+        g_copy(A("ghx", 128 * b, 128 * b + 128), A("fgx", P1 * b, P1 * b + 128))
+
+    def a_before(b):
+        need(V, "arrl", 8)
+        tt(B4("atx", 0, 512, b), A("fgx", P1 * b, P1 * b + P1), A("ghx", 128 * b, 128 * b + 128), ALU.add, li=A("llx"))
+
+    pick_b(0)
+    pick_b(1)
     add(0, 0)
     add(0, 1)
-    slot_list("sl1", 128)
+    if far:
+        slot_list("sl1", 128)
     add(0, 2)
     add(0, 3)
-    score(0)
-    xb = ["p4", "p7", "p4", "p7"]
+    pick_b(2)
+    pick_b(3)
     if far:
-        need(E, "arrx", 24)
-        for b in range(2):
-            mm(xb[b], P1, "qe", "se", 128 * b, "lcx", "lsx", 0)
-    quant("qvv", "svv", 0, 128, "vs", 0)
-    ts(A("a2", 0, 16, 2, 0), A("adx", 0, 8), 2.0, ALU.mult, 1.0, ALU.add)
-    ts(A("a2", 0, 16, 2, 1), A("adx", 8, 16), 2.0, ALU.mult, 1.0, ALU.add)
-    ts(A("cd2"), A("cw"), 1.0, ALU.add, odd, ALU.mult)
-    for b in range(4):
+        sb[:] = ["p0", "p1"]
+        for b in range(4):
+            x_product(b)
+        add(1, 0)
+    score(0)
+    for h in range(2):
+        ts(A("ad2", 0, 16, 2, h), A("adx", 8 * h, 8 * h + 8), 2.0, ALU.mult, even, ALU.add)
+    for b in range(1 if far else 0, 4):
         add(1, b)
-    act(A("t0s"), A("p5", 0, 320))
-    score(1)
-    tt(A("cd2"), A("a2"), A("cd2"), ALU.subtract)
     lb = ["p0", "p1", "p2", "p3"]
     if far:
+        lb = ["p2", "p3", "p4", "p7"]
+        score(1)
         for b in range(4):
-            if b >= 2:
-                mm(xb[b], P1, "qe", "se", 128 * b, "lcx", "lsx", 0)
-            act(A("fgx", P1 * b, P1 * b + P1), A(xb[b], 0, P1))
-            act(A("ghx", 128 * b, 128 * b + 128), A(xb[b], 0, 128))
-        need(V, "arrl", 8)
+            x_plane(b)
+        second_copy(2)
+        second_copy(3)
+        act(A("t0s"), A(sb[0], 0, 320))
         for b in range(4):
-            if b == 2:
-                choose()
-            tt(B4("atx", 0, 512, b), A("fgx", P1 * b, P1 * b + P1), A("ghx", 128 * b, 128 * b + 128), ALU.add, li=A("llx"))
+            a_before(b)
         quant("qax", "sax", 0, 128, "atx", 0)
         layer("qax", "sax", 128, lb)
+        choose(1)
     else:
+        act(A("t0s"), A(sb[0], 0, 320))
+        score(1)
         need(E, "arr1", 16)
         layer("lc1", "ls1", 128, lb)
-        choose()
+        slot_list("sl1", 128)
+        choose(1)
+    next_means()
     for b in range(4):
         part_of_L(b, 128, lb, S)
     tt(A("j2"), A("mt"), A("pt2"), ALU.add, li=A("dl"))
@@ -507,72 +598,104 @@ def rank_program(g, core, T, topo):
     choose3()
     new_state(128, "xt2")
     act(A("msk"), A("tabm"), li=A("ptv"))
-    quant("qx", "sx2", 0, 320, "xt2", 0)
-    mm("p4", 320, "qur", "sur", 0, "qx", "sx2", 0)
+    act(A("x2", 0, 1024), A("gd"), scale=2.0)
+    for h in range(2):
+        quant("qx", "sx2", 160 * h, 160 * h + 160, "xt2", 640 * h)
+        mm("p%d" % (5 + h), 160, "qur", "sur", 0, "qx", "sx2", 160 * h)
     for b in range(4):
         mm("p%d" % b, 320, "qe", "se", 128 * b, "qx", "sx2", 0)
-    for b in range(4):
-        ts(A("l4", 20 * b, 20 * b + 20), A("j2", 0, 20), 4.0, ALU.mult, float(b), ALU.add)
-    tt(A("t1"), A("mt"), A("ptq"), ALU.add, li=A("dl"))
+    quant("qvv", "svv", 0, 128, "vs", 0)
+    ts(A("t1"), A("j2"), 1.0 / 256, ALU.mult)
 
     at[0] = 0
-    tt(A("sx", 8, 328), A("p4", 0, 320), A("msk"), ALU.subtract)
+    lb = ["p0", "p1", "p2", "p3"]
+    sb[:] = ["p5", "p6"]
+    for h in range(2):
+        tt(A("sx", 8 + 160 * h, 168 + 160 * h), A("p%d" % (5 + h), 0, 160), A("msk", 160 * h, 160 * h + 160), ALU.subtract)
+
+    def pick1(b):
+        pick(1, b, A("x2", 1024 + 256 * b, 1280 + 256 * b), A("ptv"), 0.5)
+
+    def z_half(h, p):
+        mm(p, 256, "qvv", "svv", 0, "qg", "sg3", 256 * h)
+
+    def z_out(h, p):
+        for k in range(2):
+            act(A("zs", 256 * h + 128 * k, 256 * h + 128 * k + 128), A(p, 0, 256, 2, k))
+        dma(Y, T.z[:, 256 * h:256 * h + 256], T.zs[:, 256 * h:256 * h + 256], "d_out1", ins=[A("zs", 256 * h, 256 * h + 256)[1]])
+
+    def list4(b):
+        ts(A("l4", 20 * b, 20 * b + 20), A("j2", 0, 20), 4.0, ALU.mult, float(b), ALU.add)
+
+    list4(0)
+    sort_scores()
     for b in range(4):
         act(A("fg2", P2 * b + 256, P2 * b + P2), A("p%d" % b, 0, 320))
-    argmax([lambda: ts(A("t1"), A("t1"), 0.5, ALU.mult)])
+    for b in range(4):
+        pick1(b)
+    act(A("iw8"), A("iw8"), scale=1.0 / 2048, bias=hq, func=AF.Identity)
+    argmax([lambda: None] + [lambda b=b: list4(b) for b in (1, 2, 3)])
     tt(A("o16"), A("s2"), A("c2"), ALU.max, li=A("el", 0, 1))
     ts(A("offv"), A("o16"), 656.0, ALU.add)
-    steps = near(16, A("o16"), A("cd2"))
+    ts(A("ins"), A("o16"), -400.0, ALU.is_ge, 1024.0, ALU.mult)
+    n = 128 if rel else 256
+    for lo in range(0, 256, n):
+        for b in range(4):
+            tt(B4("g3", 4 * lo, 4 * (lo + n), b), A("fg2", P2 * b, P2 * b + P2), A("gd", 256 * b + lo, 256 * b + lo + n), ALU.add, li=A("offv", lo // 16, (lo + n) // 16))
+        quant("qg", "sg3", lo, lo + n, "g3", 4 * lo)
+        if rel:
+            send_half(lo // 128)
+        else:
+            send("2", "qg", "sg3", 256)
+    for b in (0, 2):
+        act(A("tv", 320 * b, 320 * b + 640), A("g3", 0, 1024), li=A("l4", 20 * b, 20 * b + 40), scale=0.5)
+    z_half(0, "p7")
+    tt(A("ins"), A("ins"), A("cw"), ALU.add)
+    add(1, 0)
+    cp(A("adu"), A("ins"))
+    for b in range(1, 4):
+        add(1, b)
+    score(1)
+    slot_scatter("sl2", A("offv"), 256)
     for b in range(4):
-        steps[b]()
-        tt(B4("g3", 0, 1024, b), A("fg2", P2 * b, P2 * b + P2), A("gh2", 256 * b, 256 * b + 256), ALU.add, li=A("offv"))
-    quant("qg", "sg3", 0, 256, "g3", 0)
-    send("2", "qg", "sg3", 256)
-    for b in range(4):
-        pick(0, b, A("g3", 0, 1024), A("l4", 20 * b, 20 * b + 20), 0.5)
-    for b in range(4):
-        tt(B4("g3", 1024, 2048, b), A("fg2", P2 * b, P2 * b + 256), A("gh2", 256 * b, 256 * b + 256), ALU.add, li=A("adu"))
-    for b in range(4):
-        pick(1, b, A("g3", 1024, 2048), A("l4", 20 * b, 20 * b + 20), 0.5)
+        act(B4("g3", 1024, 2048, b), A("x2", 256 * b, 256 * b + 1280), li=A("adu"))
     for b in range(4):
         add(0, b)
+    act(A("t0s"), A("p6", 0, 320))
     score(0)
-    slot_scatter("sl2", A("offv"), 256)
-    add(1, 0)
-    add(1, 1)
-    add(1, 2)
-    add(1, 3)
-    act(A("t0s"), A("p5", 0, 320))
-    score(1)
-    slot_list("sl2", 256)
-    need(E, "arr2", 24 if far else 16)
-    layer("lc2", "ls2", 256, lb)
-    for b in range(4):
-        part_of_L(b, 256, lb, S)
-    choose()
+    z_out(0, "p7")
     quant("qg", "sg3", 256, 512, "g3", 1024)
-    mm("p7", 512, "qvv", "svv", 0, "qg", "sg3", 0)
-    choose2()
+    z_half(1, "p4")
+    turn("lt", "sl2", 256)
+    ts(A("slw8"), A("lt"), -1.0, ALU.add, 1.0 / 2048, ALU.mult, li=A("dl8"))
+    z_out(1, "p4")
+    need(E, "arr2", 40 if far else 16)
+    layer("lc2", "ls2", 256, lb)
+    tt(A("more"), A("p5", 0, 320), A("t0s"), ALU.is_lt)
+    turn("mt", "more", 0)
+    tt(A("wf8"), A("mt"), A("iw8"), ALU.add, li=A("dl8"))
     tt(A("opv"), A("mt"), A("t1"), ALU.add, li=A("dl"))
-    choose3()
-    new_state(256, "xt3")
-    quant("qx3", "sx3", 0, 320, "xt3", 0)
-    mm("p4", 320, "qvv", "svv", 0, "qx3", "sx3", 0)
+    tt(A("wf8"), A("wf8"), A("slw8"), ALU.min)
+    ts(A("ptu"), A("opv", 0, 20), 256.0, ALU.mult)
+    ts(A("wu"), A("wf8"), 2048.0, ALU.mult)
+    for b in range(4):
+        act(A("lvl", 768 - 256 * b, VB - 256 * b), A(lb[b], 0, 256), scale=0.03125)
+    for b in range(4):
+        (cp if b < 2 else act)(B4("xt3", 0, 1280, b), A("lvl", 768 - 256 * b, VB + 4 * LL), li=A("wu", 32 * b, 32 * b + 20))
+    act(A("opr"), A("tabo"), li=A("ptu"))
+    dma(S, T.op[:, :], T.opr[0:128:16, 0:320], "d_out2", ins=[A("opr")[1]])
+    for h in range(2):
+        quant("qx3", "sx3", 160 * h, 160 * h + 160, "xt3", 640 * h)
+        mm("p%d" % (5 + h), 160, "qvv", "svv", 0, "qx3", "sx3", 160 * h)
     dma(Y, T.oc[:, :], T.qx3[:, 0:320].bitcast(dt.uint8), "d_out1", ins=[A("qx3")[1]])
     for k in range(4):
         dma(Y, T.osc[4 * k:4 * k + 4, :], T.sx3[32 * k:32 * k + 4, 0:320], "d_out1", ins=[A("sx3")[1]])
-    for h in range(4):
-        act(A("zs", 128 * h, 128 * h + 128), A("p7", 256 * (h // 2), 256 * (h // 2) + 256, 2, h % 2))
-    dma(S, T.z[:, :], T.zs[:, 0:512], "d_out2", ins=[A("zs", 0, 512)[1]])
-    ts(A("opv"), A("opv"), 256.0, ALU.mult)
-    turn1(A("opt"), A("opv"))
-    cp(A("zs", 512, 832), A("p4", 0, 320))
+    for h in range(2):
+        cp(A("zs", 512 + 160 * h, 672 + 160 * h), A("p%d" % (5 + h), 0, 160))
     dma(S, T.y[:, :], T.zs[:, 512:832], "d_out2", ins=[A("zs", 512, 832)[1]])
-    for k in range(8):
-        dma(Y, T.op[k:k + 1, :], T.opt[32 * (k // 2):32 * (k // 2) + 20, 16 * (k % 2):16 * (k % 2) + 16], "d_out1", ins=[A("opt")[1]])
 
     for q in (V, S, E, G):
         need(G, qsem[q], cnt[q])
-    for s, n in (("d_ptw", 16), ("d_x", 16), ("d_k", 16), ("d_u", 16), ("d_v", 16), ("d_w", 16), ("d_ws", 16), ("d_ad", 16), ("d_adx", 128), ("d_cp", 64), ("d_out1", 208), ("d_out2", 32),
-                 ("loc", sent[0])) + ((("arrx", 24), ("arrl", 8), ("arr2", 24)) if far else (("arr1", 16), ("arr2", 16))):
+    for s, n in (("d_ptw", 16), ("d_x", 16), ("d_k", 16), ("d_u", 16), ("d_v", 16), ("d_w", 16), ("d_ws", 16), ("d_ad", 16), ("d_adx", 128), ("d_add", 16), ("d_out1", 112), ("d_out2", 32),
+                 ("loc", sent[0])) + ((("arrx", 24), ("arrl", 8), ("arr2", 40)) if far else (("arr1", 16), ("arr2", 16))):
         need(G, s, n)

@@ -2,12 +2,12 @@ from concourse.bass import DstId, RemoteDMATransfer
 from concourse.mybir import dt, AluOpType as ALU, AxisListType, ActivationFunctionType as AF
 
 F4, BF, I4, U2, C8, S8 = "float32", "bfloat16", "int32", "uint16", "float8_e4m3fn_x4", "uint8"
-P1, P2 = 448, 576
+P1, P2 = 448, 704
 L = 336
 TW = 352
 V1, LL = 512, 832
-VB = 1024
 BIG = 2.0 ** 86
+K = 1.0 / 1024
 
 
 def _sb(n, d):
@@ -19,24 +19,31 @@ SCRATCH = {
     "qxk": _sb(448, C8), "sxk": _sb(448, S8), "qu": _sb(128, C8), "su": _sb(128, S8), "qur": _sb(128, C8), "sur": _sb(128, S8),
     "qvv": _sb(128, C8), "svv": _sb(128, S8), "qw": _sb(512, C8), "sw": _sb(512, S8),
     "et": _sb(1056, BF), "ones": _sb(128, BF), "qe": _sb(512, C8), "se": _sb(512, S8),
-    "ptw": _sb(20, I4), "adw": _sb(8, I4), "adx": _sb(16, I4), "pidx": _sb(4, I4),
-    "c8": _sb(128, BF), "j16": _sb(128, BF), "tabi": _sb(128, BF), "tabl": _sb(128, BF), "tabm": _sb(256, BF),
-    "ind": _sb(L, BF), "z0": _sb(L, BF), "junk": _sb(320, BF), "rows": _sb(1424, BF), "vk": _sb(L, BF), "cid": _sb(256, BF),
+    "ints": _sb(36, I4), "z0": _sb(544, BF), "rows": _sb(1600 + L, BF), "vki": _sb(320, BF), "slb": _sb(480, BF),
     "gt": _sb(2 * TW, BF), "ct": _sb(2 * TW, BF), "sel": _sb(2 * TW, BF), "vt": _sb(2 * TW, BF), "mt": _sb(2 * TW, BF), "lt": _sb(2 * TW, BF),
-    "sl1": _sb(128 + TW, BF), "sl2": _sb(256 + TW, BF),
-    "msk": _sb(320, F4), "sx": _sb(328, F4), "ss": _sb(L, F4), "st": _sb(L + 8, F4), "nr": _sb(L, BF), "s2": _sb(L, F4), "d0": _sb(L, F4), "uu": _sb(L, F4),
-    "offu": _sb(16, U2), "opr": _sb(320, F4), "tabo": _sb(512, F4),
-    "fg1": _sb(4 * P1, BF), "fg2": _sb(4 * P2, BF), "at1": _sb(512, BF), "g3": _sb(2048, BF),
-    "lvl": _sb(VB + 4 * (LL + 128), BF), "xt2": _sb(1280, BF), "xt3": _sb(1280, BF), "fgx": _sb(4 * P1, BF), "atx": _sb(512, BF),
-    "tv": _sb(2560, BF), "gh": _sb(512, BF), "gd": _sb(1024, BF), "x2": _sb(2048, BF), "ah": _sb(512, BF), "tabg": _sb(128, BF), "ghx": _sb(512, BF),
-    "qa1": _sb(128, C8), "sa1": _sb(128, S8), "qax": _sb(128, C8), "sax": _sb(128, S8), "qg": _sb(512, C8), "sg3": _sb(512, S8), "qv": _sb(640, C8), "sv3": _sb(640, S8),
+    "qrow": _sb(256, BF), "sx": _sb(672, F4), "sst": _sb(2 * L, F4), "nr": _sb(L, BF), "s2": _sb(L, BF), "d0": _sb(L, BF),
+    "offu": _sb(16, U2), "opr": _sb(320, F4), "tabo": _sb(512, F4), "at1": _sb(512, BF), "qa1": _sb(128, C8), "sa1": _sb(128, S8), "lc1": _sb(128, C8), "ls1": _sb(128, S8),
+    "fg1": _sb(4 * P1, BF), "fg2": _sb(4 * P2, BF), "g3": _sb(3072, BF),
+    "vl": _sb(4 * (LL + 256), BF), "xt2": _sb(1280, BF), "xt3": _sb(1280, BF), "fgx": _sb(4 * P1, BF), "atx": _sb(512, BF),
+    "tv": _sb(2560, BF), "gh": _sb(512, BF), "gd": _sb(2304, BF), "ghx": _sb(512, BF),
+    "qax": _sb(128, C8), "sax": _sb(128, S8), "qg": _sb(512, C8), "sg3": _sb(512, S8), "qv": _sb(640, C8), "sv3": _sb(640, S8),
     "qx": _sb(320, C8), "sx2": _sb(320, S8), "qx3": _sb(320, C8), "sx3": _sb(320, S8),
     "t0s": _sb(320, F4), "zs": _sb(832, F4),
-    "lcx": _sb(448, C8), "lsx": _sb(448, S8), "llx": _sb(8, U2), "lc1": _sb(128, C8), "ls1": _sb(128, S8), "lc2": _sb(256, C8), "ls2": _sb(256, S8),
-    "rcx": _sb(224, C8), "rsx": _sb(448, S8), "rlx": _sb(8, U2), "rc2": _sb(128, C8), "rs2": _sb(256, S8),
+    "lcx": _sb(448, C8), "lsx": _sb(448, S8), "llx": _sb(8, U2), "lc2": _sb(256, C8), "ls2": _sb(256, S8),
+    "rck": _sb(64, C8), "rsk": _sb(128, S8), "rcx": _sb(224, C8), "rsx": _sb(448, S8), "rlx": _sb(8, U2), "rc2": _sb(128, C8), "rs2": _sb(256, S8), "rsh": _sb(128, S8), "lsh": _sb(128, S8),
 }
-ALIAS = {"vl": ("lvl", VB, 4 * (LL + 128)), "gate": ("rows", 16, L), "cum": ("rows", 368, L), "vv": ("rows", 720, L), "more": ("rows", 1072, 320)}
-PADS = [(0, 16), (352, 368), (704, 720), (1056, 1072), (1392, 1424)]
+ALIAS = {"junk": ("rows", 0, 320), "cum": ("rows", 320, 320), "ind": ("rows", 640, 320), "gate": ("rows", 960, 320), "vv": ("rows", 1280, L), "vk": ("rows", 1280 + L, 320),
+         "more": ("rows", 320, 320), "qp": ("rows", 960, 320), "sl": ("slb", 128, 320), "vkw": ("rows", 1024 + L, 576), "msk": ("sx", 32, 320), "ss": ("sst", 0, L), "st": ("sst", L, L),
+         "ptw": ("ints", 0, 20), "adw": ("ints", 20, 8), "pidx": ("ints", 28, 8),
+         "tabi": ("vl", 1280, 128), "tabl": ("vl", 1408, 128), "tabg": ("vl", 1536, 128), "j16": ("vl", 1664, 128), "c16": ("vl", 1792, 256)}
+OPT = dict(sym=0, split=1, five=1, early=1, ksplit=1, tail=3, wlate=1, ghs=2, lv=0, slotv=3, nh=0, kv=0, t0v=0, v1d=0, gv=1, lh=0, defer=1, oq="ssyy", l2v=0, ze=3, b1n=4, oo=0, ys=0,
+           sched=0, mix=0.0, step=0.1, alpha=20.0, wake=0.15, self=0.08, vfix=0.03, sfix=0.1, dk=8.0, dx=6.5, dl=3.3, d2=4.2, nk=5.0, nx=3.5, nl=1.9, n2=2.6, n1=5.0, lead=0.0)
+CYC, PICK = 0.83e-3, 1.5
+FIVE = [4, 4, 4, 2, 2]
+
+
+def _ahead():
+    return [("k", 0, 128), ("x", 128, 320)] if OPT["split"] else [("x", 0, 448)]
 
 
 def _pack(base, dtype, parts):
@@ -47,14 +54,14 @@ def _pack(base, dtype, parts):
     SCRATCH[base] = _sb(at, dtype)
 
 
-_pack("sm", F4, [("pt2", 32), ("ptq", 32), ("cst", 16), ("m16", 32), ("c1p", 16), ("colc", 8), ("iw8", 128), ("wf8", 128), ("slw8", 128), ("uif", 8), ("iw", 32), ("cw", 16), ("c1", 16), ("c2", 16), ("acc", 1), ("low", 16),
-                 ("o16", 16), ("o8", 8), ("ins", 16), ("adf", 8), ("cd", 8), ("cd2", 16), ("a2", 16), ("slw", 32), ("wf", 32), ("j2", 32), ("t1", 32), ("opv", 32)])
-_pack("ul", U2, [("uiu", 8), ("dl8", 8), ("ptu", 20), ("plist", 32), ("el", 2), ("order", 32), ("offv", 16), ("adu", 16), ("ad2", 16), ("l0", 20), ("l1", 20), ("ptv", 20), ("l4", 80), ("wu", 128)])
-ALIAS["dl"] = ALIAS["dl8"][:2] + (2,)
+_pack("sm", F4, [("pt1", 32), ("ptl", 32), ("cst", 16), ("m16", 32), ("iw", 32), ("iq", 32), ("cw", 32), ("c1", 32), ("c2", 32), ("acc", 1),
+                 ("o32", 32), ("ot", 32), ("ins", 16), ("slw", 32), ("wf", 32), ("j2", 32), ("opv", 32)])
+_pack("ul", U2, [("uiu", 16), ("dl", 2), ("ptu", 20), ("plist", 32), ("el", 2), ("order", 32), ("offv", 16), ("adu", 8), ("bl", 64), ("of4", 64), ("ptv", 20), ("l4", 80), ("wu", 80)])
+ALIAS["own"] = ("ul", ALIAS["adu"][1] + 8, 2)
 for _i in range(8):
     SCRATCH["p%d" % _i] = ("psum", [128, 512], F4)
-_DS = ["d_ptw", "d_x", "d_k", "d_u", "d_v", "d_w", "d_ws", "d_ad", "d_adx", "d_add", "d_out1", "d_out2"]
-SEMAPHORES = ["qv_s", "qs_s", "qt_s", "qg_s", "arr1", "arr2", "arrx", "arrl", "rinx", "rinl", "rin2", "rin3", "loc"] + _DS
+_DS = ["d_ptw", "d_x", "d_k", "d_u", "d_v", "d_w", "d_ws", "d_ad", "d_add", "d_ad2", "d_out1", "d_out2", "d_out3"]
+SEMAPHORES = ["qv_s", "qs_s", "qt_s", "qg_s", "arr1", "arr2", "arrh", "arrk", "arrx", "arrl", "rink", "rinx", "rinl", "rin2", "rin3", "loc", "loca"] + _DS
 
 
 def _bits(es):
@@ -80,28 +87,31 @@ def _hand_on(g, core, T, topo):
         rid, pid = topo.addr(dst, core)
         m = _bits(topo.engines(core, dst)[:8])
 
-        def piece(tag, n):
-            g.wait_ge(T.sem["rin" + tag], 8)
+        for tag, lo, n in _ahead():
+            g.wait_ge(T.sem["rin" + tag], sum(FIVE[2 * j:2 * j + 2]) if OPT["five"] else 8)
             if j < 2:
                 h = n // 2
-                o, i = T["lc" + tag][:, h * j:h * j + h].bitcast(dt.uint8), T["rc" + tag][:, 0:h].bitcast(dt.uint8)
+                o, i = T.lcx[:, lo + h * j:lo + h * j + h].bitcast(dt.uint8), T["rc" + tag][:, 0:h].bitcast(dt.uint8)
             else:
-                o, i = T["ls" + tag][:, 0:n], T["rs" + tag][:, 0:n]
+                o, i = T.lsx[:, lo:lo + n], T["rs" + tag][:, 0:n]
             g.remote_dma(o, i, T.sem["arr" + tag], T.sem["loc"], pid, rid, m)
-        piece("x", 448)
+            sent += 8
         if j == 2:
             g.wait_ge(T.sem["rinl"], 8)
             g.remote_dma(T.llx[:, 0:8], T.rlx[:, 0:8], T.sem["arrl"], T.sem["loc"], pid, rid, m)
-            sent += 8
-        if j == 2:
-            piece("2", 256)
+            if OPT["lh"]:
+                g.wait_ge(T.sem["rin3"], FIVE[4])
+                g.remote_dma(T.lsh[:, 0:128], T.rsh[:, 0:128], T.sem["arrh"], T.sem["loc"], pid, rid, m)
+                sent += 8
+            g.wait_ge(T.sem["rin2"], 8)
+            g.remote_dma(T.ls2[:, 0:256], T.rs2[:, 0:256], T.sem["arr2"], T.sem["loc"], pid, rid, m)
             sent += 16
             continue
         for h in range(2):
-            g.wait_ge(T.sem["rin%d" % (2 + h)], 8 - 4 * h)
+            g.wait_ge(T.sem["rin%d" % (2 + h)], sum(FIVE[2 * j:2 * j + 2]) if OPT["lh"] and h == 0 else 8 - 4 * h)
             at = 128 * h + 64 * j
-            g.remote_dma(T.lc2[:, at:at + 64].bitcast(dt.uint8), T.rc2[:, 64 * h:64 * h + 64].bitcast(dt.uint8), T.sem["arr2"], T.sem["loc"], pid, rid, m)
-        sent += 24
+            g.remote_dma(T.lc2[:, at:at + 64].bitcast(dt.uint8), T.rc2[:, 64 * h:64 * h + 64].bitcast(dt.uint8), T.sem["arrh" if OPT["lh"] and h == 0 else "arr2"], T.sem["loc"], pid, rid, m)
+        sent += 16
     if sent:
         g.wait_ge(T.sem["loc"], sent)
 
@@ -120,6 +130,7 @@ def rank_program(g, core, T, topo):
     cnt = {V: 0, S: 0, E: 0, G: 0}
     seen = {q: {} for q in eng}
     hist = {}
+    dcnt = {}
 
     def need(q, sem, n):
         if seen[q].get(sem, 0) < n:
@@ -149,9 +160,72 @@ def rank_program(g, core, T, topo):
             h.append((lo, hi, ph, w, token, q))
         return token
 
-    def run(q, outs, ins, f):
-        track(q, [o[1] for o in outs], [i[1] for i in ins])
-        f().then_inc(T.sem[qsem[q]], 1)
+    calls, ahead_of, marks = [], {}, {}
+
+    def put(q, outs, ins, f, busy, done=None, token=None):
+        calls.append(dict(q=q, outs=outs, ins=ins, f=f, busy=busy, done=busy if done is None else done, token=token, pre=ahead_of.pop(q, [])))
+
+    def expect(q, sem, n):
+        ahead_of.setdefault(q, []).append((sem, n))
+
+    def mark(sem, way_in, way_out):
+        marks[sem] = (len(calls) - 1, way_in, way_out)
+
+    def width(a):
+        return -(-(a[1][2] - a[1][1]) // (a[1][3][0] if a[1][3] else 1))
+
+    def short(*xs):
+        return all(SCRATCH[x[1][0]][2] in (BF, U2) for x in xs)
+
+    def run(q, outs, ins, f, rate=1.0, n=None):
+        n = width(outs[0]) if n is None else n
+        busy = {V: max(64, n * rate) * CYC + OPT["vfix"], S: OPT["sfix"] + max(64, n * rate) * CYC, E: (n + 16) * 1.25 * CYC, G: 0.15 + 2 * n * CYC}[q]
+        put(q, [o[1] for o in outs], [i[1] for i in ins], lambda: f().then_inc(T.sem[qsem[q]], 1), busy)
+
+    def issue():
+        n, seen_by = len(calls), {}
+        before, after = [{} for _ in calls], [{} for _ in calls]
+        for j, c in enumerate(calls):
+            acc = [(r, True) for r in c["outs"]] + [(r, False) for r in c["ins"]]
+            for (name, lo, hi, ph), w in acc:
+                ps = name[0] == "p" and name[1:].isdigit()
+                for (l2, h2, p2, w2, i) in seen_by.get(name, []):
+                    if (ps and calls[i]["q"] != c["q"]) or (l2 < hi and lo < h2 and not apart(ph, p2) and (w or w2)):
+                        before[j][i] = after[i][j] = calls[i]["done"] + OPT["wake" if calls[i]["q"] != c["q"] else "self"]
+            for (name, lo, hi, ph), w in acc:
+                seen_by.setdefault(name, []).append((lo, hi, ph, w, j))
+            for sem, _ in c["pre"]:
+                if sem in marks:
+                    i, way_in, way_out = marks[sem]
+                    before[j][i], after[i][j] = way_in, way_out
+        way = [0.0] * n
+        for i in reversed(range(n)):
+            way[i] = max([calls[i]["done"]] + [d + way[j] for j, d in after[i].items()])
+        if OPT["sched"] == 2:
+            way = [OPT["mix"] * way[i] - OPT["step"] * i for i in range(n)]
+        if "hook" in OPT:
+            OPT["hook"](core, calls, before, marks)
+        start, free, left, order = {}, {q: 0.0 for q in eng}, [len(b) for b in before], []
+        ready = {i: 0.0 for i in range(n) if not left[i]}
+        while ready:
+            q = min(eng, key=lambda q: min([max(free[q], t) for i, t in ready.items() if calls[i]["q"] == q] + [1e9]))
+            mine = {i: max(free[q], t) for i, t in ready.items() if calls[i]["q"] == q}
+            i = max(mine, key=lambda i: (way[i] - OPT["alpha"] * mine[i], -i))
+            start[i], free[q] = mine[i], mine[i] + calls[i]["busy"]
+            order.append(i)
+            del ready[i]
+            for j in after[i]:
+                left[j] -= 1
+                if not left[j]:
+                    ready[j] = max(start[k] + d for k, d in before[j].items())
+        if "order" in OPT:
+            order = OPT["order"][far]
+        for i in (order if OPT["sched"] else range(n)):
+            c = calls[i]
+            for sem, k in c["pre"]:
+                need(c["q"], sem, k)
+            track(c["q"], c["outs"], c["ins"], c["token"])
+            c["f"]()
 
     def A(name, lo=0, hi=None, step=1, phase=0):
         if name in ALIAS:
@@ -174,39 +248,43 @@ def rank_program(g, core, T, topo):
     def val(x):
         return x[0] if isinstance(x, tuple) else x
 
+    def rate(o, a, li):
+        return PICK if li else 0.5 if short(o, a) else 1.0
+
     def tt(o, a, b, op, li=None):
-        run(V, [o], [a, b] + opt(li), lambda: g.vector.tensor_tensor(o[0], ind(a, li), b[0], op))
+        run(V, [o], [a, b] + opt(li), lambda: g.vector.tensor_tensor(o[0], ind(a, li), b[0], op), 1.0 if SCRATCH[a[1][0]][0] == "psum" else 2.0)
 
     def ts(o, a, s1, op0, s2=None, op1=None, li=None):
         if op1 is None:
-            run(V, [o], [a] + opt(li, s1), lambda: g.vector.tensor_scalar(o[0], ind(a, li), val(s1), None, op0))
+            run(V, [o], [a] + opt(li, s1), lambda: g.vector.tensor_scalar(o[0], ind(a, li), val(s1), None, op0), rate(o, a, li))
         else:
-            run(V, [o], [a] + opt(li, s1, s2), lambda: g.vector.tensor_scalar(o[0], ind(a, li), val(s1), val(s2), op0, op1))
+            run(V, [o], [a] + opt(li, s1, s2), lambda: g.vector.tensor_scalar(o[0], ind(a, li), val(s1), val(s2), op0, op1), rate(o, a, li))
+
+    def lin(o, a, m, c, li=None):
+        ts(o, a, m, ALU.mult, c, ALU.add, li=li)
 
     def cp(o, a, li=None):
-        run(V, [o], [a] + opt(li), lambda: g.vector.tensor_copy(o[0], ind(a, li)))
+        run(V, [o], [a] + opt(li), lambda: g.vector.tensor_copy(o[0], ind(a, li)), rate(o, a, li))
 
     def scatter(o, li, a):
-        run(V, [o], [a, li], lambda: g.vector.tensor_copy(o[0].indirect(li[0]), a[0]))
+        run(V, [o], [a, li], lambda: g.vector.tensor_copy(o[0].indirect(li[0]), a[0]), 3.0, width(a))
 
     def fill(o, c):
-        run(V, [o], [], lambda: g.vector.memset(o[0], c))
+        run(V, [o], [], lambda: g.vector.memset(o[0], c), rate(o, o, None))
 
     def scan(o, a, b, init, op0, op1):
-        run(V, [o], [a, b] + opt(init), lambda: g.vector.tensor_tensor_scan(o[0], a[0], b[0], val(init), op0, op1))
+        run(V, [o], [a, b] + opt(init), lambda: g.vector.tensor_tensor_scan(o[0], a[0], b[0], val(init), op0, op1), 0.5 if short(o, a, b) else 1.0)
 
     def turn1(o, a):
-        run(V, [o], [a], lambda: g.vector.transpose(o[0], a[0]))
+        run(V, [o], [a], lambda: g.vector.transpose(o[0], a[0]), rate(o, a, None))
 
-    def turn(o, name, lo):
-        if name in ALIAS:
-            name, at, _ = ALIAS[name]
-            lo += at
+    def turn(o, name):
+        name, lo, _ = ALIAS[name]
         turn1(A(o, 0, TW), A(name, lo, lo + TW))
         turn1(A(o, TW, 2 * TW), A(name, lo - 16, lo - 16 + TW))
 
     def act(o, a, scale=1.0, bias=0.0, func=None, li=None, accum=None):
-        fn = AF.Copy if func is None else func
+        fn = (AF.Identity if isinstance(bias, tuple) or bias != 0.0 else AF.Copy) if func is None else func
 
         def f():
             kw = {}
@@ -217,7 +295,7 @@ def rank_program(g, core, T, topo):
             if accum is not None:
                 kw["accum_out"] = accum[0]
             return g.scalar.activation(o[0], ind(a, li), fn, **kw)
-        run(S, [o] + opt(accum), [a] + opt(li, bias, scale), f)
+        run(S, [o] + opt(accum), [a] + opt(li, bias, scale), f, PICK if li else 1.0)
 
     def iota(o, pattern, base, cm=0):
         def f():
@@ -226,9 +304,12 @@ def rank_program(g, core, T, topo):
             return g.iota(o[0], pattern, base, cm, allow_small_or_imprecise_dtypes=True)
         run(G, [o], [], f)
 
+    def g_copy(o, i, n):
+        run(G, [o], [i], lambda: g.affine_select(o[0], i[0], [[0, n]], ALU.is_gt, 0.0, 1, 0))
+
     def quant(q, s, lo, hi, t, tlo):
         a, b, c = A(q, lo, hi), A(s, lo, hi), A(t, tlo, tlo + 4 * (hi - lo))
-        run(V, [a, b], [c], lambda: g.vector.quantize_mx(a[0], b[0], c[0]))
+        run(V, [a, b], [c], lambda: g.vector.quantize_mx(a[0], b[0], c[0]), 1.1)
 
     def mm(p, n, wq, ws, wlo, xq, xs, xlo):
         o = A(p, 0, n)
@@ -236,45 +317,68 @@ def rank_program(g, core, T, topo):
         run(E, [o], [w, w2, x, x2], lambda: g.tensor.matmul_mx(o[0], w[0], w2[0], x[0], x2[0], True, True))
 
     def dma(q, out, in_, sem, n=16, outs=(), ins=()):
-        track(q, list(outs), list(ins), token=(sem, n))
-        eng[q].dma_start(out, in_).then_inc(T.sem[sem], 16)
+        r = (list(outs) + list(ins))[0]
+        size = (r[2] - r[1]) * (2 if SCRATCH[r[0]][2] == BF else 1 if SCRATCH[r[0]][2] == S8 else 4)
+        put(q, list(outs), list(ins), lambda: eng[q].dma_start(out, in_).then_inc(T.sem[sem], 16), 0.15, 1.4 + size / 2500.0, (sem, n))
+        dcnt[sem] = dcnt.get(sem, 0) + 16
+
+    def dma_add(o, i, sem, busy):
+        put(G, [o[1]], [i[1]], lambda: g.dma_start(o[0], i[0], accum_op=ALU.add).then_inc(T.sem[sem], 16), busy, busy + 1.4 + width(o) / 600.0, (sem, 16))
+        dcnt[sem] = 16
 
     def load(q, name, src, sem):
         a = A(name)
         dma(q, a[0], src, sem, outs=[a[1]])
 
-    sent = [0]
+    def store(q, out, a):
+        dma(q, out, a[0], "d_out1" if q == Y else "d_out2", ins=[a[1]])
+
+    sent = [0, 0]
+    gives, takes = bool(rel) or OPT["sym"], far or OPT["sym"]
+    landed = 24 if far or not OPT["five"] else 16
 
     def remote(out, src, reg, sem, dst, es):
-        track(G, [], [reg], token=("loc", 0))
         rid, pid = topo.addr(dst, core)
-        g.remote_dma(out, src, T.sem[sem], T.sem["loc"], pid, rid, _bits(es))
+        put(G, [("p9", 0, 1, None)], [reg], lambda: g.remote_dma(out, src, T.sem[sem], T.sem["loc"], pid, rid, _bits(es)), 0.6 if sum(sent) else 3.0, None, ("loc", 0))
         sent[0] += len(es)
 
     def send(tag, qn, sn, n):
         c, s = A(qn, 0, n), A(sn, 0, n)
-        if not rel:
-            es = topo.engines(core, nxt)
-            remote(T["lc" + tag][:, 0:n].bitcast(dt.uint8), c[0].bitcast(dt.uint8), c[1], "arr" + tag, nxt, es[0::2])
-            remote(T["ls" + tag][:, 0:n], s[0], s[1], "arr" + tag, nxt, es[0::2])
-            return
-        h = n // 2
-        fused([c[1]], [(rel[j], topo.engines(core, rel[j])[j::2], "rin" + tag, T[qn][:, h * j:h * j + h].bitcast(dt.uint8), T["rc" + tag][:, 0:h].bitcast(dt.uint8))
-                       for j in range(2)])
-        remote(T["rs" + tag][:, 0:n], s[0], s[1], "rin" + tag, rel[2], topo.engines(core, rel[2])[0::2])
+        es = topo.engines(core, nxt)
+        remote(T["lc" + tag][:, 0:n].bitcast(dt.uint8), c[0].bitcast(dt.uint8), c[1], "arr" + tag, nxt, es[0::2])
+        remote(T["ls" + tag][:, 0:n], s[0], s[1], "arr" + tag, nxt, es[1::2] if gives else es[0::2])
 
-    def fused(regs, pieces):
-        track(G, [], regs, token=("loc", 0))
-        tr = []
+    def ahead(tag, lo, n):
+        m = 4 if OPT["five"] else 2
+        es, w, pieces = topo.engines(core, rel[0] if rel else nxt), n // m, []
+        masks = [es[0::4], es[1::4], es[2::4], es[3::8], es[7::8]] if m == 4 else [es[0::2], es[1::2], es[0::2]]
+        for k in range(m):
+            a = w * (k % (m // 2))
+            out = T["rc" + tag][:, a:a + w] if rel else T.lcx[:, lo + w * k:lo + w * k + w]
+            pieces.append((T.qxk[:, lo + w * k:lo + w * k + w].bitcast(dt.uint8), out.bitcast(dt.uint8)))
+        pieces.append((T.sxk[:, lo:lo + n], T["rs" + tag][:, 0:n] if rel else T.lsx[:, lo:lo + n]))
+        pieces = [(rel[2 * k // m] if rel else nxt, masks[k], ("rin" if rel else "arr") + tag, i, o) for k, (i, o) in enumerate(pieces)]
+        for part in ([pieces] if m == 4 else [pieces[:2], pieces[2:]]):
+            fused([A("qxk", lo, lo + n)[1], A("sxk", lo, lo + n)[1]], part, "loca")
+
+    def fused(regs, pieces, loc="loc"):
+        tr, busy = [], 0.6 if sum(sent) else 3.0
         for dst, es, sem, src, out in pieces:
             rid, pid = topo.addr(dst, core)
             tr.append(RemoteDMATransfer(dst_ids=[DstId(rid=rid, pnc=pid)], dma_engine_mask=_bits(es), remote_sem=T.sem[sem], src=src, dst=out))
-            sent[0] += len(es)
-        g.remote_dma_fused(tr, local_sem=T.sem["loc"])
+            sent[loc == "loca"] += len(es)
+        put(G, [("p9", 0, 1, None)], regs, lambda: g.remote_dma_fused(tr, local_sem=T.sem[loc]), busy, None, ("loc", 0))
 
     def send_half(h):
         es = topo.engines(core, rel[0])
         pieces = []
+        if OPT["lh"] and h == 0:
+            masks = [es[0::4], es[1::4], es[2::4], es[3::8], es[7::8]]
+            for k in range(4):
+                pieces.append((rel[k // 2], masks[k], "rin2", T.qg[:, 32 * k:32 * k + 32].bitcast(dt.uint8), T.rc2[:, 32 * (k % 2):32 * (k % 2) + 32].bitcast(dt.uint8)))
+            pieces.append((rel[2], masks[4], "rin3", T.sg3[:, 0:128], T.rsh[:, 0:128]))
+            fused([A("qg", 0, 128)[1], A("sg3", 0, 128)[1]], pieces)
+            return
         for k in range(2):
             at = 128 * h + 64 * k
             pieces.append((rel[k], es[1::2][k::2] if h else es[k::2], "rin%d" % (2 + h), T.qg[:, at:at + 64].bitcast(dt.uint8), T.rc2[:, 64 * h:64 * h + 64].bitcast(dt.uint8)))
@@ -283,419 +387,574 @@ def rank_program(g, core, T, topo):
         fused([A("qg", 128 * h, 128 * h + 128)[1], A("sg3", 0, 128 * h + 128)[1]], pieces)
 
     load(S, "ptw", T.pt[:, :], "d_ptw")
+    load(Y, "ks", T.k[:, :], "d_k")
     load(Y, "xs", T.x[:, :], "d_x")
-    load(S, "ks", T.k[:, :], "d_k")
-    load(Y, "us", T.u[:, :], "d_u")
     load(S, "adw", T.ad[:, :], "d_ad")
-    need(Y, "d_u", 16)
-    dma(Y, T.qw[:, 0:512].bitcast(dt.uint8), T.wc[:, :], "d_w", outs=[("qw", 0, 512, None)])
-    load(Y, "sw", T.ws[:, :], "d_ws")
-    load(Y, "vs", T.v[:, :], "d_v")
+    load(Y, "us", T.u[:, :], "d_u")
 
-    fill(A("ones"), 0.5)
-    fill(A("et"), 0.0)
-    iota(A("pidx", 0, 1), [[1, 1]], 0, 17)
-    iota(A("c8"), [[1, 16], [0, 8]], 0)
-    iota(A("j16"), [[0, 8], [1, 16]], 0)
-    for h in range(2):
-        o, i = A("et", 528 * h, 528 * h + 512, 4, 2 + h), A("ones")
-        run(G, [o], [i], lambda: g.affine_select(o[0], i[0], [[-1, 128]], ALU.is_equal, 0.0, 0, 1))
-    iota(A("uif"), [[16, 8]], 0)
-    iota(A("colc"), [[0, 4], [256, 2]], 15)
-    iota(A("vk", 16, L), [[1, 320]], -128)
+    def late_loads():
+        w = ("loca", sent[1]) if gives and OPT["wlate"] else ("d_u", 16)
+        mark(w[0], 2.0, 2.0)
+        expect(Y, *w)
+        dma(Y, T.qw[:, 0:512].bitcast(dt.uint8), T.wc[:, :], "d_w", outs=[("qw", 0, 512, None)])
+        expect(Y, *w)
+        load(Y, "sw", T.ws[:, :], "d_ws")
+        if OPT["gv"] in (1, 2 + far):
+            load(G, "vs", T.v[:, :], "d_v")
+        else:
+            expect(Y, *w)
+            load(Y, "vs", T.v[:, :], "d_v")
 
     def const(o, c):
         n = o[1][2] - o[1][1]
-        act(o, A("ones" if n <= 128 else "et", 0, n), scale=0.0, bias=c, func=AF.Identity)
+        act(o, A("ones", 0, n) if n <= 128 else A("z0", 16, 16 + n), scale=0.0, bias=c, func=AF.Identity)
 
-    q_, par, odd, s16, mq, hq, even = [A("cst", j, j + 1) for j in range(7)]
-    for j, m in enumerate((15, 16, 1)):
-        ts(A("pidx", 1 + j, 2 + j), A("pidx", 0, 1), m, ALU.bitwise_and)
     fill(A("z0"), 0.0)
-    cp(A("cst", 0, 3), A("pidx", 1, 4))
-    for lo, hi in PADS[:3]:
-        const(A("rows", lo, hi), 0.0)
-    const(A("vk", 0, 16), -768.0)
-    ts(A("tabl"), A("c8"), q_, ALU.is_lt)
-    ts(A("tabi"), A("c8"), q_, ALU.is_equal)
-    ts(A("z0", 0, 1), q_, -129.0, ALU.add)
-    act(s16, q_, scale=16.0)
-    act(mq, q_, scale=-BIG)
-    act(s16, par, scale=23.0, bias=s16, func=AF.Identity)
-    ts(A("ind", 0, 16), A("j16", 0, 16), q_, ALU.is_equal)
-    ts(A("tabg"), A("tabi"), 1024.0, ALU.mult, -512.0, ALU.add)
-    ts(A("gate", 0, 16), A("ind", 0, 16), 1024.0, ALU.mult, -512.0, ALU.add)
+    fill(A("ones"), 0.5)
+    fill(A("et", 0, 528), 0.0)
+    const(A("et", 528, 1056), 0.0)
+    iota(A("pidx", 4, 5), [[1, 1]], 0, 17)
+    iota(A("j16"), [[0, 8], [1, 16]], 0)
+    iota(A("m16"), [[16, 32]], 0)
     for h in range(2):
-        act(A("tabm", 128 * h, 128 * h + 128), A("j16"), scale=BIG, bias=mq, func=AF.Abs)
-    for b in (0, 2, 1, 3):
+        o, i = A("et", 528 * h, 528 * h + 512, 4, 2 + h), A("ones")
+        run(G, [o], [i], lambda o=o, i=i: g.affine_select(o[0], i[0], [[-1, 128]], ALU.is_equal, 0.0, 0, 1))
+    iota(A("pidx", 6, 8), [[0, 2]], 0, 1)
+    iota(A("vki"), [[1, 320]], -160)
+
+    q_, par, s16, mq, bq = [A("cst", j, j + 1) for j in range(5)]
+    for j, m in enumerate((15, 16)):
+        ts(A("pidx", 2 + j, 3 + j), A("pidx", 4, 5), m, ALU.bitwise_and)
+    cp(A("cst", 0, 2), A("pidx", 2, 4))
+    ts(A("tabl"), A("j16"), q_, ALU.is_lt)
+    ts(A("tabi"), A("j16"), q_, ALU.is_equal)
+    act(A("z0", 0, 1), q_, bias=-128.0)
+    act(A("tabg"), A("tabi"), scale=1024.0, bias=-512.0)
+    const(A("vv"), -0.5)
+    cp(A("uiu"), A("m16", 0, 16))
+
+    def unit(b):
         quant("qe", "se", 128 * b, 128 * b + 128, "et", 528 * (b % 2) + 2 - 2 * (b // 2))
 
+    unit(0)
+    unit(2)
+
+    const(A("sx", 0, 32), -BIG / 2)
     cp(A("ptu"), A("ptw"))
-    cp(A("uiu"), A("uif"))
     act(A("junk"), A("tabl"), li=A("ptu"), accum=A("acc"))
-    cp(A("ind", 16, L), A("tabi"), li=A("ptu"))
-    ts(A("dl8"), A("colc"), s16, ALU.add, 2.0 * TW - 1, ALU.min)
-    act(A("gate", 16, L), A("tabg"), li=A("ptu"))
-    o1, i1, l1 = A("qur"), A("qu"), A("uiu")
-    scan(A("cum"), A("ind"), A("z0"), A("acc"), ALU.add, ALU.add)
-    quant("qxk", "sxk", 128, 448, "xs", 0)
-    act(A("msk"), A("tabm", 0, 128), li=A("ptu"))
-    turn("ct", "cum", 0)
-    turn("gt", "gate", 0)
+    cp(A("ind"), A("tabi"), li=A("ptu"))
     quant("qxk", "sxk", 0, 128, "ks", 0)
-    iota(A("m16"), [[16, 32]], 0)
-    iota(A("c1p"), [[16, 8], [0, 2]], -528)
-    iota(A("a2"), [[16, 2], [32, 8]], 0)
-    for o in (A("rows", *PADS[3]), A("st", 0, 8), A("rows", *PADS[4]), A("pt2", 20, 32)):
-        if rel:
-            const(o, 0.0)
-        else:
-            iota(o, [[0, o[1][2] - o[1][1]]], 0)
-    const(A("sx", 0, 8), -BIG / 2)
-    act(A("c1"), A("c1p"), bias=q_, func=AF.Identity)
-    act(A("cw"), A("m16", 0, 16), bias=q_, func=AF.Identity)
 
-    def blanks(h):
-        if h == 0:
-            iota(A("vl", 1280, 4 * V1), [[0, 4 * V1 - 1280]], 0)
-            return
-        iota(A("sl2"), [[0, 256 + TW]], 8192)
-        iota(A("iw8"), [[257, 4], [64, 32]], 256)
-        iota(A("tabo"), [[256, 2], [1, 128], [128, 2]], 0)
+    def ways(t):
+        a, b = OPT["d" + t], OPT["n" + t]
+        return (a - OPT["lead"], b - OPT["lead"]) if far else (b + OPT["lead"], a + OPT["lead"])
 
-    if rel:
-        send("x", "qxk", "sxk", 448)
-    else:
-        iota(A("cid"), [[1, 256]], 1)
-        iota(A("sl1"), [[0, 128 + TW]], -1024)
-        blanks(0)
-        blanks(1)
+    if gives and OPT["split"]:
+        ahead(*_ahead()[0])
+    mark("arrk", *ways("k"))
+    unit(1)
+    unit(3)
+    act(A("gate"), A("tabg"), li=A("ptu"))
+    act(s16, q_, scale=16.0, bias=15.0)
+    act(A("vk"), A("vki"), scale=K)
+    act(s16, par, scale=23.0, bias=s16)
+    act(A("c16"), A("vki"), li=A("uiu"))
+    act(mq, q_, scale=-BIG, bias=10 * BIG)
+    o1, i1, l1 = A("qur"), A("qu"), A("uiu", 0, 8)
+    scan(A("cum"), A("ind"), A("z0", 0, 320), A("acc"), ALU.add, ALU.add)
+    quant("qxk", "sxk", 128, 448, "xs", 0)
+    if gives:
+        ahead(*_ahead()[-1])
+    mark("arrx", *(ways("x") if gives else (8.5, 0.0)))
+    late_loads()
+    turn("ct", "cum")
+    turn("gt", "gate")
+    ts(A("dl"), A("m16", 0, 32, 16), s16, ALU.add, 2.0 * TW - 1, ALU.min)
+
+    def others(M, li):
+        act(A("msk"), A("c16", 0, M), scale=BIG / 16, bias=mq, func=AF.Abs, li=li)
+
+    others(128, A("ptu"))
     for b in range(3):
         mm("p%d" % b, 448, "qe", "se", 128 * b, "qxk", "sxk", 0)
     scan(A("sel"), A("gt"), A("ct"), 0.0, ALU.max, ALU.min)
     quant("qu", "su", 0, 128, "us", 0)
     ts(A("plist"), A("sel"), 128.0, ALU.add, li=A("dl"))
+    ts(A("pidx", 0, 2), A("pidx", 6, 8), 31, ALU.bitwise_and)
     act(A("sur"), A("su"), li=l1)
-    run(V, [o1], [i1, l1], lambda: g.vector.tensor_copy(T.qur[:, 0:128].bitcast(dt.uint32), T.qu[:, 0:128].bitcast(dt.uint32).indirect(l1[0])))
+    run(V, [o1], [i1, l1], lambda: g.vector.tensor_copy(T.qur[:, 0:128].bitcast(dt.uint32), T.qu[:, 0:128].bitcast(dt.uint32).indirect(l1[0])), PICK)
     mm("p4", 320, "qur", "sur", 0, "qxk", "sxk", 128)
     mm("p3", 448, "qe", "se", 384, "qxk", "sxk", 0)
-    scatter(A("vv"), A("plist", 0, 21), A("vk"))
-    ts(A("el", 0, 1), A("cum", L - 1, L), 128.0, ALU.add)
-    turn("vt", "vv", 0)
-    tt(A("sx", 8, 328), A("p4", 0, 320), A("msk"), ALU.subtract)
-    ts(A("order"), A("vt"), 136.0, ALU.add, 0.0, ALU.max, li=A("dl"))
+    scatter(A("vv"), A("plist", 0, 20), A("vk"))
+    cp(A("adu", 0, 10), A("ints", 20, 30))
+    turn("vt", "vv")
+    ts(A("el"), A("z0", 2, 4), A("cum", 319, 320), ALU.add, 128.0, ALU.add)
 
     def unpack1(b):
         act(A("fg1", P1 * b, P1 * b + P1), A("p%d" % b, 0, P1), scale=0.5)
+        if OPT["ghs"] in (1, 2 + far):
+            act(A("gh", 128 * b, 128 * b + 128), A("p%d" % b, 0, 128), scale=0.5)
+        else:
+            g_copy(A("gh", 128 * b, 128 * b + 128), A("fg1", P1 * b, P1 * b + 128), 128)
 
-    unpack1(0)
-    unpack1(1)
-    unpack1(2)
+    def mean1(b):
+        tt(A("fg2", P2 * b, P2 * b + 128), A("fg1", P1 * b, P1 * b + 128), A("gh", 128 * b, 128 * b + 128), ALU.add, li=A("adu"))
 
-    def sort_scores():
-        cp(A("ss"), A("sx"), li=A("order", 0, 21))
-
-    act(A("d0"), A("vv"), scale=2.0 ** 80, bias=200 * 2.0 ** 80, func=AF.Identity)
-    sort_scores()
-    act(A("uu"), A("vv"), bias=-272.0, func=AF.Identity)
-    unpack1(3)
-    for b in range(4):
-        act(A("gh", 128 * b, 128 * b + 128), A("p%d" % b, 0, 128), scale=0.5)
-    act(even, odd, scale=-1.0, bias=1.0, func=AF.Identity)
-    act(hq, q_, scale=1.0 / 512)
-    act(A("iw"), A("m16"), bias=q_, func=AF.Identity)
-    act(A("c2"), A("cw"), bias=-656.0, func=AF.Identity)
-    act(A("iw"), A("iw"), scale=1.0 / 512)
-    if rel:
-        act(A("cid"), A("vk", 16, 272), bias=129.0, func=AF.Identity)
-        const(A("sl1"), -1024.0)
-
-    def argmax(fills):
-        fills = list(fills) + [lambda: None] * 4
-        fills[0]()
-        fills[1]()
-        scan(A("st", 8, L + 8), A("d0"), A("ss"), -BIG, ALU.min, ALU.max)
-        fills[2]()
-        tt(A("nr"), A("st", 8, L + 8), A("st", 7, L + 7), ALU.is_equal)
-        fills[3]()
-        scan(A("s2"), A("nr"), A("uu"), 0.0, ALU.mult, ALU.min)
-
-    argmax([lambda: None,
-            lambda: ts(A("adx"), A("a2"), q_, ALU.add, 0.5, ALU.mult),
-            lambda: ts(A("pt2", 0, 20), A("ptw"), 2.0, ALU.mult),
-            lambda: ts(A("l1"), A("ptw"), 2.0, ALU.mult, 1.0, ALU.add)])
-    for l in range(8):
-        dma(Y, T.adx[2 * l + 1:128:16, 0:16], T.ad[l:128:8, :], "d_adx", n=128, outs=[("adx", 0, 16, None)] if l == 0 else ())
-    tt(A("cd"), A("adw"), A("cw", 0, 8), ALU.subtract)
-    tt(A("o16"), A("s2"), A("c1"), ALU.max, li=A("el", 0, 1))
-    tt(A("o8"), A("o16", 0, 16, 2, 0), A("o16", 0, 16, 2, 1), ALU.max)
-    ts(A("offu", 0, 8), A("o8"), 528.0, ALU.add)
-    if rel:
-        r = A("offu", 0, 8)
-        remote(T.rlx[:, 0:8], r[0], r[1], "rinl", rel[2], topo.engines(core, rel[2])[0:8])
-
-    def a1(b):
-        tt(A("ah", 128 * b, 128 * b + 128), A("fg1", P1 * b, P1 * b + P1), A("gh", 128 * b, 128 * b + 128), ALU.add, li=A("offu", 0, 8))
-
-    def b1(b):
-        tt(A("fg2", P2 * b, P2 * b + 256, 2, 1), A("fg1", P1 * b, P1 * b + 128), A("gh", 128 * b, 128 * b + 128), ALU.add, li=A("adu", 0, 8))
-
-    def g_copy(o, i):
-        run(G, [o], [i], lambda: g.affine_select(o[0], i[0], [[0, o[1][2] - o[1][1]]], ALU.is_gt, 0.0, 1, 0))
-
-    def second_copy(b):
-        g_copy(A("gd", 256 * b, 256 * b + 256), A("fg2", P2 * b, P2 * b + 256))
-
-    def near(n, o, cd):
-        return [lambda: ts(A("ins", 0, n), o, -400.0, ALU.is_ge),
-                lambda: tt(A("ins", 0, n), A("ins", 0, n), cd, ALU.mult),
-                lambda: tt(A("ins", 0, n), A("ins", 0, n), A("cw", 0, n), ALU.add),
-                lambda: cp(A("adu", 0, n), A("ins", 0, n))]
-
-    def pick(h, b, win, li, scale):
-        act(A("tv", 1280 * h + 320 * b, 1280 * h + 320 * b + 320), win, li=li, scale=scale)
+    def pick(h, b, win, li, scale=1.0, n=1):
+        act(A("tv", 1280 * h + 320 * b, 1280 * h + 320 * (b + n)), win, li=li, scale=scale)
 
     at = [128]
-    sb = ["p5", "p6"]
 
     def add(h, b):
         tt(B4("vl", 4 * V1 * h, 4 * V1 * h + 1280, b), A("p%d" % b, at[0], at[0] + 320), A("tv", 1280 * h + 320 * b, 1280 * h + 320 * b + 320), ALU.add)
 
-    def score(h):
+    def score(h, bank):
         quant("qv", "sv3", 320 * h, 320 * h + 320, "vl", 4 * V1 * h)
-        mm(sb[h], 320, "qur", "sur", 0, "qv", "sv3", 320 * h)
+        mm(bank, 320, "qur", "sur", 0, "qv", "sv3", 320 * h)
 
-    def slot_scatter(sl, offs, M):
-        scatter(A(sl, 0, M + 320), offs, A("cid", 0, M))
+    def masked(bank, lo, n):
+        tt(A("sx", 352 + lo, 352 + lo + n), A(bank, 0, n), A("msk", lo, lo + n), ALU.subtract)
 
-    def slot_list(sl, M):
-        turn("lt", sl, M)
-        ts(A("slw"), A("lt"), LL - 1.0, ALU.add, 1.0 / 512, ALU.mult, li=A("dl"))
+    def argmax(fills, cells):
+        fills = list(fills) + [lambda: None] * 7
+        cp(A("ss"), A("sx"), li=A("order", 0, 21))
+        fills[0]()
+        scan(A("st"), A("d0"), A("ss"), -BIG, ALU.min, ALU.max)
+        fills[1]()
+        tt(A("nr"), A("st"), A("st", -1, L - 1), ALU.not_equal)
+        fills[2]()
+        scan(A("s2"), A("nr"), A("vv"), 0.0, ALU.add, ALU.min)
+        fills[3]()
+        tt(A("o32"), A("s2"), cells, ALU.max, li=A("el"))
+        fills[4]()
+        turn1(A("ot"), A("o32"))
+        fills[5]()
 
-    def choose(h):
-        tt(A("more"), A(sb[h], 0, 320), A("t0s"), ALU.is_gt if h else ALU.is_lt)
-        turn("mt", "more", 0)
+    unpack1(0)
+    unpack1(1)
+    lin(A("order"), A("vt"), 1024.0, 512.0, li=A("dl"))
+    act(A("d0"), A("vv"), scale=2.0 ** 95, bias=0.25 * 2.0 ** 95)
+    masked("p4", 0, 320)
+    unpack1(2)
+    unpack1(3)
+    act(bq, q_, scale=16 * K, bias=-288 * K)
+    act(A("cw"), A("m16"), bias=q_)
+    act(A("c1"), A("j16", 0, 32), scale=K, bias=bq)
+    if OPT["slotv"] in (1, 2 + far):
+        iota(A("slb"), [[0, 480]], 0)
+    else:
+        iota(A("tabo"), [[1, 512]], 0)
+
+    def mean_pick(b):
+        mean1(b)
+        pick(1, b, A("fg2", P2 * b, P2 * b + 128), A("ptu"))
+
+    def pt1():
+        ts(A("pt1"), A("ints", 0, 32), 1.0 / 128, ALU.mult)
+
+    early = OPT["early"] in (1, 2 + far)
+    slotv = OPT["slotv"] in (1, 2 + far)
+    if early:
+        mean_pick(0)
+        argmax([lambda: mean_pick(1), lambda: mean_pick(2), lambda: mean_pick(3), lambda: None, lambda: None, pt1], A("c1"))
+    else:
+        argmax([pt1], A("c1"))
+    if not slotv:
+        act(A("iq"), A("cw"), scale=K, bias=-160 * K)
+        act(A("iw"), A("cw"), scale=1.0 / 512)
+    act(A("ptl"), A("pt1"), scale=0.25 * (1 + slotv), bias=LL / 512.0 * (1 + slotv))
+    lin(A("offu"), A("ot"), 1024.0, 288.0, li=A("own", 0, 1))
+    r = A("offu", 0, 8)
+    if rel:
+        remote(T.rlx[:, 0:8], r[0], r[1], "rinl", rel[2], topo.engines(core, rel[2])[0:8])
+    elif gives:
+        remote(T.llx[:, 0:8], r[0], r[1], "arrl", nxt, topo.engines(core, nxt)[0:8])
+    mark("arrl", *ways("l"))
+    mark("arr1", OPT["n1"] + 1.7, OPT["dl"] + 2.0)
+
+    def a1(b):
+        tt(A("fg2", P2 * b + 128, P2 * b + 256), A("fg1", P1 * b, P1 * b + P1), A("gh", 128 * b, 128 * b + 128), ALU.add, li=A("offu", 0, 8))
+
+    def b1(b):
+        act(B4("gd", 512, 1024, b), A("fg2", P2 * b, P2 * b + 256), li=A("bl", 0, 8))
+
+    def second_a(b):
+        g_copy(B4("gd", 0, 512, b), A("fg2", P2 * b + 128, P2 * b + 256), 128)
+
+    def b_list(offs, n):
+        return [lambda: ts(A("ins", 0, n), offs, 16.0 * n, ALU.is_lt, 16.0 * n, ALU.mult),
+                lambda: tt(A("ins", 0, n), A("ins", 0, n), A("cw", 0, n), ALU.add)]
+
+    def inserter_rows(offs, M, li):
+        act(A("qrow", 0, M), A("vkw", 256 - M, 576), li=offs)
+        act(A("qp"), A("qrow", 0, M), li=li)
+
+    def choose(bank, cell, cells, M, own=True, gt=False):
+        if own == 1:
+            turn("lt", "qp")
+        if own:
+            tt(A("slw"), A("lt"), A("iq"), ALU.is_equal, li=A("dl"))
+        tt(A("more"), A(bank, 0, 320), A("t0s"), ALU.is_gt if gt else ALU.is_lt)
+        turn("mt", "more")
+        if own:
+            tt(A("slw"), A("slw"), A("ptl"), ALU.mult)
         tt(A("wf"), A("mt"), A("iw"), ALU.add, li=A("dl"))
-
-    def choose2():
+        tt(A(cell), A("mt"), A("pt1"), ALU.add, li=A("dl"))
         tt(A("wf"), A("wf"), A("slw"), ALU.max)
-
-    def choose3():
+        ts(A(cells), A(cell, 0, 20), float(M), ALU.mult)
         for b in (1, 0, 3, 2):
-            ts(A("wu", 20 * b, 20 * b + 20), A("wf", 0, 20), 2048.0, ALU.mult, float(b), ALU.add)
+            lin(A("wu", 20 * b, 20 * b + 20), A("wf", 0, 20), 2048.0, float(b))
 
     def layer(qn, sn, M, banks):
         for b in range(4):
             mm(banks[b], M, "qw", "sw", 128 * b, qn, sn, 0)
 
-    def part_of_L(b, M, banks, q):
+    def part_of_L(b, M, banks, q=S):
         o, i = B4("vl", 4 * LL, 4 * LL + 4 * M, b), A(banks[b], 0, M)
         if q == V:
             ts(o, i, 0.03125, ALU.mult)
         else:
             act(o, i, scale=0.03125)
 
-    def new_state(M, xt, own=(0, 2)):
-        for b in (1, 0, 3, 2):
-            o, i, li = B4(xt, 0, 1280, b), A("vl", 0, 4 * LL + 4 * M), A("wu", 20 * b, 20 * b + 20)
-            if b in own:
-                cp(o, i, li=li)
-            else:
-                act(o, i, li=li)
+    def new_state(M, xt, b, lo=0, hi=20):
+        o, i, li = B4(xt, 64 * lo, 64 * hi, b), A("vl", 0, 4 * LL + 4 * M), A("wu", 20 * b + lo, 20 * b + hi)
+        (act if b % 2 else cp)(o, i, li=li)
 
-    steps = near(8, A("o8"), A("cd"))
-    for b in range(4):
-        steps[b]()
-        a1(b)
-        pick(0, b, A("ah", 128 * b, 128 * b + 128), A("ptu"), 1.0)
-    if rel:
-        blanks(0)
-    else:
+    def near_halves():
         for b in range(4):
-            ts(B4("at1", 0, 512, b), A("ah", 128 * b, 128 * b + 128), 2.0, ALU.mult)
-        quant("qa1", "sa1", 0, 128, "at1", 0)
-        send("1", "qa1", "sa1", 128)
-    for b in range(4):
-        (act if rel else cp)(A("fg2", P2 * b, P2 * b + 256, 2, 0), A("ah", 128 * b, 128 * b + 128))
-        b1(b)
-        if not far or b < 2:
-            second_copy(b)
-    if rel:
-        blanks(1)
-    slot_scatter("sl1", A("offu", 0, 8), 128)
+            act(B4("g3", 512, 1024, b), A("fg2", P2 * b + 128, P2 * b + 256), li=A("adu"))
 
-    def pick_b(b):
-        pick(1, b, A("fg2", P2 * b, P2 * b + 256), A("l1"), 1.0)
+    def next_means(n):
+        dma_add(A("g3", 0, n), A("gd", 0, n), "d_add", 2.5)
 
-    def next_means():
-        for b in range(4):
-            act(A("x2", 1024 + 256 * b, 1280 + 256 * b), A("fg2", P2 * b, P2 * b + 256), li=A("ad2"))
-        o = A("x2", 1024, 2048)
-        track(G, [o[1]], [A("gd")[1]], token=("d_add", 16))
-        g.dma_start(o[0], T.gd[:, :], accum_op=ALU.add).then_inc(T.sem["d_add"], 16)
+    def near_mean(b):
+        tt(B4("g3", 512, 1024, b), A("fg2", P2 * b + 128, P2 * b + 256), B4("gd", 512, 1024, b), ALU.add, li=A("adu"))
 
-    xb = ["p4", "p7", "p6", "p5"]
+    xb = ["p4", "p5", "p6", "p7"]
 
-    def x_product(b):
-        need(E, "arrx", 24)
-        mm(xb[b], P1, "qe", "se", 128 * b, "lcx", "lsx", 0)
-
-    def x_plane(b):
-        act(A("fgx", P1 * b, P1 * b + P1), A(xb[b], 0, P1))
-        g_copy(A("ghx", 128 * b, 128 * b + 128), A("fgx", P1 * b, P1 * b + 128))
+    def x_plane(b, lo, hi):
+        if lo == 0 and OPT["split"]:
+            expect(E, "arrk", landed)
+        if hi == P1:
+            expect(E, "arrx", landed)
+        mm(xb[b], hi - lo, "qe", "se", 128 * b, "lcx", "lsx", lo)
+        (cp if hi == 128 and OPT["kv"] else act)(A("fgx", P1 * b + lo, P1 * b + hi), A(xb[b], 0, hi - lo))
+        if lo == 0:
+            g_copy(A("ghx", 128 * b, 128 * b + 128), A("fgx", P1 * b, P1 * b + 128), 128)
 
     def a_before(b):
-        need(V, "arrl", 8)
+        expect(V, "arrl", 8)
         tt(B4("atx", 0, 512, b), A("fgx", P1 * b, P1 * b + P1), A("ghx", 128 * b, 128 * b + 128), ALU.add, li=A("llx"))
 
-    pick_b(0)
-    pick_b(1)
-    add(0, 0)
-    add(0, 1)
-    if far:
-        slot_list("sl1", 128)
-    add(0, 2)
-    add(0, 3)
-    pick_b(2)
-    pick_b(3)
-    if far:
-        sb[:] = ["p0", "p1"]
+    steps = b_list(A("offu", 0, 8), 8) + [lambda: cp(A("bl", 0, 8), A("ins", 0, 8)), lambda: None]
+    for b in range(4):
+        a1(b)
+        if gives:
+            steps[b]()
+        elif b:
+            ts(B4("at1", 0, 512, b - 1), A("fg2", P2 * b - P2 + 128, P2 * b - P2 + 256), 2.0, ALU.mult)
+        pick(0, b, A("fg2", P2 * b + 128, P2 * b + 256), A("ptu"))
+        if gives or b < 3:
+            second_a(b)
+
+    def means():
+        g_copy(A("g3", 0, 512), A("gd", 512, 1024), 512)
+        near_halves()
+        if slotv:
+            act(A("iw"), A("cw"), scale=1.0 / 512)
+        next_means(1024)
         for b in range(4):
-            x_product(b)
-        add(1, 0)
-    score(0)
-    for h in range(2):
-        ts(A("ad2", 0, 16, 2, h), A("adx", 8 * h, 8 * h + 8), 2.0, ALU.mult, even, ALU.add)
-    for b in range(1 if far else 0, 4):
-        add(1, b)
-    lb = ["p0", "p1", "p2", "p3"]
-    if far:
-        lb = ["p2", "p3", "p4", "p7"]
-        score(1)
+            g_copy(A("fg2", P2 * b + 256, P2 * b + 384), B4("gd", 512, 1024, b), 128)
+
+    if not takes:
+        lb = ["p1", "p2", "p3", "p4"]
         for b in range(4):
-            x_plane(b)
-        second_copy(2)
-        second_copy(3)
-        act(A("t0s"), A(sb[0], 0, 320))
+            add(1, b)
+        score(1, "p7")
+        inserter_rows(A("offu", 0, 8), 128, A("ptu"))
+        act(A("t0s"), A("p7", 0, 320))
+        for b in range(4):
+            b1(b)
+            add(0, b)
+        score(0, "p0")
+        means()
+        for b in range(4):
+            expect(E, "arr1", 16)
+            mm(lb[b], 128, "qw", "sw", 128 * b, "lc1", "ls1", 0)
+        choose("p0", "j2", "ptv", 128)
+    else:
+        if not gives:
+            steps[0]()
+            ts(B4("at1", 0, 512, 3), A("fg2", P2 * 3 + 128, P2 * 3 + 256), 2.0, ALU.mult)
+            steps[1]()
+            quant("qa1", "sa1", 0, 128, "at1", 0)
+            steps[2]()
+            send("1", "qa1", "sa1", 128)
+        if not early:
+            for b in range(4):
+                mean_pick(b)
+        ks = OPT["ksplit"] and OPT["split"] and far
+        if ks:
+            for b in range(4):
+                x_plane(b, 0, 128)
+        first = 1 if early else 0
+        for b in range(4):
+            add(first, b)
+        if slotv:
+            scatter(A("slb", 0, 448), A("offu", 0, 8), A("ones"))
+        for b in range(OPT["b1n"]):
+            b1(b)
+        lb = ["p2", "p3", "p4", "p5"]
+        for b in range(4):
+            x_plane(b, 128 if ks else 0, P1)
+            add(1 - first, b)
+        if not gives:
+            second_a(3)
+        score(1, "p0")
+        if slotv:
+            turn("lt", "sl")
+        score(0, "p1")
+        if slotv:
+            tt(A("slw"), A("lt"), A("ptl"), ALU.mult, li=A("dl"))
+        act(A("t0s"), A("p0", 0, 320))
+        if not slotv:
+            inserter_rows(A("offu", 0, 8), 128, A("ptu"))
+        for b in range(OPT["b1n"], 4):
+            b1(b)
+        means()
         for b in range(4):
             a_before(b)
         quant("qax", "sax", 0, 128, "atx", 0)
         layer("qax", "sax", 128, lb)
-        choose(1)
-    else:
-        act(A("t0s"), A(sb[0], 0, 320))
-        score(1)
-        need(E, "arr1", 16)
-        layer("lc1", "ls1", 128, lb)
-        slot_list("sl1", 128)
-        choose(1)
-    next_means()
+        choose("p1", "j2", "ptv", 128, not slotv)
     for b in range(4):
-        part_of_L(b, 128, lb, S)
-    tt(A("j2"), A("mt"), A("pt2"), ALU.add, li=A("dl"))
-    choose2()
-    cp(A("ptv"), A("j2", 0, 20))
-    choose3()
-    new_state(128, "xt2")
-    act(A("msk"), A("tabm"), li=A("ptv"))
-    act(A("x2", 0, 1024), A("gd"), scale=2.0)
+        part_of_L(b, 128, lb, V if b < OPT["lv"] else S)
+    for b in (1, 0, 3, 2):
+        new_state(128, "xt2", b)
+    others(256, A("ptv"))
     for h in range(2):
         quant("qx", "sx2", 160 * h, 160 * h + 160, "xt2", 640 * h)
         mm("p%d" % (5 + h), 160, "qur", "sur", 0, "qx", "sx2", 160 * h)
     for b in range(4):
         mm("p%d" % b, 320, "qe", "se", 128 * b, "qx", "sx2", 0)
-    quant("qvv", "svv", 0, 128, "vs", 0)
-    ts(A("t1"), A("j2"), 1.0 / 256, ALU.mult)
+    defer = OPT["defer"] and rel
+
+    def list4(b):
+        lin(A("l4", 20 * b, 20 * b + 20), A("j2", 0, 20), 512.0, float(b))
+
+    def later():
+        quant("qvv", "svv", 0, 128, "vs", 0)
+
+    act(A("c2"), A("c1"), bias=-128 * K)
+    if slotv:
+        act(A("iq"), A("cw"), scale=K, bias=-160 * K)
+    act(A("ptl"), A("j2"), scale=0.25, bias=LL / 512.0)
+    act(A("pt1"), A("j2"), scale=0.5)
+    list4(0)
+    list4(1)
+    if not defer:
+        quant("qvv", "svv", 0, 128, "vs", 0)
+    if OPT["nh"] == 2:
+        tt(A("g3", 0, 512), A("gd", 0, 512), A("gd", 512, 1024), ALU.add)
 
     at[0] = 0
-    lb = ["p0", "p1", "p2", "p3"]
-    sb[:] = ["p5", "p6"]
     for h in range(2):
-        tt(A("sx", 8 + 160 * h, 168 + 160 * h), A("p%d" % (5 + h), 0, 160), A("msk", 160 * h, 160 * h + 160), ALU.subtract)
+        masked("p%d" % (5 + h), 160 * h, 160)
 
-    def pick1(b):
-        pick(1, b, A("x2", 1024 + 256 * b, 1280 + 256 * b), A("ptv"), 0.5)
+    def picks(h, lo, b):
+        pick(h, b, A("g3", lo, lo + 1024), A("l4", 20 * b, 20 * b + 40), 0.5, 2)
 
     def z_half(h, p):
         mm(p, 256, "qvv", "svv", 0, "qg", "sg3", 256 * h)
 
-    def z_out(h, p):
-        for k in range(2):
-            act(A("zs", 256 * h + 128 * k, 256 * h + 128 * k + 128), A(p, 0, 256, 2, k))
-        dma(Y, T.z[:, 256 * h:256 * h + 256], T.zs[:, 256 * h:256 * h + 256], "d_out1", ins=[A("zs", 256 * h, 256 * h + 256)[1]])
+    def z_out(h, p, how=act, q=Y):
+        o = A("zs", 256 * h, 256 * h + 256)
+        how(o, A(p, 0, 256))
+        store(q, T.z[:, 256 * h:256 * h + 256], o)
 
-    def list4(b):
-        ts(A("l4", 20 * b, 20 * b + 20), A("j2", 0, 20), 4.0, ALU.mult, float(b), ALU.add)
+    vd = OPT["v1d"] == 2 or OPT["v1d"] == 1 and far
+    for b in range(4):
+        act(B4("gd", 1024, 2304, b) if vd else A("fg2", P2 * b + 384, P2 * b + P2), A("p%d" % b, 0, 320))
+    argmax([lambda: list4(2), lambda: None, lambda: list4(3)], A("c2"))
+    steps = b_list(A("offv"), 16) + [lambda b=b: lin(A("bl", 16 * b, 16 * b + 16), A("ins"), 4.0, float(b)) for b in range(4)]
+    if vd:
+        lin(A("of4", 0, 16), A("ot"), 4096.0, 1664.0, li=A("own", 0, 1))
+    lin(A("offv"), A("ot"), 1024.0, 416.0, li=A("own", 0, 1))
+    if vd:
+        for b in range(4):
+            act(B4("vl", 4 * V1, 4 * V1 + 1280, b), A("g3", 0, 1024), li=A("l4", 20 * b, 20 * b + 20), scale=0.5)
 
-    list4(0)
-    sort_scores()
-    for b in range(4):
-        act(A("fg2", P2 * b + 256, P2 * b + P2), A("p%d" % b, 0, 320))
-    for b in range(4):
-        pick1(b)
-    act(A("iw8"), A("iw8"), scale=1.0 / 2048, bias=hq, func=AF.Identity)
-    argmax([lambda: None] + [lambda b=b: list4(b) for b in (1, 2, 3)])
-    tt(A("o16"), A("s2"), A("c2"), ALU.max, li=A("el", 0, 1))
-    ts(A("offv"), A("o16"), 656.0, ALU.add)
-    ts(A("ins"), A("o16"), -400.0, ALU.is_ge, 1024.0, ALU.mult)
+        def v1_sum():
+            dma_add(A("vl", 4 * V1, 4 * V1 + 1280), A("gd", 1024, 2304), "d_ad2", 0.8)
+        if not rel:
+            v1_sum()
+    else:
+        picks(1, 0, 0)
+        act(A("qrow"), A("vkw"), li=A("offv"))
+        picks(1, 0, 2)
+        act(A("qp"), A("qrow"), li=A("ptv"))
+    if vd:
+        inserter_rows(A("offv"), 256, A("ptv"))
     n = 128 if rel else 256
     for lo in range(0, 256, n):
         for b in range(4):
-            tt(B4("g3", 4 * lo, 4 * (lo + n), b), A("fg2", P2 * b, P2 * b + P2), A("gd", 256 * b + lo, 256 * b + lo + n), ALU.add, li=A("offv", lo // 16, (lo + n) // 16))
-        quant("qg", "sg3", lo, lo + n, "g3", 4 * lo)
+            o = B4("g3", 1024 + 4 * lo, 1024 + 4 * (lo + n), b)
+            if vd:
+                tt(o, A("gd"), A("fg2", P2 * b + 128 + lo, P2 * b + 128 + lo + n), ALU.add, li=A("of4", 16 * b + lo // 16, 16 * b + (lo + n) // 16))
+                if lo == 0 and b < 3:
+                    lin(A("of4", 16 * b + 16, 16 * b + 32), A("offv"), 4.0, b + 1.0)
+            else:
+                tt(o, A("fg2", P2 * b + 128, P2 * b + P2), B4("gd", 4 * lo, 4 * (lo + n), b), ALU.add, li=A("offv", lo // 16, (lo + n) // 16))
+            if lo + n == 256 and b in (1, 3) and not defer:
+                steps[b // 2]()
+        quant("qg", "sg3", lo, lo + n, "g3", 1024 + 4 * lo)
         if rel:
             send_half(lo // 128)
+            if vd and lo == 0:
+                v1_sum()
         else:
             send("2", "qg", "sg3", 256)
-    for b in (0, 2):
-        act(A("tv", 320 * b, 320 * b + 640), A("g3", 0, 1024), li=A("l4", 20 * b, 20 * b + 40), scale=0.5)
+        if not (rel and vd):
+            mark("arr2", *ways("2"))
+    if slotv:
+        iota(A("tabo"), [[1, 512]], 0)
+    if defer:
+        steps[0]()
+        later()
+        steps[1]()
+    picks(0, 1024, 0)
+    picks(0, 1024, 2)
     z_half(0, "p7")
-    tt(A("ins"), A("ins"), A("cw"), ALU.add)
-    add(1, 0)
-    cp(A("adu"), A("ins"))
-    for b in range(1, 4):
-        add(1, b)
-    score(1)
-    slot_scatter("sl2", A("offv"), 256)
     for b in range(4):
-        act(B4("g3", 1024, 2048, b), A("x2", 256 * b, 256 * b + 1280), li=A("adu"))
-    for b in range(4):
-        add(0, b)
-    act(A("t0s"), A("p6", 0, 320))
-    score(0)
+        steps[2 + b]()
     z_out(0, "p7")
-    quant("qg", "sg3", 256, 512, "g3", 1024)
-    z_half(1, "p4")
-    turn("lt", "sl2", 256)
-    ts(A("slw8"), A("lt"), -1.0, ALU.add, 1.0 / 2048, ALU.mult, li=A("dl8"))
-    z_out(1, "p4")
-    need(E, "arr2", 40 if far else 16)
-    layer("lc2", "ls2", 256, lb)
-    tt(A("more"), A("p5", 0, 320), A("t0s"), ALU.is_lt)
-    turn("mt", "more", 0)
-    tt(A("wf8"), A("mt"), A("iw8"), ALU.add, li=A("dl8"))
-    tt(A("opv"), A("mt"), A("t1"), ALU.add, li=A("dl"))
-    tt(A("wf8"), A("wf8"), A("slw8"), ALU.min)
-    ts(A("ptu"), A("opv", 0, 20), 256.0, ALU.mult)
-    ts(A("wu"), A("wf8"), 2048.0, ALU.mult)
-    for b in range(4):
-        act(A("lvl", 768 - 256 * b, VB - 256 * b), A(lb[b], 0, 256), scale=0.03125)
-    for b in range(4):
-        (cp if b < 2 else act)(B4("xt3", 0, 1280, b), A("lvl", 768 - 256 * b, VB + 4 * LL), li=A("wu", 32 * b, 32 * b + 20))
-    act(A("opr"), A("tabo"), li=A("ptu"))
-    dma(S, T.op[:, :], T.opr[0:128:16, 0:320], "d_out2", ins=[A("opr")[1]])
+
+    def b2(b):
+        act(B4("g3", 2048, 3072, b), A("g3", 0, 2048), li=A("bl", 16 * b, 16 * b + 16))
+
+    lb = ["p4", "p7", "p0", "p1"]
+
+    def l2(b):
+        expect(E, "arr2", 40 if far else 16)
+        mm(lb[b], 256, "qw", "sw", 128 * b, "lc2", "ls2", 0)
+
+    if vd:
+        turn("lt", "qp")
+        tt(A("slw"), A("lt"), A("iq"), ALU.is_equal, li=A("dl"))
+        add(0, 0)
+        tt(A("slw"), A("slw"), A("ptl"), ALU.mult)
+        add(0, 1)
+        score(1, "p6")
+        add(0, 2)
+        add(0, 3)
+        score(0, "p5")
+        b2(0)
+        act(A("t0s"), A("p6", 0, 320))
+        for b in range(1, 4):
+            b2(b)
+    else:
+        for b in range(4):
+            add(1, b)
+        score(1, "p6")
+        for b in range(4):
+            b2(b)
+            add(0, b)
+        act(A("t0s"), A("p6", 0, 320))
+        score(0, "p5")
+        turn("lt", "qp")
+    lh = OPT["lh"] and far
+    zb = "p2"
+
+    def l_half(h, banks):
+        for b in range(4):
+            expect(E, *(("arr2", 24) if h else ("arrh", 24)))
+            mm(banks[b], 128, "qw", "sw", 128 * b, "lc2", "ls2" if h else "lsh", 128 * h)
+            o, i = B4("vl", 4 * LL + 512 * h, 4 * LL + 512 * h + 512, b), A(banks[b], 0, 128)
+            if h and b % 2:
+                ts(o, i, 0.03125, ALU.mult)
+            else:
+                act(o, i, scale=0.03125)
+
+    def op_out(q):
+        act(A("opr"), A("tabo"), li=A("ptu"))
+        dma(q, T.op[:, :], T.opr[0:128:16, 0:320], "d_out1" if q == Y else "d_out2", ins=[A("opr")[1]])
+
+    ze = OPT["ze"] in (1, 2 + far)
+    if not ze and not lh:
+        for b in range(4):
+            l2(b)
+    if lh and not ze:
+        l_half(0, lb)
+    if not vd:
+        quant("qg", "sg3", 256, 512, "g3", 2048)
+        if ze:
+            z_half(1, "p2")
+            z_out(1, "p2")
+    if lh and ze:
+        l_half(0, lb)
+    choose("p5", "opv", "ptu", 256, 0 if vd else 2)
+    if vd:
+        quant("qg", "sg3", 256, 512, "g3", 2048)
+        if ze:
+            z_half(1, "p2")
+            z_out(1, "p2")
+    if ze and OPT["oo"]:
+        op_out(Y)
+    if not ze:
+        z_half(1, zb)
+    if lh:
+        l_half(1, ["p2" if ze else "p4", "p3", "p6", "p7"])
+    else:
+        for b in range(4):
+            if ze:
+                l2(b)
+            part_of_L(b, 256, lb, V if b % 2 and OPT["l2v"] in (1, 2 + far) else S)
+
+    def scales_out(q, k):
+        dma(q, T.osc[4 * k:4 * k + 4, :], T.sx3[32 * k:32 * k + 4, 0:320], {Y: "d_out1", S: "d_out2", G: "d_out3"}[q], ins=[A("sx3")[1]])
+
+    if OPT["tail"] < 5:
+        for b in (1, 0, 3, 2):
+            new_state(256, "xt3", b)
+        if not ze:
+            z_out(1, zb)
+        if not (ze and OPT["oo"]):
+            op_out(S if OPT["tail"] == 0 else Y)
     for h in range(2):
+        if OPT["tail"] == 5:
+            for b in (1, 0, 3, 2):
+                new_state(256, "xt3", b, 10 * h, 10 * h + 10)
         quant("qx3", "sx3", 160 * h, 160 * h + 160, "xt3", 640 * h)
-        mm("p%d" % (5 + h), 160, "qvv", "svv", 0, "qx3", "sx3", 160 * h)
-    dma(Y, T.oc[:, :], T.qx3[:, 0:320].bitcast(dt.uint8), "d_out1", ins=[A("qx3")[1]])
-    for k in range(4):
-        dma(Y, T.osc[4 * k:4 * k + 4, :], T.sx3[32 * k:32 * k + 4, 0:320], "d_out1", ins=[A("sx3")[1]])
-    for h in range(2):
-        cp(A("zs", 512 + 160 * h, 672 + 160 * h), A("p%d" % (5 + h), 0, 160))
-    dma(S, T.y[:, :], T.zs[:, 512:832], "d_out2", ins=[A("zs", 512, 832)[1]])
+        mm(("p5", "p3")[h], 160, "qvv", "svv", 0, "qx3", "sx3", 160 * h)
+        if OPT["tail"] == 5:
+            a = A("qx3", 160 * h, 160 * h + 160)
+            dma(Y, T.oc[:, 640 * h:640 * h + 640], a[0].bitcast(dt.uint8), "d_out1", ins=[a[1]])
+    if OPT["tail"] < 5:
+        dma(Y, T.oc[:, :], T.qx3[:, 0:320].bitcast(dt.uint8), "d_out1", ins=[A("qx3")[1]])
+        for k in range(4):
+            scales_out(OPT["oq"][k], k)
+        for h in range(2):
+            cp(A("zs", 512 + 160 * h, 672 + 160 * h), A(("p5", "p3")[h], 0, 160))
+            if OPT["ys"]:
+                store((Y, S)[h], T.y[:, 160 * h:160 * h + 160], A("zs", 512 + 160 * h, 672 + 160 * h))
+        if not OPT["ys"]:
+            store(S, T.y[:, :], A("zs", 512, 832))
+    else:
+        act(A("zs", 512, 672), A("p5", 0, 160))
+        store(S, T.y[:, 0:160], A("zs", 512, 672))
+        if not ze:
+            z_out(1, zb, act, S)
+            op_out(S)
+        for k in range(4):
+            scales_out(OPT["oq"][k], k)
+        cp(A("zs", 672, 832), A("p3", 0, 160))
+        store(Y, T.y[:, 160:320], A("zs", 672, 832))
+
+    issue()
 
     for q in (V, S, E, G):
         need(G, qsem[q], cnt[q])
-    for s, n in (("d_ptw", 16), ("d_x", 16), ("d_k", 16), ("d_u", 16), ("d_v", 16), ("d_w", 16), ("d_ws", 16), ("d_ad", 16), ("d_adx", 128), ("d_add", 16), ("d_out1", 112), ("d_out2", 32),
-                 ("loc", sent[0])) + ((("arrx", 24), ("arrl", 8), ("arr2", 40)) if far else (("arr1", 16), ("arr2", 16))):
+    ends = [("loc", sent[0]), ("loca", sent[1]), ("arr2", 24 if lh else 40 if far else 16), ("arrh", 24 if lh else 0)]
+    ends += [("arr" + t, landed) for t, _, _ in _ahead()] + [("arrl", 8)] if takes else [("arr1", 16)]
+    for s, n in list(dcnt.items()) + ends:
         need(G, s, n)

from concourse.bass import DstId, RemoteDMATransfer
from concourse.mybir import dt, AluOpType as ALU, AxisListType, ActivationFunctionType as AF

F4, BF, I4, U2, C8, S8 = "float32", "bfloat16", "int32", "uint16", "float8_e4m3fn_x4", "uint8"
P1, P2 = 448, 704
L = 336
TW = 352
V1, LL = 512, 832
BIG = 2.0 ** 86
K = 1.0 / 1024


def _sb(n, d):
    return ("sbuf", [128, n], d)


SCRATCH = {
    "xs": _sb(1280, BF), "ks": _sb(512, BF), "us": _sb(512, BF), "vs": _sb(512, BF),
    "qxk": _sb(448, C8), "sxk": _sb(448, S8), "qu": _sb(128, C8), "su": _sb(128, S8), "qur": _sb(128, C8), "sur": _sb(128, S8),
    "qvv": _sb(128, C8), "svv": _sb(128, S8), "qw": _sb(512, C8), "sw": _sb(512, S8),
    "et": _sb(1056, BF), "ones": _sb(128, BF), "qe": _sb(512, C8), "se": _sb(512, S8),
    "ints": _sb(36, I4), "z0": _sb(544, BF), "rows": _sb(1600 + L, BF), "vki": _sb(320, BF), "slb": _sb(480, BF),
    "gt": _sb(2 * TW, BF), "ct": _sb(2 * TW, BF), "sel": _sb(2 * TW, BF), "vt": _sb(2 * TW, BF), "mt": _sb(2 * TW, BF), "lt": _sb(2 * TW, BF),
    "qrow": _sb(256, BF), "sx": _sb(672, F4), "sst": _sb(2 * L, F4), "nr": _sb(L, BF), "s2": _sb(L, BF), "d0": _sb(L, BF),
    "offu": _sb(16, U2), "opr": _sb(320, F4), "tabo": _sb(512, F4), "at1": _sb(512, BF), "qa1": _sb(128, C8), "sa1": _sb(128, S8), "lc1": _sb(128, C8), "ls1": _sb(128, S8),
    "fg1": _sb(4 * P1, BF), "fg2": _sb(4 * P2, BF), "g3": _sb(3072, BF),
    "vl": _sb(4 * (LL + 256), BF), "xt2": _sb(1280, BF), "xt3": _sb(1280, BF), "fgx": _sb(4 * P1, BF), "atx": _sb(512, BF),
    "tv": _sb(2560, BF), "gh": _sb(512, BF), "gd": _sb(2304, BF), "ghx": _sb(512, BF),
    "qax": _sb(128, C8), "sax": _sb(128, S8), "qg": _sb(512, C8), "sg3": _sb(512, S8), "qv": _sb(640, C8), "sv3": _sb(640, S8),
    "qx": _sb(320, C8), "sx2": _sb(320, S8), "qx3": _sb(320, C8), "sx3": _sb(320, S8),
    "t0s": _sb(320, F4), "zs": _sb(832, F4),
    "lcx": _sb(448, C8), "lsx": _sb(448, S8), "llx": _sb(8, U2), "lc2": _sb(256, C8), "ls2": _sb(256, S8),
    "rck": _sb(64, C8), "rsk": _sb(128, S8), "rcx": _sb(224, C8), "rsx": _sb(448, S8), "rlx": _sb(8, U2), "rc2": _sb(128, C8), "rs2": _sb(256, S8), "rsh": _sb(128, S8), "lsh": _sb(128, S8),
}
ALIAS = {"junk": ("rows", 0, 320), "cum": ("rows", 320, 320), "ind": ("rows", 640, 320), "gate": ("rows", 960, 320), "vv": ("rows", 1280, L), "vk": ("rows", 1280 + L, 320),
         "more": ("rows", 320, 320), "qp": ("rows", 960, 320), "sl": ("slb", 128, 320), "vkw": ("rows", 1024 + L, 576), "msk": ("sx", 32, 320), "ss": ("sst", 0, L), "st": ("sst", L, L),
         "ptw": ("ints", 0, 20), "adw": ("ints", 20, 8), "pidx": ("ints", 28, 8),
         "tabi": ("vl", 1280, 128), "tabl": ("vl", 1408, 128), "tabg": ("vl", 1536, 128), "j16": ("vl", 1664, 128), "c16": ("vl", 1792, 256)}
OPT = dict(sym=0, split=1, five=1, early=1, ksplit=1, tail=3, wlate=1, ghs=2, lv=0, slotv=3, nh=0, kv=0, t0v=0, v1d=0, gv=1, lh=0, defer=1, oq="ssyy", l2v=0, ze=3, b1n=4, oo=0, ys=0,
           sched=0, mix=0.0, step=0.1, alpha=20.0, wake=0.15, self=0.08, vfix=0.03, sfix=0.1, dk=8.0, dx=6.5, dl=3.3, d2=4.2, nk=5.0, nx=3.5, nl=1.9, n2=2.6, n1=5.0, lead=0.0)
CYC, PICK = 0.83e-3, 1.5
FIVE = [4, 4, 4, 2, 2]


def _ahead():
    return [("k", 0, 128), ("x", 128, 320)] if OPT["split"] else [("x", 0, 448)]


def _pack(base, dtype, parts):
    at = 0
    for n, w in parts:
        ALIAS[n] = (base, at, w)
        at += -(-w // 16) * 16
    SCRATCH[base] = _sb(at, dtype)


_pack("sm", F4, [("pt1", 32), ("ptl", 32), ("cst", 16), ("m16", 32), ("iw", 32), ("iq", 32), ("cw", 32), ("c1", 32), ("c2", 32), ("acc", 1),
                 ("o32", 32), ("ot", 32), ("ins", 16), ("slw", 32), ("wf", 32), ("j2", 32), ("opv", 32)])
_pack("ul", U2, [("uiu", 16), ("dl", 2), ("ptu", 20), ("plist", 32), ("el", 2), ("order", 32), ("offv", 16), ("adu", 8), ("bl", 64), ("of4", 64), ("ptv", 20), ("l4", 80), ("wu", 80)])
ALIAS["own"] = ("ul", ALIAS["adu"][1] + 8, 2)
for _i in range(8):
    SCRATCH["p%d" % _i] = ("psum", [128, 512], F4)
_DS = ["d_ptw", "d_x", "d_k", "d_u", "d_v", "d_w", "d_ws", "d_ad", "d_add", "d_ad2", "d_out1", "d_out2", "d_out3"]
SEMAPHORES = ["qv_s", "qs_s", "qt_s", "qg_s", "arr1", "arr2", "arrh", "arrk", "arrx", "arrl", "rink", "rinx", "rinl", "rin2", "rin3", "loc", "loca"] + _DS


def _bits(es):
    return sum(1 << e for e in es)


def _relays(src, dst, T, topo):
    if topo.may_write(src, dst):
        return []
    c = [d for d in topo.cores_of(src) if d != src and T.rank_of(d) is None and topo.may_write(d, dst)]
    a, b = [d for d in c if topo.die(d) == topo.die(src)], [d for d in c if topo.die(d) != topo.die(src)]
    return [d for p in zip(a, b) for d in p][:3]


def _hand_on(g, core, T, topo):
    sent = 0
    for r, src in enumerate(T.cores):
        dst = T.cores[(r + 1) % len(T.cores)]
        rel = _relays(src, dst, T, topo)
        if core not in rel:
            continue
        j = rel.index(core)
        rid, pid = topo.addr(dst, core)
        m = _bits(topo.engines(core, dst)[:8])

        for tag, lo, n in _ahead():
            g.wait_ge(T.sem["rin" + tag], sum(FIVE[2 * j:2 * j + 2]) if OPT["five"] else 8)
            if j < 2:
                h = n // 2
                o, i = T.lcx[:, lo + h * j:lo + h * j + h].bitcast(dt.uint8), T["rc" + tag][:, 0:h].bitcast(dt.uint8)
            else:
                o, i = T.lsx[:, lo:lo + n], T["rs" + tag][:, 0:n]
            g.remote_dma(o, i, T.sem["arr" + tag], T.sem["loc"], pid, rid, m)
            sent += 8
        if j == 2:
            g.wait_ge(T.sem["rinl"], 8)
            g.remote_dma(T.llx[:, 0:8], T.rlx[:, 0:8], T.sem["arrl"], T.sem["loc"], pid, rid, m)
            if OPT["lh"]:
                g.wait_ge(T.sem["rin3"], FIVE[4])
                g.remote_dma(T.lsh[:, 0:128], T.rsh[:, 0:128], T.sem["arrh"], T.sem["loc"], pid, rid, m)
                sent += 8
            g.wait_ge(T.sem["rin2"], 8)
            g.remote_dma(T.ls2[:, 0:256], T.rs2[:, 0:256], T.sem["arr2"], T.sem["loc"], pid, rid, m)
            sent += 16
            continue
        for h in range(2):
            g.wait_ge(T.sem["rin%d" % (2 + h)], sum(FIVE[2 * j:2 * j + 2]) if OPT["lh"] and h == 0 else 8 - 4 * h)
            at = 128 * h + 64 * j
            g.remote_dma(T.lc2[:, at:at + 64].bitcast(dt.uint8), T.rc2[:, 64 * h:64 * h + 64].bitcast(dt.uint8), T.sem["arrh" if OPT["lh"] and h == 0 else "arr2"], T.sem["loc"], pid, rid, m)
        sent += 16
    if sent:
        g.wait_ge(T.sem["loc"], sent)


def rank_program(g, core, T, topo):
    rank = T.rank_of(core)
    if rank is None:
        _hand_on(g, core, T, topo)
        return
    nranks = len(T.cores)
    prev, nxt = T.cores[(rank - 1) % nranks], T.cores[(rank + 1) % nranks]
    rel, far = _relays(core, nxt, T, topo), bool(_relays(prev, core, T, topo))
    V, S, E, G, Y = "v", "s", "t", "g", "y"
    eng = {V: g.vector, S: g.scalar, E: g.tensor, G: g, Y: g.sync}
    qsem = {V: "qv_s", S: "qs_s", E: "qt_s", G: "qg_s"}
    cnt = {V: 0, S: 0, E: 0, G: 0}
    seen = {q: {} for q in eng}
    hist = {}
    dcnt = {}

    def need(q, sem, n):
        if seen[q].get(sem, 0) < n:
            eng[q].wait_ge(T.sem[sem], n)
            seen[q][sem] = n

    def apart(a, b):
        return a is not None and b is not None and a[0] == b[0] and a[1] != b[1]

    def track(q, outs, ins, token=None):
        acc = [(r, True) for r in outs] + [(r, False) for r in ins]
        waits = {}
        for (name, lo, hi, ph), w in acc:
            ps = name[0] == "p" and name[1:].isdigit()
            for (l2, h2, p2, w2, tok, q2) in hist.get(name, []):
                if (ps and q2 != q) or (l2 < hi and lo < h2 and not apart(ph, p2) and (w or w2)):
                    waits[tok[0]] = max(waits.get(tok[0], 0), tok[1])
        for s, n in waits.items():
            need(q, s, n)
        if token is None:
            cnt[q] += 1
            token = (qsem[q], cnt[q])
        for (name, lo, hi, ph), w in acc:
            h = hist.setdefault(name, [])
            if w and ph is None:
                h[:] = [e for e in h if not (lo <= e[0] and e[1] <= hi)]
            h.append((lo, hi, ph, w, token, q))
        return token

    calls, ahead_of, marks = [], {}, {}

    def put(q, outs, ins, f, busy, done=None, token=None):
        calls.append(dict(q=q, outs=outs, ins=ins, f=f, busy=busy, done=busy if done is None else done, token=token, pre=ahead_of.pop(q, [])))

    def expect(q, sem, n):
        ahead_of.setdefault(q, []).append((sem, n))

    def mark(sem, way_in, way_out):
        marks[sem] = (len(calls) - 1, way_in, way_out)

    def width(a):
        return -(-(a[1][2] - a[1][1]) // (a[1][3][0] if a[1][3] else 1))

    def short(*xs):
        return all(SCRATCH[x[1][0]][2] in (BF, U2) for x in xs)

    def run(q, outs, ins, f, rate=1.0, n=None):
        n = width(outs[0]) if n is None else n
        busy = {V: max(64, n * rate) * CYC + OPT["vfix"], S: OPT["sfix"] + max(64, n * rate) * CYC, E: (n + 16) * 1.25 * CYC, G: 0.15 + 2 * n * CYC}[q]
        put(q, [o[1] for o in outs], [i[1] for i in ins], lambda: f().then_inc(T.sem[qsem[q]], 1), busy)

    def issue():
        n, seen_by = len(calls), {}
        before, after = [{} for _ in calls], [{} for _ in calls]
        for j, c in enumerate(calls):
            acc = [(r, True) for r in c["outs"]] + [(r, False) for r in c["ins"]]
            for (name, lo, hi, ph), w in acc:
                ps = name[0] == "p" and name[1:].isdigit()
                for (l2, h2, p2, w2, i) in seen_by.get(name, []):
                    if (ps and calls[i]["q"] != c["q"]) or (l2 < hi and lo < h2 and not apart(ph, p2) and (w or w2)):
                        before[j][i] = after[i][j] = calls[i]["done"] + OPT["wake" if calls[i]["q"] != c["q"] else "self"]
            for (name, lo, hi, ph), w in acc:
                seen_by.setdefault(name, []).append((lo, hi, ph, w, j))
            for sem, _ in c["pre"]:
                if sem in marks:
                    i, way_in, way_out = marks[sem]
                    before[j][i], after[i][j] = way_in, way_out
        way = [0.0] * n
        for i in reversed(range(n)):
            way[i] = max([calls[i]["done"]] + [d + way[j] for j, d in after[i].items()])
        if OPT["sched"] == 2:
            way = [OPT["mix"] * way[i] - OPT["step"] * i for i in range(n)]
        if "hook" in OPT:
            OPT["hook"](core, calls, before, marks)
        start, free, left, order = {}, {q: 0.0 for q in eng}, [len(b) for b in before], []
        ready = {i: 0.0 for i in range(n) if not left[i]}
        while ready:
            q = min(eng, key=lambda q: min([max(free[q], t) for i, t in ready.items() if calls[i]["q"] == q] + [1e9]))
            mine = {i: max(free[q], t) for i, t in ready.items() if calls[i]["q"] == q}
            i = max(mine, key=lambda i: (way[i] - OPT["alpha"] * mine[i], -i))
            start[i], free[q] = mine[i], mine[i] + calls[i]["busy"]
            order.append(i)
            del ready[i]
            for j in after[i]:
                left[j] -= 1
                if not left[j]:
                    ready[j] = max(start[k] + d for k, d in before[j].items())
        if "order" in OPT:
            order = OPT["order"][far]
        for i in (order if OPT["sched"] else range(n)):
            c = calls[i]
            for sem, k in c["pre"]:
                need(c["q"], sem, k)
            track(c["q"], c["outs"], c["ins"], c["token"])
            c["f"]()

    def A(name, lo=0, hi=None, step=1, phase=0):
        if name in ALIAS:
            name, at, w = ALIAS[name]
            lo, hi = at + lo, at + (w if hi is None else hi)
        hi = SCRATCH[name][1][1] if hi is None else hi
        if step == 1:
            return (T[name][:, lo:hi], (name, lo, hi, None))
        return (T[name][:, lo + phase:hi:step], (name, lo, hi, (step, (lo + phase) % step)))

    def B4(name, lo, hi, b):
        return A(name, lo, hi, 4, b)

    def ind(a, li):
        return a[0] if li is None else a[0].indirect(li[0])

    def opt(*xs):
        return [x for x in xs if isinstance(x, tuple)]

    def val(x):
        return x[0] if isinstance(x, tuple) else x

    def rate(o, a, li):
        return PICK if li else 0.5 if short(o, a) else 1.0

    def tt(o, a, b, op, li=None):
        run(V, [o], [a, b] + opt(li), lambda: g.vector.tensor_tensor(o[0], ind(a, li), b[0], op), 1.0 if SCRATCH[a[1][0]][0] == "psum" else 2.0)

    def ts(o, a, s1, op0, s2=None, op1=None, li=None):
        if op1 is None:
            run(V, [o], [a] + opt(li, s1), lambda: g.vector.tensor_scalar(o[0], ind(a, li), val(s1), None, op0), rate(o, a, li))
        else:
            run(V, [o], [a] + opt(li, s1, s2), lambda: g.vector.tensor_scalar(o[0], ind(a, li), val(s1), val(s2), op0, op1), rate(o, a, li))

    def lin(o, a, m, c, li=None):
        ts(o, a, m, ALU.mult, c, ALU.add, li=li)

    def cp(o, a, li=None):
        run(V, [o], [a] + opt(li), lambda: g.vector.tensor_copy(o[0], ind(a, li)), rate(o, a, li))

    def scatter(o, li, a):
        run(V, [o], [a, li], lambda: g.vector.tensor_copy(o[0].indirect(li[0]), a[0]), 3.0, width(a))

    def fill(o, c):
        run(V, [o], [], lambda: g.vector.memset(o[0], c), rate(o, o, None))

    def scan(o, a, b, init, op0, op1):
        run(V, [o], [a, b] + opt(init), lambda: g.vector.tensor_tensor_scan(o[0], a[0], b[0], val(init), op0, op1), 0.5 if short(o, a, b) else 1.0)

    def turn1(o, a):
        run(V, [o], [a], lambda: g.vector.transpose(o[0], a[0]), rate(o, a, None))

    def turn(o, name):
        name, lo, _ = ALIAS[name]
        turn1(A(o, 0, TW), A(name, lo, lo + TW))
        turn1(A(o, TW, 2 * TW), A(name, lo - 16, lo - 16 + TW))

    def act(o, a, scale=1.0, bias=0.0, func=None, li=None, accum=None):
        fn = (AF.Identity if isinstance(bias, tuple) or bias != 0.0 else AF.Copy) if func is None else func

        def f():
            kw = {}
            if isinstance(bias, tuple) or bias != 0.0:
                kw["bias"] = val(bias)
            if isinstance(scale, tuple) or scale != 1.0:
                kw["scale"] = val(scale)
            if accum is not None:
                kw["accum_out"] = accum[0]
            return g.scalar.activation(o[0], ind(a, li), fn, **kw)
        run(S, [o] + opt(accum), [a] + opt(li, bias, scale), f, PICK if li else 1.0)

    def iota(o, pattern, base, cm=0):
        def f():
            if SCRATCH[o[1][0]][2] == I4:
                return g.iota(o[0], pattern, base, cm)
            return g.iota(o[0], pattern, base, cm, allow_small_or_imprecise_dtypes=True)
        run(G, [o], [], f)

    def g_copy(o, i, n):
        run(G, [o], [i], lambda: g.affine_select(o[0], i[0], [[0, n]], ALU.is_gt, 0.0, 1, 0))

    def quant(q, s, lo, hi, t, tlo):
        a, b, c = A(q, lo, hi), A(s, lo, hi), A(t, tlo, tlo + 4 * (hi - lo))
        run(V, [a, b], [c], lambda: g.vector.quantize_mx(a[0], b[0], c[0]), 1.1)

    def mm(p, n, wq, ws, wlo, xq, xs, xlo):
        o = A(p, 0, n)
        w, w2, x, x2 = A(wq, wlo, wlo + 128), A(ws, wlo, wlo + 128), A(xq, xlo, xlo + n), A(xs, xlo, xlo + n)
        run(E, [o], [w, w2, x, x2], lambda: g.tensor.matmul_mx(o[0], w[0], w2[0], x[0], x2[0], True, True))

    def dma(q, out, in_, sem, n=16, outs=(), ins=()):
        r = (list(outs) + list(ins))[0]
        size = (r[2] - r[1]) * (2 if SCRATCH[r[0]][2] == BF else 1 if SCRATCH[r[0]][2] == S8 else 4)
        put(q, list(outs), list(ins), lambda: eng[q].dma_start(out, in_).then_inc(T.sem[sem], 16), 0.15, 1.4 + size / 2500.0, (sem, n))
        dcnt[sem] = dcnt.get(sem, 0) + 16

    def dma_add(o, i, sem, busy):
        put(G, [o[1]], [i[1]], lambda: g.dma_start(o[0], i[0], accum_op=ALU.add).then_inc(T.sem[sem], 16), busy, busy + 1.4 + width(o) / 600.0, (sem, 16))
        dcnt[sem] = 16

    def load(q, name, src, sem):
        a = A(name)
        dma(q, a[0], src, sem, outs=[a[1]])

    def store(q, out, a):
        dma(q, out, a[0], "d_out1" if q == Y else "d_out2", ins=[a[1]])

    sent = [0, 0]
    gives, takes = bool(rel) or OPT["sym"], far or OPT["sym"]
    landed = 24 if far or not OPT["five"] else 16

    def remote(out, src, reg, sem, dst, es):
        rid, pid = topo.addr(dst, core)
        put(G, [("p9", 0, 1, None)], [reg], lambda: g.remote_dma(out, src, T.sem[sem], T.sem["loc"], pid, rid, _bits(es)), 0.6 if sum(sent) else 3.0, None, ("loc", 0))
        sent[0] += len(es)

    def send(tag, qn, sn, n):
        c, s = A(qn, 0, n), A(sn, 0, n)
        es = topo.engines(core, nxt)
        remote(T["lc" + tag][:, 0:n].bitcast(dt.uint8), c[0].bitcast(dt.uint8), c[1], "arr" + tag, nxt, es[0::2])
        remote(T["ls" + tag][:, 0:n], s[0], s[1], "arr" + tag, nxt, es[1::2] if gives else es[0::2])

    def ahead(tag, lo, n):
        m = 4 if OPT["five"] else 2
        es, w, pieces = topo.engines(core, rel[0] if rel else nxt), n // m, []
        masks = [es[0::4], es[1::4], es[2::4], es[3::8], es[7::8]] if m == 4 else [es[0::2], es[1::2], es[0::2]]
        for k in range(m):
            a = w * (k % (m // 2))
            out = T["rc" + tag][:, a:a + w] if rel else T.lcx[:, lo + w * k:lo + w * k + w]
            pieces.append((T.qxk[:, lo + w * k:lo + w * k + w].bitcast(dt.uint8), out.bitcast(dt.uint8)))
        pieces.append((T.sxk[:, lo:lo + n], T["rs" + tag][:, 0:n] if rel else T.lsx[:, lo:lo + n]))
        pieces = [(rel[2 * k // m] if rel else nxt, masks[k], ("rin" if rel else "arr") + tag, i, o) for k, (i, o) in enumerate(pieces)]
        for part in ([pieces] if m == 4 else [pieces[:2], pieces[2:]]):
            fused([A("qxk", lo, lo + n)[1], A("sxk", lo, lo + n)[1]], part, "loca")

    def fused(regs, pieces, loc="loc"):
        tr, busy = [], 0.6 if sum(sent) else 3.0
        for dst, es, sem, src, out in pieces:
            rid, pid = topo.addr(dst, core)
            tr.append(RemoteDMATransfer(dst_ids=[DstId(rid=rid, pnc=pid)], dma_engine_mask=_bits(es), remote_sem=T.sem[sem], src=src, dst=out))
            sent[loc == "loca"] += len(es)
        put(G, [("p9", 0, 1, None)], regs, lambda: g.remote_dma_fused(tr, local_sem=T.sem[loc]), busy, None, ("loc", 0))

    def send_half(h):
        es = topo.engines(core, rel[0])
        pieces = []
        if OPT["lh"] and h == 0:
            masks = [es[0::4], es[1::4], es[2::4], es[3::8], es[7::8]]
            for k in range(4):
                pieces.append((rel[k // 2], masks[k], "rin2", T.qg[:, 32 * k:32 * k + 32].bitcast(dt.uint8), T.rc2[:, 32 * (k % 2):32 * (k % 2) + 32].bitcast(dt.uint8)))
            pieces.append((rel[2], masks[4], "rin3", T.sg3[:, 0:128], T.rsh[:, 0:128]))
            fused([A("qg", 0, 128)[1], A("sg3", 0, 128)[1]], pieces)
            return
        for k in range(2):
            at = 128 * h + 64 * k
            pieces.append((rel[k], es[1::2][k::2] if h else es[k::2], "rin%d" % (2 + h), T.qg[:, at:at + 64].bitcast(dt.uint8), T.rc2[:, 64 * h:64 * h + 64].bitcast(dt.uint8)))
        if h:
            pieces.append((rel[2], es[0::2], "rin2", T.sg3[:, 0:256], T.rs2[:, 0:256]))
        fused([A("qg", 128 * h, 128 * h + 128)[1], A("sg3", 0, 128 * h + 128)[1]], pieces)

    load(S, "ptw", T.pt[:, :], "d_ptw")
    load(Y, "ks", T.k[:, :], "d_k")
    load(Y, "xs", T.x[:, :], "d_x")
    load(S, "adw", T.ad[:, :], "d_ad")
    load(Y, "us", T.u[:, :], "d_u")

    def late_loads():
        w = ("loca", sent[1]) if gives and OPT["wlate"] else ("d_u", 16)
        mark(w[0], 2.0, 2.0)
        expect(Y, *w)
        dma(Y, T.qw[:, 0:512].bitcast(dt.uint8), T.wc[:, :], "d_w", outs=[("qw", 0, 512, None)])
        expect(Y, *w)
        load(Y, "sw", T.ws[:, :], "d_ws")
        if OPT["gv"] in (1, 2 + far):
            load(G, "vs", T.v[:, :], "d_v")
        else:
            expect(Y, *w)
            load(Y, "vs", T.v[:, :], "d_v")

    def const(o, c):
        n = o[1][2] - o[1][1]
        act(o, A("ones", 0, n) if n <= 128 else A("z0", 16, 16 + n), scale=0.0, bias=c, func=AF.Identity)

    fill(A("z0"), 0.0)
    fill(A("ones"), 0.5)
    fill(A("et", 0, 528), 0.0)
    const(A("et", 528, 1056), 0.0)
    iota(A("pidx", 4, 5), [[1, 1]], 0, 17)
    iota(A("j16"), [[0, 8], [1, 16]], 0)
    iota(A("m16"), [[16, 32]], 0)
    for h in range(2):
        o, i = A("et", 528 * h, 528 * h + 512, 4, 2 + h), A("ones")
        run(G, [o], [i], lambda o=o, i=i: g.affine_select(o[0], i[0], [[-1, 128]], ALU.is_equal, 0.0, 0, 1))
    iota(A("pidx", 6, 8), [[0, 2]], 0, 1)
    iota(A("vki"), [[1, 320]], -160)

    q_, par, s16, mq, bq = [A("cst", j, j + 1) for j in range(5)]
    for j, m in enumerate((15, 16)):
        ts(A("pidx", 2 + j, 3 + j), A("pidx", 4, 5), m, ALU.bitwise_and)
    cp(A("cst", 0, 2), A("pidx", 2, 4))
    ts(A("tabl"), A("j16"), q_, ALU.is_lt)
    ts(A("tabi"), A("j16"), q_, ALU.is_equal)
    act(A("z0", 0, 1), q_, bias=-128.0)
    act(A("tabg"), A("tabi"), scale=1024.0, bias=-512.0)
    const(A("vv"), -0.5)
    cp(A("uiu"), A("m16", 0, 16))

    def unit(b):
        quant("qe", "se", 128 * b, 128 * b + 128, "et", 528 * (b % 2) + 2 - 2 * (b // 2))

    unit(0)
    unit(2)

    const(A("sx", 0, 32), -BIG / 2)
    cp(A("ptu"), A("ptw"))
    act(A("junk"), A("tabl"), li=A("ptu"), accum=A("acc"))
    cp(A("ind"), A("tabi"), li=A("ptu"))
    quant("qxk", "sxk", 0, 128, "ks", 0)

    def ways(t):
        a, b = OPT["d" + t], OPT["n" + t]
        return (a - OPT["lead"], b - OPT["lead"]) if far else (b + OPT["lead"], a + OPT["lead"])

    if gives and OPT["split"]:
        ahead(*_ahead()[0])
    mark("arrk", *ways("k"))
    unit(1)
    unit(3)
    act(A("gate"), A("tabg"), li=A("ptu"))
    act(s16, q_, scale=16.0, bias=15.0)
    act(A("vk"), A("vki"), scale=K)
    act(s16, par, scale=23.0, bias=s16)
    act(A("c16"), A("vki"), li=A("uiu"))
    act(mq, q_, scale=-BIG, bias=10 * BIG)
    o1, i1, l1 = A("qur"), A("qu"), A("uiu", 0, 8)
    scan(A("cum"), A("ind"), A("z0", 0, 320), A("acc"), ALU.add, ALU.add)
    quant("qxk", "sxk", 128, 448, "xs", 0)
    if gives:
        ahead(*_ahead()[-1])
    mark("arrx", *(ways("x") if gives else (8.5, 0.0)))
    late_loads()
    turn("ct", "cum")
    turn("gt", "gate")
    ts(A("dl"), A("m16", 0, 32, 16), s16, ALU.add, 2.0 * TW - 1, ALU.min)

    def others(M, li):
        act(A("msk"), A("c16", 0, M), scale=BIG / 16, bias=mq, func=AF.Abs, li=li)

    others(128, A("ptu"))
    for b in range(3):
        mm("p%d" % b, 448, "qe", "se", 128 * b, "qxk", "sxk", 0)
    scan(A("sel"), A("gt"), A("ct"), 0.0, ALU.max, ALU.min)
    quant("qu", "su", 0, 128, "us", 0)
    ts(A("plist"), A("sel"), 128.0, ALU.add, li=A("dl"))
    ts(A("pidx", 0, 2), A("pidx", 6, 8), 31, ALU.bitwise_and)
    act(A("sur"), A("su"), li=l1)
    run(V, [o1], [i1, l1], lambda: g.vector.tensor_copy(T.qur[:, 0:128].bitcast(dt.uint32), T.qu[:, 0:128].bitcast(dt.uint32).indirect(l1[0])), PICK)
    mm("p4", 320, "qur", "sur", 0, "qxk", "sxk", 128)
    mm("p3", 448, "qe", "se", 384, "qxk", "sxk", 0)
    scatter(A("vv"), A("plist", 0, 20), A("vk"))
    cp(A("adu", 0, 10), A("ints", 20, 30))
    turn("vt", "vv")
    ts(A("el"), A("z0", 2, 4), A("cum", 319, 320), ALU.add, 128.0, ALU.add)

    def unpack1(b):
        act(A("fg1", P1 * b, P1 * b + P1), A("p%d" % b, 0, P1), scale=0.5)
        if OPT["ghs"] in (1, 2 + far):
            act(A("gh", 128 * b, 128 * b + 128), A("p%d" % b, 0, 128), scale=0.5)
        else:
            g_copy(A("gh", 128 * b, 128 * b + 128), A("fg1", P1 * b, P1 * b + 128), 128)

    def mean1(b):
        tt(A("fg2", P2 * b, P2 * b + 128), A("fg1", P1 * b, P1 * b + 128), A("gh", 128 * b, 128 * b + 128), ALU.add, li=A("adu"))

    def pick(h, b, win, li, scale=1.0, n=1):
        act(A("tv", 1280 * h + 320 * b, 1280 * h + 320 * (b + n)), win, li=li, scale=scale)

    at = [128]

    def add(h, b):
        tt(B4("vl", 4 * V1 * h, 4 * V1 * h + 1280, b), A("p%d" % b, at[0], at[0] + 320), A("tv", 1280 * h + 320 * b, 1280 * h + 320 * b + 320), ALU.add)

    def score(h, bank):
        quant("qv", "sv3", 320 * h, 320 * h + 320, "vl", 4 * V1 * h)
        mm(bank, 320, "qur", "sur", 0, "qv", "sv3", 320 * h)

    def masked(bank, lo, n):
        tt(A("sx", 352 + lo, 352 + lo + n), A(bank, 0, n), A("msk", lo, lo + n), ALU.subtract)

    def argmax(fills, cells):
        fills = list(fills) + [lambda: None] * 7
        cp(A("ss"), A("sx"), li=A("order", 0, 21))
        fills[0]()
        scan(A("st"), A("d0"), A("ss"), -BIG, ALU.min, ALU.max)
        fills[1]()
        tt(A("nr"), A("st"), A("st", -1, L - 1), ALU.not_equal)
        fills[2]()
        scan(A("s2"), A("nr"), A("vv"), 0.0, ALU.add, ALU.min)
        fills[3]()
        tt(A("o32"), A("s2"), cells, ALU.max, li=A("el"))
        fills[4]()
        turn1(A("ot"), A("o32"))
        fills[5]()

    unpack1(0)
    unpack1(1)
    lin(A("order"), A("vt"), 1024.0, 512.0, li=A("dl"))
    act(A("d0"), A("vv"), scale=2.0 ** 95, bias=0.25 * 2.0 ** 95)
    masked("p4", 0, 320)
    unpack1(2)
    unpack1(3)
    act(bq, q_, scale=16 * K, bias=-288 * K)
    act(A("cw"), A("m16"), bias=q_)
    act(A("c1"), A("j16", 0, 32), scale=K, bias=bq)
    if OPT["slotv"] in (1, 2 + far):
        iota(A("slb"), [[0, 480]], 0)
    else:
        iota(A("tabo"), [[1, 512]], 0)

    def mean_pick(b):
        mean1(b)
        pick(1, b, A("fg2", P2 * b, P2 * b + 128), A("ptu"))

    def pt1():
        ts(A("pt1"), A("ints", 0, 32), 1.0 / 128, ALU.mult)

    early = OPT["early"] in (1, 2 + far)
    slotv = OPT["slotv"] in (1, 2 + far)
    if early:
        mean_pick(0)
        argmax([lambda: mean_pick(1), lambda: mean_pick(2), lambda: mean_pick(3), lambda: None, lambda: None, pt1], A("c1"))
    else:
        argmax([pt1], A("c1"))
    if not slotv:
        act(A("iq"), A("cw"), scale=K, bias=-160 * K)
        act(A("iw"), A("cw"), scale=1.0 / 512)
    act(A("ptl"), A("pt1"), scale=0.25 * (1 + slotv), bias=LL / 512.0 * (1 + slotv))
    lin(A("offu"), A("ot"), 1024.0, 288.0, li=A("own", 0, 1))
    r = A("offu", 0, 8)
    if rel:
        remote(T.rlx[:, 0:8], r[0], r[1], "rinl", rel[2], topo.engines(core, rel[2])[0:8])
    elif gives:
        remote(T.llx[:, 0:8], r[0], r[1], "arrl", nxt, topo.engines(core, nxt)[0:8])
    mark("arrl", *ways("l"))
    mark("arr1", OPT["n1"] + 1.7, OPT["dl"] + 2.0)

    def a1(b):
        tt(A("fg2", P2 * b + 128, P2 * b + 256), A("fg1", P1 * b, P1 * b + P1), A("gh", 128 * b, 128 * b + 128), ALU.add, li=A("offu", 0, 8))

    def b1(b):
        act(B4("gd", 512, 1024, b), A("fg2", P2 * b, P2 * b + 256), li=A("bl", 0, 8))

    def second_a(b):
        g_copy(B4("gd", 0, 512, b), A("fg2", P2 * b + 128, P2 * b + 256), 128)

    def b_list(offs, n):
        return [lambda: ts(A("ins", 0, n), offs, 16.0 * n, ALU.is_lt, 16.0 * n, ALU.mult),
                lambda: tt(A("ins", 0, n), A("ins", 0, n), A("cw", 0, n), ALU.add)]

    def inserter_rows(offs, M, li):
        act(A("qrow", 0, M), A("vkw", 256 - M, 576), li=offs)
        act(A("qp"), A("qrow", 0, M), li=li)

    def choose(bank, cell, cells, M, own=True, gt=False):
        if own == 1:
            turn("lt", "qp")
        if own:
            tt(A("slw"), A("lt"), A("iq"), ALU.is_equal, li=A("dl"))
        tt(A("more"), A(bank, 0, 320), A("t0s"), ALU.is_gt if gt else ALU.is_lt)
        turn("mt", "more")
        if own:
            tt(A("slw"), A("slw"), A("ptl"), ALU.mult)
        tt(A("wf"), A("mt"), A("iw"), ALU.add, li=A("dl"))
        tt(A(cell), A("mt"), A("pt1"), ALU.add, li=A("dl"))
        tt(A("wf"), A("wf"), A("slw"), ALU.max)
        ts(A(cells), A(cell, 0, 20), float(M), ALU.mult)
        for b in (1, 0, 3, 2):
            lin(A("wu", 20 * b, 20 * b + 20), A("wf", 0, 20), 2048.0, float(b))

    def layer(qn, sn, M, banks):
        for b in range(4):
            mm(banks[b], M, "qw", "sw", 128 * b, qn, sn, 0)

    def part_of_L(b, M, banks, q=S):
        o, i = B4("vl", 4 * LL, 4 * LL + 4 * M, b), A(banks[b], 0, M)
        if q == V:
            ts(o, i, 0.03125, ALU.mult)
        else:
            act(o, i, scale=0.03125)

    def new_state(M, xt, b, lo=0, hi=20):
        o, i, li = B4(xt, 64 * lo, 64 * hi, b), A("vl", 0, 4 * LL + 4 * M), A("wu", 20 * b + lo, 20 * b + hi)
        (act if b % 2 else cp)(o, i, li=li)

    def near_halves():
        for b in range(4):
            act(B4("g3", 512, 1024, b), A("fg2", P2 * b + 128, P2 * b + 256), li=A("adu"))

    def next_means(n):
        dma_add(A("g3", 0, n), A("gd", 0, n), "d_add", 2.5)

    def near_mean(b):
        tt(B4("g3", 512, 1024, b), A("fg2", P2 * b + 128, P2 * b + 256), B4("gd", 512, 1024, b), ALU.add, li=A("adu"))

    xb = ["p4", "p5", "p6", "p7"]

    def x_plane(b, lo, hi):
        if lo == 0 and OPT["split"]:
            expect(E, "arrk", landed)
        if hi == P1:
            expect(E, "arrx", landed)
        mm(xb[b], hi - lo, "qe", "se", 128 * b, "lcx", "lsx", lo)
        (cp if hi == 128 and OPT["kv"] else act)(A("fgx", P1 * b + lo, P1 * b + hi), A(xb[b], 0, hi - lo))
        if lo == 0:
            g_copy(A("ghx", 128 * b, 128 * b + 128), A("fgx", P1 * b, P1 * b + 128), 128)

    def a_before(b):
        expect(V, "arrl", 8)
        tt(B4("atx", 0, 512, b), A("fgx", P1 * b, P1 * b + P1), A("ghx", 128 * b, 128 * b + 128), ALU.add, li=A("llx"))

    steps = b_list(A("offu", 0, 8), 8) + [lambda: cp(A("bl", 0, 8), A("ins", 0, 8)), lambda: None]
    for b in range(4):
        a1(b)
        if gives:
            steps[b]()
        elif b:
            ts(B4("at1", 0, 512, b - 1), A("fg2", P2 * b - P2 + 128, P2 * b - P2 + 256), 2.0, ALU.mult)
        pick(0, b, A("fg2", P2 * b + 128, P2 * b + 256), A("ptu"))
        if gives or b < 3:
            second_a(b)

    def means():
        g_copy(A("g3", 0, 512), A("gd", 512, 1024), 512)
        near_halves()
        if slotv:
            act(A("iw"), A("cw"), scale=1.0 / 512)
        next_means(1024)
        for b in range(4):
            g_copy(A("fg2", P2 * b + 256, P2 * b + 384), B4("gd", 512, 1024, b), 128)

    if not takes:
        lb = ["p1", "p2", "p3", "p4"]
        for b in range(4):
            add(1, b)
        score(1, "p7")
        inserter_rows(A("offu", 0, 8), 128, A("ptu"))
        act(A("t0s"), A("p7", 0, 320))
        for b in range(4):
            b1(b)
            add(0, b)
        score(0, "p0")
        means()
        for b in range(4):
            expect(E, "arr1", 16)
            mm(lb[b], 128, "qw", "sw", 128 * b, "lc1", "ls1", 0)
        choose("p0", "j2", "ptv", 128)
    else:
        if not gives:
            steps[0]()
            ts(B4("at1", 0, 512, 3), A("fg2", P2 * 3 + 128, P2 * 3 + 256), 2.0, ALU.mult)
            steps[1]()
            quant("qa1", "sa1", 0, 128, "at1", 0)
            steps[2]()
            send("1", "qa1", "sa1", 128)
        if not early:
            for b in range(4):
                mean_pick(b)
        ks = OPT["ksplit"] and OPT["split"] and far
        if ks:
            for b in range(4):
                x_plane(b, 0, 128)
        first = 1 if early else 0
        for b in range(4):
            add(first, b)
        if slotv:
            scatter(A("slb", 0, 448), A("offu", 0, 8), A("ones"))
        for b in range(OPT["b1n"]):
            b1(b)
        lb = ["p2", "p3", "p4", "p5"]
        for b in range(4):
            x_plane(b, 128 if ks else 0, P1)
            add(1 - first, b)
        if not gives:
            second_a(3)
        score(1, "p0")
        if slotv:
            turn("lt", "sl")
        score(0, "p1")
        if slotv:
            tt(A("slw"), A("lt"), A("ptl"), ALU.mult, li=A("dl"))
        act(A("t0s"), A("p0", 0, 320))
        if not slotv:
            inserter_rows(A("offu", 0, 8), 128, A("ptu"))
        for b in range(OPT["b1n"], 4):
            b1(b)
        means()
        for b in range(4):
            a_before(b)
        quant("qax", "sax", 0, 128, "atx", 0)
        layer("qax", "sax", 128, lb)
        choose("p1", "j2", "ptv", 128, not slotv)
    for b in range(4):
        part_of_L(b, 128, lb, V if b < OPT["lv"] else S)
    for b in (1, 0, 3, 2):
        new_state(128, "xt2", b)
    others(256, A("ptv"))
    for h in range(2):
        quant("qx", "sx2", 160 * h, 160 * h + 160, "xt2", 640 * h)
        mm("p%d" % (5 + h), 160, "qur", "sur", 0, "qx", "sx2", 160 * h)
    for b in range(4):
        mm("p%d" % b, 320, "qe", "se", 128 * b, "qx", "sx2", 0)
    defer = OPT["defer"] and rel

    def list4(b):
        lin(A("l4", 20 * b, 20 * b + 20), A("j2", 0, 20), 512.0, float(b))

    def later():
        quant("qvv", "svv", 0, 128, "vs", 0)

    act(A("c2"), A("c1"), bias=-128 * K)
    if slotv:
        act(A("iq"), A("cw"), scale=K, bias=-160 * K)
    act(A("ptl"), A("j2"), scale=0.25, bias=LL / 512.0)
    act(A("pt1"), A("j2"), scale=0.5)
    list4(0)
    list4(1)
    if not defer:
        quant("qvv", "svv", 0, 128, "vs", 0)
    if OPT["nh"] == 2:
        tt(A("g3", 0, 512), A("gd", 0, 512), A("gd", 512, 1024), ALU.add)

    at[0] = 0
    for h in range(2):
        masked("p%d" % (5 + h), 160 * h, 160)

    def picks(h, lo, b):
        pick(h, b, A("g3", lo, lo + 1024), A("l4", 20 * b, 20 * b + 40), 0.5, 2)

    def z_half(h, p):
        mm(p, 256, "qvv", "svv", 0, "qg", "sg3", 256 * h)

    def z_out(h, p, how=act, q=Y):
        o = A("zs", 256 * h, 256 * h + 256)
        how(o, A(p, 0, 256))
        store(q, T.z[:, 256 * h:256 * h + 256], o)

    vd = OPT["v1d"] == 2 or OPT["v1d"] == 1 and far
    for b in range(4):
        act(B4("gd", 1024, 2304, b) if vd else A("fg2", P2 * b + 384, P2 * b + P2), A("p%d" % b, 0, 320))
    argmax([lambda: list4(2), lambda: None, lambda: list4(3)], A("c2"))
    steps = b_list(A("offv"), 16) + [lambda b=b: lin(A("bl", 16 * b, 16 * b + 16), A("ins"), 4.0, float(b)) for b in range(4)]
    if vd:
        lin(A("of4", 0, 16), A("ot"), 4096.0, 1664.0, li=A("own", 0, 1))
    lin(A("offv"), A("ot"), 1024.0, 416.0, li=A("own", 0, 1))
    if vd:
        for b in range(4):
            act(B4("vl", 4 * V1, 4 * V1 + 1280, b), A("g3", 0, 1024), li=A("l4", 20 * b, 20 * b + 20), scale=0.5)

        def v1_sum():
            dma_add(A("vl", 4 * V1, 4 * V1 + 1280), A("gd", 1024, 2304), "d_ad2", 0.8)
        if not rel:
            v1_sum()
    else:
        picks(1, 0, 0)
        act(A("qrow"), A("vkw"), li=A("offv"))
        picks(1, 0, 2)
        act(A("qp"), A("qrow"), li=A("ptv"))
    if vd:
        inserter_rows(A("offv"), 256, A("ptv"))
    n = 128 if rel else 256
    for lo in range(0, 256, n):
        for b in range(4):
            o = B4("g3", 1024 + 4 * lo, 1024 + 4 * (lo + n), b)
            if vd:
                tt(o, A("gd"), A("fg2", P2 * b + 128 + lo, P2 * b + 128 + lo + n), ALU.add, li=A("of4", 16 * b + lo // 16, 16 * b + (lo + n) // 16))
                if lo == 0 and b < 3:
                    lin(A("of4", 16 * b + 16, 16 * b + 32), A("offv"), 4.0, b + 1.0)
            else:
                tt(o, A("fg2", P2 * b + 128, P2 * b + P2), B4("gd", 4 * lo, 4 * (lo + n), b), ALU.add, li=A("offv", lo // 16, (lo + n) // 16))
            if lo + n == 256 and b in (1, 3) and not defer:
                steps[b // 2]()
        quant("qg", "sg3", lo, lo + n, "g3", 1024 + 4 * lo)
        if rel:
            send_half(lo // 128)
            if vd and lo == 0:
                v1_sum()
        else:
            send("2", "qg", "sg3", 256)
        if not (rel and vd):
            mark("arr2", *ways("2"))
    if slotv:
        iota(A("tabo"), [[1, 512]], 0)
    if defer:
        steps[0]()
        later()
        steps[1]()
    picks(0, 1024, 0)
    picks(0, 1024, 2)
    z_half(0, "p7")
    for b in range(4):
        steps[2 + b]()
    z_out(0, "p7")

    def b2(b):
        act(B4("g3", 2048, 3072, b), A("g3", 0, 2048), li=A("bl", 16 * b, 16 * b + 16))

    lb = ["p4", "p7", "p0", "p1"]

    def l2(b):
        expect(E, "arr2", 40 if far else 16)
        mm(lb[b], 256, "qw", "sw", 128 * b, "lc2", "ls2", 0)

    if vd:
        turn("lt", "qp")
        tt(A("slw"), A("lt"), A("iq"), ALU.is_equal, li=A("dl"))
        add(0, 0)
        tt(A("slw"), A("slw"), A("ptl"), ALU.mult)
        add(0, 1)
        score(1, "p6")
        add(0, 2)
        add(0, 3)
        score(0, "p5")
        b2(0)
        act(A("t0s"), A("p6", 0, 320))
        for b in range(1, 4):
            b2(b)
    else:
        for b in range(4):
            add(1, b)
        score(1, "p6")
        for b in range(4):
            b2(b)
            add(0, b)
        act(A("t0s"), A("p6", 0, 320))
        score(0, "p5")
        turn("lt", "qp")
    lh = OPT["lh"] and far
    zb = "p2"

    def l_half(h, banks):
        for b in range(4):
            expect(E, *(("arr2", 24) if h else ("arrh", 24)))
            mm(banks[b], 128, "qw", "sw", 128 * b, "lc2", "ls2" if h else "lsh", 128 * h)
            o, i = B4("vl", 4 * LL + 512 * h, 4 * LL + 512 * h + 512, b), A(banks[b], 0, 128)
            if h and b % 2:
                ts(o, i, 0.03125, ALU.mult)
            else:
                act(o, i, scale=0.03125)

    def op_out(q):
        act(A("opr"), A("tabo"), li=A("ptu"))
        dma(q, T.op[:, :], T.opr[0:128:16, 0:320], "d_out1" if q == Y else "d_out2", ins=[A("opr")[1]])

    ze = OPT["ze"] in (1, 2 + far)
    if not ze and not lh:
        for b in range(4):
            l2(b)
    if lh and not ze:
        l_half(0, lb)
    if not vd:
        quant("qg", "sg3", 256, 512, "g3", 2048)
        if ze:
            z_half(1, "p2")
            z_out(1, "p2")
    if lh and ze:
        l_half(0, lb)
    choose("p5", "opv", "ptu", 256, 0 if vd else 2)
    if vd:
        quant("qg", "sg3", 256, 512, "g3", 2048)
        if ze:
            z_half(1, "p2")
            z_out(1, "p2")
    if ze and OPT["oo"]:
        op_out(Y)
    if not ze:
        z_half(1, zb)
    if lh:
        l_half(1, ["p2" if ze else "p4", "p3", "p6", "p7"])
    else:
        for b in range(4):
            if ze:
                l2(b)
            part_of_L(b, 256, lb, V if b % 2 and OPT["l2v"] in (1, 2 + far) else S)

    def scales_out(q, k):
        dma(q, T.osc[4 * k:4 * k + 4, :], T.sx3[32 * k:32 * k + 4, 0:320], {Y: "d_out1", S: "d_out2", G: "d_out3"}[q], ins=[A("sx3")[1]])

    if OPT["tail"] < 5:
        for b in (1, 0, 3, 2):
            new_state(256, "xt3", b)
        if not ze:
            z_out(1, zb)
        if not (ze and OPT["oo"]):
            op_out(S if OPT["tail"] == 0 else Y)
    for h in range(2):
        if OPT["tail"] == 5:
            for b in (1, 0, 3, 2):
                new_state(256, "xt3", b, 10 * h, 10 * h + 10)
        quant("qx3", "sx3", 160 * h, 160 * h + 160, "xt3", 640 * h)
        mm(("p5", "p3")[h], 160, "qvv", "svv", 0, "qx3", "sx3", 160 * h)
        if OPT["tail"] == 5:
            a = A("qx3", 160 * h, 160 * h + 160)
            dma(Y, T.oc[:, 640 * h:640 * h + 640], a[0].bitcast(dt.uint8), "d_out1", ins=[a[1]])
    if OPT["tail"] < 5:
        dma(Y, T.oc[:, :], T.qx3[:, 0:320].bitcast(dt.uint8), "d_out1", ins=[A("qx3")[1]])
        for k in range(4):
            scales_out(OPT["oq"][k], k)
        for h in range(2):
            cp(A("zs", 512 + 160 * h, 672 + 160 * h), A(("p5", "p3")[h], 0, 160))
            if OPT["ys"]:
                store((Y, S)[h], T.y[:, 160 * h:160 * h + 160], A("zs", 512 + 160 * h, 672 + 160 * h))
        if not OPT["ys"]:
            store(S, T.y[:, :], A("zs", 512, 832))
    else:
        act(A("zs", 512, 672), A("p5", 0, 160))
        store(S, T.y[:, 0:160], A("zs", 512, 672))
        if not ze:
            z_out(1, zb, act, S)
            op_out(S)
        for k in range(4):
            scales_out(OPT["oq"][k], k)
        cp(A("zs", 672, 832), A("p3", 0, 160))
        store(Y, T.y[:, 160:320], A("zs", 672, 832))

    issue()

    for q in (V, S, E, G):
        need(G, qsem[q], cnt[q])
    ends = [("loc", sent[0]), ("loca", sent[1]), ("arr2", 24 if lh else 40 if far else 16), ("arrh", 24 if lh else 0)]
    ends += [("arr" + t, landed) for t, _, _ in _ahead()] + [("arrl", 8)] if takes else [("arr1", 16)]
    for s, n in list(dcnt.items()) + ends:
        need(G, s, n)
